import numpy as np
import ml_dtypes


def mxq(x, axis, fmt="e4m3"):
    dtype, down = {"e4m3": (ml_dtypes.float8_e4m3fn, 7), "e5m2": (ml_dtypes.float8_e5m2, 14)}[fmt]
    v = np.moveaxis(np.asarray(x, np.float32).astype(ml_dtypes.bfloat16).astype(np.float64), axis, -1)
    blocks = v.reshape(v.shape[:-1] + (-1, 32))
    amax = np.abs(blocks).max(-1, keepdims=True)
    byte = np.maximum(np.where(amax > 0, np.frexp(amax)[1] - 1 + 127, 0) - down, 1)
    scale = np.exp2(byte - 127.0)
    codes = (blocks / scale).astype(np.float32).astype(dtype).astype(np.float64)
    return np.moveaxis((codes * scale).reshape(v.shape), -1, axis)


WIDE = False


def mx_kscale(k):
    if not WIDE:
        return np.ones(k)
    levels = np.array([10, -10, 5, -5, 0])
    if k % 512:
        return np.exp2(np.random.permutation(np.resize(levels, k // 32))).repeat(32)
    a = np.empty((k // 512, 16))
    for p in range(k // 512):
        a[p, :8] = np.random.permutation(np.resize(levels, 8))
        for g in range(8):
            far = levels[np.abs(levels - a[p, g]) >= 10]
            a[p, g + 8] = far[np.random.randint(len(far))]
    return np.exp2(a.ravel()).repeat(32)


def f64(x):
    return np.asarray(x).astype(np.float64)


def striped(idx):
    return np.tile(idx.reshape(-1, 16).T, (8, 1)).astype(np.uint16)


def unstriped(offs):
    return offs[:16].T.reshape(-1).astype(np.int64)


E2M1 = np.array([0.0, 0.5, 1.0, 1.5, 2.0, 3.0, 4.0, 6.0, -0.0, -0.5, -1.0, -1.5, -2.0, -3.0, -4.0, -6.0])


def pack_weight(w, fmt):
    k, n = w.shape
    w = f64(np.asarray(w, np.float32).astype(ml_dtypes.bfloat16)).reshape(k // 32, 32, n)
    amax = np.abs(w).max(1)
    if fmt == "e4m3":
        byte = np.frexp(amax)[1] - 1 + 127 - 7
    else:
        mant, ex = np.frexp(amax / 6.0)
        byte = np.where(mant > 0.5, ex, ex - 1) + 127
    byte = np.clip(np.where(amax > 0, byte, 1), 1, 254)
    scaled = (w * np.exp2(127.0 - byte)[:, None, :]).reshape(k, n).astype(np.float32)
    by_word = np.ascontiguousarray(scaled.reshape(k // 512, 128, 4, n).transpose(0, 1, 3, 2))
    if fmt == "e4m3":
        words = by_word.astype(ml_dtypes.float8_e4m3fn).view(np.uint8)
    else:
        c = by_word.astype(ml_dtypes.float4_e2m1fn).view(np.uint8) & 0xF
        words = (c[..., 0::2] | (c[..., 1::2] << 4)).reshape(k // 512, 128, 2 * n)
    return np.ascontiguousarray(words), np.ascontiguousarray(byte.astype(np.uint8).reshape(k // 512, 16, n))


def unpack_weight(words, scales, fmt):
    g, _, n = scales.shape
    words = np.ascontiguousarray(words).reshape(g, 128, n, -1)
    if fmt == "e4m3":
        vals = words.view(ml_dtypes.float8_e4m3fn).astype(np.float64)
    else:
        nib = np.empty((g, 128, n, 4), np.uint8)
        nib[..., 0::2] = words & 0xF
        nib[..., 1::2] = words >> 4
        vals = E2M1[nib]
    vals = vals * np.repeat(np.exp2(scales.astype(np.float64) - 127.0), 8, axis=1)[..., None]
    return vals.transpose(0, 1, 3, 2).reshape(g * 512, n)


def gelu(v):
    return 0.5 * v * (1.0 + np.tanh(np.sqrt(2.0 / np.pi) * (v + 0.044715 * v**3)))


K, K2, H, N, T, T2, T3, S = 1024, 512, 1024, 768, 2048, 2048, 1024, 512

def setup_inputs():
    n = np.random.standard_normal
    s = mx_kscale(K)[:, None]
    s2 = mx_kscale(K2)[:, None]
    u = mx_kscale(H)[:, None]
    tab_words, tab_scales = pack_weight(n((K, T)) * s, "e4m3")
    tab2_words, tab2_scales = pack_weight(n((K2, T2)) * s2, "e4m3")
    tab3_words, tab3_scales = pack_weight(n((K2, T3)) * s2, "e2m1")
    w2_words, w2_scales = pack_weight(n((K2, H)) / np.sqrt(K2) / s2, "e2m1")
    wr_words, wr_scales = pack_weight(n((K, N)) / np.sqrt(K) / s, "e4m3")
    return {
        "tab_words": tab_words, "tab_scales": tab_scales,
        "tab2_words": tab2_words, "tab2_scales": tab2_scales,
        "tab3_words": tab3_words, "tab3_scales": tab3_scales,
        "offs": striped(np.random.permutation(T)[:S]),
        "offs2": striped(np.random.permutation(T2)[:S]),
        "offs3": striped(np.random.permutation(T3)[:S]),
        "w2_words": w2_words, "w2_scales": w2_scales,
        "w3": (n((K2, H)) / np.sqrt(K2) / s2).astype(np.float32),
        "b3": (0.5 * n(H)).astype(np.float32),
        "gain": (np.exp(0.3 * n(H)) * u[:, 0]).astype(np.float32),
        "w4": (1.5 * n((H, N)) / np.sqrt(H) / u).astype(np.float32),
        "wr_words": wr_words, "wr_scales": wr_scales,
        "bo": (0.5 * n(N)).astype(np.float32),
    }

def reference(tab_words, tab_scales, tab2_words, tab2_scales, tab3_words, tab3_scales, offs, offs2, offs3,
              w2_words, w2_scales, w3, b3, gain, w4, wr_words, wr_scales, bo):
    v = unpack_weight(tab_words, tab_scales, "e4m3")[:, unstriped(offs)]
    v2 = unpack_weight(tab2_words, tab2_scales, "e4m3")[:, unstriped(offs2)]
    v3 = unpack_weight(tab3_words, tab3_scales, "e2m1")[:, unstriped(offs3)]
    site = unpack_weight(w2_words, w2_scales, "e2m1").T @ v2
    buf = (mxq(f64(w3), 0, "e4m3").T @ v3) + f64(b3)[:, None]
    x = site * buf
    gl = 0.5 * x * (1.0 + np.tanh(0.7978845608 * (x + 0.044715 * x * x * x)))
    h = gl * f64(gain)[:, None]
    hq = mxq(h, 0, "e4m3")
    wr = unpack_weight(wr_words, wr_scales, "e4m3")
    y = mxq(f64(w4), 0, "e4m3").T @ hq + wr.T @ v
    return y + f64(bo)[:, None]

@@ -1,0 +1,237 @@
+from contextlib import ExitStack
+
+import concourse.mybir as mybir
+
+K, K2, H, N, T, T2, T3, S = 1024, 512, 1024, 768, 2048, 2048, 1024, 512
+FLOPS = 2 * S * (2 * K2 * H + H * N + K * N)
+
+F32 = mybir.dt.float32
+BF16 = mybir.dt.bfloat16
+I32 = mybir.dt.int32
+U32 = mybir.dt.uint32
+U16 = mybir.dt.uint16
+U8 = mybir.dt.uint8
+FP8X4 = mybir.dt.float8_e4m3fn_x4
+FP4X4 = mybir.dt.float4_e2m1fn_x4
+ACT = mybir.ActivationFunctionType
+MULT = mybir.AluOpType.mult
+ADD = mybir.AluOpType.add
+
+P = 128
+PACK = 4
+KP = P * PACK
+
+
+def tile_list_warhead_site_triage_kernel(
+    tc, tab_words, tab_scales, tab2_words, tab2_scales, tab3_words, tab3_scales, offs, offs2, offs3,
+    w2_words, w2_scales, w3, b3, gain, w4, wr_words, wr_scales, bo, out,
+):
+    nc = tc.nc
+    with ExitStack() as ctx:
+        sb = ctx.enter_context(tc.tile_pool(name="sb", bufs=1))
+        ps = ctx.enter_context(tc.psum_pool(name="ps", bufs=1))
+
+        def tile(name, shape, dtype):
+            return sb.tile(shape, dtype, name=name, align_bytes=64)
+
+        def zeroed_plane(name, width, engine):
+            plane = tile(name, [P, width], U8)
+            engine.memset(plane[:].bitcast(I32), 0)
+            return plane
+
+        def load_plane(queue, plane, scales):
+            passes = scales.shape[0]
+            for q in range(4):
+                src = scales[0, 4 * q : 4 * q + 4, :] if passes == 1 else scales[:, 4 * q : 4 * q + 4, :]
+                queue.dma_start(out=plane[32 * q : 32 * q + 4 * passes, :].bitcast(I32), in_=src.bitcast(I32))
+
+        def load_list(name, src):
+            lst = sb.tile([P, S // 16], U16, name=name)
+            nc.sync.dma_start(lst[:], src)
+            return lst
+
+        def gather(name, window, lst, dtype):
+            got = tile(name, [P, S], dtype)
+            nc.vector.tensor_copy(got[:], window.indirect(lst[:]))
+            return got
+
+        warm_in = tile("warm_in", [P, 1], F32)
+        warm_out = tile("warm_out", [P, 1], F32)
+        nc.gpsimd.memset(warm_in[:], 0.0)
+        nc.scalar.activation(warm_out[:], warm_in[:], ACT.Gelu_apprx_tanh)
+
+        s3 = zeroed_plane("s3", T3, nc.gpsimd)
+        sw2 = zeroed_plane("sw2", H, nc.gpsimd)
+        s2 = zeroed_plane("s2", T2, nc.vector)
+        s1 = zeroed_plane("s1", T, nc.gpsimd)
+        swr = zeroed_plane("swr", N, nc.gpsimd)
+
+        w3v = w3.rearrange("(p j) c -> p j c", j=PACK)
+        w3_raw = [[tile("w3_raw%d_%d" % (g, u), [P, PACK, KP // 2], F32) for u in range(2)] for g in range(2)]
+
+        def load_words(name, words):
+            held = tile(name, [P, words.shape[1]], I32)
+            nc.sync.dma_start(out=held[:], in_=words.rearrange("p t i -> p (t i)").bitcast(I32))
+            return held
+
+        def load_w3(g, u):
+            lo = KP * g + 256 * u
+            nc.sync.dma_start(out=w3_raw[g][u][:], in_=w3v[:, :, lo : lo + 256])
+
+        t3 = tile("t3", [P, T3], U16)
+        nc.sync.dma_start(out=t3[:].bitcast(I32), in_=tab3_words[0].bitcast(I32))
+        l3 = load_list("l3", offs3)
+        load_w3(0, 0)
+        load_plane(nc.sync, s3, tab3_scales)
+        load_w3(0, 1)
+        w2w = tile("w2w", [P, H], U16)
+        nc.sync.dma_start(out=w2w[:].bitcast(I32), in_=w2_words[0].bitcast(I32))
+        l2 = load_list("l2", offs2)
+        load_plane(nc.sync, s2, tab2_scales)
+        t2 = load_words("t2", tab2_words[0])
+        load_plane(nc.sync, sw2, w2_scales)
+        b3t = tile("b3t", [P, 2, PACK], F32)
+        nc.sync.dma_start(out=b3t[:], in_=b3.rearrange("(g p t) -> p g t", g=2, t=PACK))
+        load_w3(1, 0)
+        load_w3(1, 1)
+        gaint = tile("gaint", [P, 2, PACK], F32)
+        nc.sync.dma_start(out=gaint[:], in_=gain.rearrange("(g p t) -> p g t", g=2, t=PACK))
+        l1 = load_list("l1", offs)
+        t1 = [load_words("t1_0", tab_words[0])]
+        load_plane(nc.sync, s1, tab_scales)
+        w4_raw = [tile("w4_raw%d" % g, [P, PACK, N], F32) for g in range(2)]
+        nc.sync.dma_start(out=w4_raw[0][:], in_=w4[0:KP, :].rearrange("(p j) n -> p j n", j=PACK))
+        t1.append(load_words("t1_1", tab_words[1]))
+        load_plane(nc.sync, swr, wr_scales)
+        bot = tile("bot", [P, N // P], F32)
+        with nc.allow_non_contiguous_dma(reason="one bias value a partition"):
+            nc.sync.dma_start(out=bot[:], in_=bo.rearrange("(c p) -> p c", p=P))
+        nc.sync.dma_start(out=w4_raw[1][:], in_=w4[KP : 2 * KP, :].rearrange("(p j) n -> p j n", j=PACK))
+        wrw = [load_words("wrw%d" % a, wr_words[a]) for a in range(2)]
+
+        def quantise(name, src, width):
+            codes = tile(name + "_c", [P, width], U32)
+            scales = tile(name + "_s", [P, width], U8)
+            nc.vector.quantize_mx(out=codes[:].bitcast(FP8X4), scales=scales[:], in_=src)
+            return codes, scales
+
+        def cast_w3(g):
+            grouped = tile("w3_bf%d" % g, [P, PACK * KP], BF16)
+            dst = grouped[:].rearrange("p (t m j) -> p m j t", t=PACK, j=PACK)
+            for u in range(2):
+                nc.scalar.copy(
+                    out=dst[:, 64 * u : 64 * (u + 1), :, :],
+                    in_=w3_raw[g][u][:].rearrange("p j (m t) -> p m j t", t=PACK),
+                )
+            return grouped
+
+        def cast_w4(g, lo, hi, engine):
+            grouped = tile("w4_bf%d_%d" % (g, lo), [P, PACK * (hi - lo)], BF16)
+            dst = grouped[:].rearrange("p (c i j) -> p c j i", i=4, j=PACK)
+            src = w4_raw[g][:, :, lo:hi].rearrange("p j (c i) -> p c j i", i=4)
+            if engine == "scalar":
+                nc.scalar.copy(out=dst, in_=src)
+            else:
+                nc.vector.tensor_copy(out=dst, in_=src)
+            return grouped
+
+        w3_bf0 = cast_w3(0)
+        v3 = gather("v3", t3[:], l3, U16)
+        v3s = gather("v3s", s3[:], l3, U8)
+        w2p = tile("w2p", [P, H], U16)
+        nc.vector.tensor_copy(
+            out=w2p[:].rearrange("p (g t m) -> p g t m", g=2, t=PACK),
+            in_=w2w[:].rearrange("p (g m t) -> p g t m", g=2, t=PACK),
+        )
+        w3q0 = quantise("w3q0", w3_bf0[:], KP)
+        v2s = gather("v2s", s2[:], l2, U8)
+        v2 = gather("v2", t2[:].bitcast(U32), l2, U32)
+        w2s = tile("w2s", [P, H], U8)
+        nc.vector.tensor_copy(
+            out=w2s[:].rearrange("p (g t m) -> p g t m", g=2, t=PACK),
+            in_=sw2[:].rearrange("p (g m t) -> p g t m", g=2, t=PACK),
+        )
+
+        def buffers(g, w3q):
+            biased = []
+            for t in range(PACK):
+                cols = slice(P * t, P * (t + 1))
+                buf_ps = ps.tile([P, S], F32, name="buf_ps", tag="bank%d" % t)
+                nc.tensor.matmul_mx(
+                    out=buf_ps[:], lhsT=w3q[0][:, cols].bitcast(FP8X4), lhsT_scale=w3q[1][:, cols],
+                    rhs=v3[:].bitcast(FP4X4), rhs_scale=v3s[:], start=True, stop=True,
+                )
+                bufb = tile("bufb%d_%d" % (g, t), [P, S], F32)
+                nc.scalar.activation(bufb[:], buf_ps[:], ACT.Identity, bias=b3t[:, g, t : t + 1])
+                biased.append(bufb)
+            return biased
+
+        def gelus(g, biased):
+            gl = tile("gl%d" % g, [P, PACK, S], F32)
+            for t in range(PACK):
+                wide = slice(KP * g + P * t, KP * g + P * (t + 1))
+                site_ps = ps.tile([P, S], F32, name="site_ps", tag="bank%d" % (4 + t))
+                nc.tensor.matmul_mx(
+                    out=site_ps[:], lhsT=w2p[:, wide].bitcast(FP4X4), lhsT_scale=w2s[:, wide],
+                    rhs=v2[:].bitcast(FP8X4), rhs_scale=v2s[:], start=True, stop=True,
+                )
+                x = tile("x%d_%d" % (g, t), [P, S], F32)
+                nc.vector.tensor_tensor(x[:], site_ps[:], biased[t][:], MULT)
+                nc.scalar.activation(gl[:, t, :], x[:], ACT.Gelu_apprx_tanh)
+            return gl
+
+        def hidden(g, gl):
+            hb = tile("hb%d" % g, [P, PACK * S], BF16)
+            nc.vector.tensor_tensor(
+                hb[:].rearrange("p (c i t) -> p c t i", i=4, t=PACK),
+                gl[:].rearrange("p t (c i) -> p c t i", i=4),
+                gaint[:, g, :].rearrange("p (a t b) -> p a t b", a=1, b=1).to_broadcast([P, S // 4, PACK, 4]),
+                MULT,
+            )
+            return quantise("hq%d" % g, hb[:], S)
+
+        biased0 = buffers(0, w3q0)
+        w3_bf1 = cast_w3(1)
+        gl0 = gelus(0, biased0)
+        biased1 = buffers(1, quantise("w3q1", w3_bf1[:], KP))
+        hq = [hidden(0, gl0)]
+        hq.append(hidden(1, gelus(1, biased1)))
+
+        v1s = gather("v1s", s1[:], l1, U8)
+        v1 = [gather("v1_%d" % a, t1[a][:].bitcast(U32), l1, U32) for a in range(2)]
+        w4q = {}
+        for lo, hi in [(0, 512), (512, 768)]:
+            quantised = quantise("w4q0_%d" % lo, cast_w4(0, lo, hi, "scalar")[:], hi - lo)
+            for c in range(lo // P, hi // P):
+                w4q[0, c] = (quantised, slice(P * c - lo, P * (c + 1) - lo))
+
+        def w4_pass(acc, g, c):
+            (codes, scales), part = w4q[g, c]
+            nc.tensor.matmul_mx(
+                out=acc[:], lhsT=codes[:, part].bitcast(FP8X4), lhsT_scale=scales[:, part],
+                rhs=hq[g][0][:].bitcast(FP8X4), rhs_scale=hq[g][1][:], start=(g == 0), stop=(g == 1),
+            )
+
+        accs = []
+        for c in range(N // P):
+            acc = ps.tile([P, S], F32, name="acc%d" % c, tag="bank%d" % (4 * (c % 2) + c // 2))
+            w4_pass(acc, 0, c)
+            accs.append(acc)
+        for a in range(2):
+            for c in range(N // P):
+                cols = slice(P * c, P * (c + 1))
+                nc.tensor.matmul_mx(
+                    out=accs[c][:], lhsT=wrw[a][:, cols].bitcast(FP8X4), lhsT_scale=swr[4 * a : P, cols],
+                    rhs=v1[a][:].bitcast(FP8X4), rhs_scale=v1s[4 * a : P, :], start=False, stop=False,
+                )
+        for lo in range(0, N, 256):
+            quantised = quantise("w4q1_%d" % lo, cast_w4(1, lo, lo + 256, "scalar")[:], 256)
+            for c in range(lo // P, lo // P + 2):
+                w4q[1, c] = (quantised, slice(P * c - lo, P * (c + 1) - lo))
+                w4_pass(accs[c], 1, c)
+                res = tile("res%d" % c, [P, S], F32)
+                if c % 2 == 0:
+                    nc.scalar.activation(res[:], accs[c][:], ACT.Identity, bias=bot[:, c : c + 1])
+                else:
+                    nc.vector.tensor_scalar(res[:], accs[c][:], bot[:, c : c + 1], None, ADD)
+                nc.sync.dma_start(out=out[P * c : P * (c + 1), :], in_=res[:])

@@ -31,8 +31,8 @@ def tile_list_warhead_site_triage_kernel(
         sb = ctx.enter_context(tc.tile_pool(name="sb", bufs=1))
         ps = ctx.enter_context(tc.psum_pool(name="ps", bufs=1))
 
-        def tile(name, shape, dtype):
-            return sb.tile(shape, dtype, name=name, align_bytes=64)
+        def tile(name, shape, dtype, after=None):
+            return sb.tile(shape, dtype, name=name, tag=after or name, align_bytes=64)
 
         def zeroed_plane(name, width, engine):
             plane = tile(name, [P, width], U8)
@@ -50,8 +50,8 @@ def tile_list_warhead_site_triage_kernel(
             nc.sync.dma_start(lst[:], src)
             return lst
 
-        def gather(name, window, lst, dtype):
-            got = tile(name, [P, S], dtype)
+        def gather(name, window, lst, dtype, after=None):
+            got = tile(name, [P, S], dtype, after)
             nc.vector.tensor_copy(got[:], window.indirect(lst[:]))
             return got
 
@@ -67,75 +67,76 @@ def tile_list_warhead_site_triage_kernel(
         swr = zeroed_plane("swr", N, nc.gpsimd)
 
         w3v = w3.rearrange("(p j) c -> p j c", j=PACK)
-        w3_raw = [[tile("w3_raw%d_%d" % (g, u), [P, PACK, KP // 2], F32) for u in range(2)] for g in range(2)]
 
         def load_words(name, words):
             held = tile(name, [P, words.shape[1]], I32)
             nc.sync.dma_start(out=held[:], in_=words.rearrange("p t i -> p (t i)").bitcast(I32))
             return held
 
-        def load_w3(g, u):
-            lo = KP * g + 256 * u
-            nc.sync.dma_start(out=w3_raw[g][u][:], in_=w3v[:, :, lo : lo + 256])
+        def load_w3(lo, hi):
+            raw = tile("w3_raw%d" % lo, [P, PACK, hi - lo], F32)
+            nc.sync.dma_start(out=raw[:], in_=w3v[:, :, lo:hi])
+            return raw
+
+        def load_w4(g):
+            raw = tile("w4_raw%d" % g, [P, PACK, N], F32)
+            nc.sync.dma_start(out=raw[:], in_=w4[KP * g : KP * (g + 1), :].rearrange("(p j) n -> p j n", j=PACK))
+            return raw
+
+        def load_channels(name, vec):
+            held = tile(name, [P, 2, PACK], F32)
+            nc.sync.dma_start(out=held[:], in_=vec.rearrange("(g p t) -> p g t", g=2, t=PACK))
+            return held
 
         t3 = tile("t3", [P, T3], U16)
         nc.sync.dma_start(out=t3[:].bitcast(I32), in_=tab3_words[0].bitcast(I32))
         l3 = load_list("l3", offs3)
-        load_w3(0, 0)
         load_plane(nc.sync, s3, tab3_scales)
-        load_w3(0, 1)
+        w3_first = load_w3(0, KP)
+        l2 = load_list("l2", offs2)
         w2w = tile("w2w", [P, H], U16)
         nc.sync.dma_start(out=w2w[:].bitcast(I32), in_=w2_words[0].bitcast(I32))
-        l2 = load_list("l2", offs2)
         load_plane(nc.sync, s2, tab2_scales)
         t2 = load_words("t2", tab2_words[0])
+        b3t = load_channels("b3t", b3)
+        w3_second = [load_w3(KP, KP + 256)]
         load_plane(nc.sync, sw2, w2_scales)
-        b3t = tile("b3t", [P, 2, PACK], F32)
-        nc.sync.dma_start(out=b3t[:], in_=b3.rearrange("(g p t) -> p g t", g=2, t=PACK))
-        load_w3(1, 0)
-        load_w3(1, 1)
-        gaint = tile("gaint", [P, 2, PACK], F32)
-        nc.sync.dma_start(out=gaint[:], in_=gain.rearrange("(g p t) -> p g t", g=2, t=PACK))
+        w3_second.append(load_w3(KP + 256, H))
         l1 = load_list("l1", offs)
         t1 = [load_words("t1_0", tab_words[0])]
+        gaint = load_channels("gaint", gain)
+        w4_raw = [load_w4(0)]
         load_plane(nc.sync, s1, tab_scales)
-        w4_raw = [tile("w4_raw%d" % g, [P, PACK, N], F32) for g in range(2)]
-        nc.sync.dma_start(out=w4_raw[0][:], in_=w4[0:KP, :].rearrange("(p j) n -> p j n", j=PACK))
-        t1.append(load_words("t1_1", tab_words[1]))
+        w4_raw.append(load_w4(1))
+        wrw = [load_words("wrw0", wr_words[0])]
         load_plane(nc.sync, swr, wr_scales)
+        wrw.append(load_words("wrw1", wr_words[1]))
+        t1.append(load_words("t1_1", tab_words[1]))
         bot = tile("bot", [P, N // P], F32)
         with nc.allow_non_contiguous_dma(reason="one bias value a partition"):
             nc.sync.dma_start(out=bot[:], in_=bo.rearrange("(c p) -> p c", p=P))
-        nc.sync.dma_start(out=w4_raw[1][:], in_=w4[KP : 2 * KP, :].rearrange("(p j) n -> p j n", j=PACK))
-        wrw = [load_words("wrw%d" % a, wr_words[a]) for a in range(2)]
 
-        def quantise(name, src, width):
-            codes = tile(name + "_c", [P, width], U32)
+        def quantise(name, src, width, after=None):
+            codes = tile(name + "_c", [P, width], U32, after)
             scales = tile(name + "_s", [P, width], U8)
             nc.vector.quantize_mx(out=codes[:].bitcast(FP8X4), scales=scales[:], in_=src)
             return codes, scales
 
-        def cast_w3(g):
+        def cast_w3(g, parts):
             grouped = tile("w3_bf%d" % g, [P, PACK * KP], BF16)
             dst = grouped[:].rearrange("p (t m j) -> p m j t", t=PACK, j=PACK)
-            for u in range(2):
-                nc.scalar.copy(
-                    out=dst[:, 64 * u : 64 * (u + 1), :, :],
-                    in_=w3_raw[g][u][:].rearrange("p j (m t) -> p m j t", t=PACK),
-                )
+            n = P // len(parts)
+            for u, raw in enumerate(parts):
+                nc.scalar.copy(out=dst[:, n * u : n * (u + 1)], in_=raw[:].rearrange("p j (m t) -> p m j t", t=PACK))
             return grouped
 
-        def cast_w4(g, lo, hi, engine):
-            grouped = tile("w4_bf%d_%d" % (g, lo), [P, PACK * (hi - lo)], BF16)
-            dst = grouped[:].rearrange("p (c i j) -> p c j i", i=4, j=PACK)
-            src = w4_raw[g][:, :, lo:hi].rearrange("p j (c i) -> p c j i", i=4)
-            if engine == "scalar":
-                nc.scalar.copy(out=dst, in_=src)
-            else:
-                nc.vector.tensor_copy(out=dst, in_=src)
-            return grouped
+        def cast_w4(g, lo, hi, grouped):
+            nc.scalar.copy(
+                out=grouped.rearrange("p (c i j) -> p c j i", i=4, j=PACK),
+                in_=w4_raw[g][:, :, lo:hi].rearrange("p j (c i) -> p c j i", i=4),
+            )
 
-        w3_bf0 = cast_w3(0)
+        w3_bf0 = cast_w3(0, [w3_first])
         v3 = gather("v3", t3[:], l3, U16)
         v3s = gather("v3s", s3[:], l3, U8)
         w2p = tile("w2p", [P, H], U16)
@@ -166,8 +167,10 @@ def tile_list_warhead_site_triage_kernel(
                 biased.append(bufb)
             return biased
 
+        halves = [slice(0, S // 2), slice(S // 2, S)]
+
         def gelus(g, biased):
-            gl = tile("gl%d" % g, [P, PACK, S], F32)
+            x = tile("x%d" % g, [P, PACK, S], F32)
             for t in range(PACK):
                 wide = slice(KP * g + P * t, KP * g + P * (t + 1))
                 site_ps = ps.tile([P, S], F32, name="site_ps", tag="bank%d" % (4 + t))
@@ -175,63 +178,86 @@ def tile_list_warhead_site_triage_kernel(
                     out=site_ps[:], lhsT=w2p[:, wide].bitcast(FP4X4), lhsT_scale=w2s[:, wide],
                     rhs=v2[:].bitcast(FP8X4), rhs_scale=v2s[:], start=True, stop=True,
                 )
-                x = tile("x%d_%d" % (g, t), [P, S], F32)
-                nc.vector.tensor_tensor(x[:], site_ps[:], biased[t][:], MULT)
-                nc.scalar.activation(gl[:, t, :], x[:], ACT.Gelu_apprx_tanh)
+                nc.vector.tensor_tensor(x[:, t, :], site_ps[:], biased[t][:], MULT)
+            gl = tile("gl%d" % g, [P, S, PACK], F32)
+            for half in halves:
+                nc.scalar.activation(
+                    gl[:, half, :].rearrange("p (c i) t -> p c t i", i=4),
+                    x[:, :, half].rearrange("p t (c i) -> p c t i", i=4),
+                    ACT.Gelu_apprx_tanh,
+                )
             return gl
 
-        def hidden(g, gl):
-            hb = tile("hb%d" % g, [P, PACK * S], BF16)
-            nc.vector.tensor_tensor(
-                hb[:].rearrange("p (c i t) -> p c t i", i=4, t=PACK),
-                gl[:].rearrange("p t (c i) -> p c t i", i=4),
-                gaint[:, g, :].rearrange("p (a t b) -> p a t b", a=1, b=1).to_broadcast([P, S // 4, PACK, 4]),
-                MULT,
-            )
-            return quantise("hq%d" % g, hb[:], S)
+        def scaled(g, gl, after):
+            hb = tile("hb%d" % g, [P, S, PACK], BF16, after)
+            factor = gaint[:, g : g + 1, :].to_broadcast([P, S // 2, PACK])
+            for half in halves:
+                nc.vector.tensor_tensor(hb[:, half, :], gl[:, half, :], factor, MULT)
+            return hb[:].rearrange("p n t -> p (n t)")
+
+        w4q = {}
+
+        def w4_cast(g, lo, hi, after):
+            grouped = tile("w4_bf%d_%d" % (g, lo), [P, PACK * (hi - lo)], BF16, after)
+            cast_w4(g, lo, hi, grouped[:])
+            return grouped
+
+        def w4_quantise(g, lo, hi, grouped, after=None):
+            quantised = quantise("w4q%d_%d" % (g, lo), grouped, hi - lo, after)
+            for c in range(lo // P, hi // P):
+                w4q[g, c] = (quantised, slice(P * c - lo, P * (c + 1) - lo))
 
         biased0 = buffers(0, w3q0)
-        w3_bf1 = cast_w3(1)
+        w3_bf1 = cast_w3(1, w3_second)
         gl0 = gelus(0, biased0)
         biased1 = buffers(1, quantise("w3q1", w3_bf1[:], KP))
-        hq = [hidden(0, gl0)]
-        hq.append(hidden(1, gelus(1, biased1)))
-
-        v1s = gather("v1s", s1[:], l1, U8)
-        v1 = [gather("v1_%d" % a, t1[a][:].bitcast(U32), l1, U32) for a in range(2)]
-        w4q = {}
-        for lo, hi in [(0, 512), (512, 768)]:
-            quantised = quantise("w4q0_%d" % lo, cast_w4(0, lo, hi, "scalar")[:], hi - lo)
-            for c in range(lo // P, hi // P):
-                w4q[0, c] = (quantised, slice(P * c - lo, P * (c + 1) - lo))
+        v1 = [gather("v1_0", t1[0][:].bitcast(U32), l1, U32, "bufb0_3")]
+        gl1 = gelus(1, biased1)
+        hb0 = scaled(0, gl0, "t1_0")
+        v1s = gather("v1s", s1[:], l1, U8, "bufb1_3")
+        hq = [quantise("hq0", hb0, S)]
+        hb1 = scaled(1, gl1, "s1")
+        w4_bf0 = w4_cast(0, 0, N, "x1")
+        hq.append(quantise("hq1", hb1, S))
+        w4_quantise(0, 0, 512, w4_bf0[:, 0 : PACK * 512])
+        w4_quantise(0, 512, N, w4_bf0[:, PACK * 512 : PACK * N])
+        last = tile("v1_1", [P, S], U32)
+        for u in range(2):
+            nc.vector.tensor_copy(
+                last[:, 256 * u : 256 * (u + 1)], t1[1][:].bitcast(U32).indirect(l1[:, 16 * u : 16 * (u + 1)])
+            )
+        v1.append(last)
+        w4_quantise(1, 0, 512, w4_cast(1, 0, 512, "w4_raw0")[:], "t1_1")
+        w4_quantise(1, 512, N, w4_cast(1, 512, N, "gl1")[:])
 
         def w4_pass(acc, g, c):
             (codes, scales), part = w4q[g, c]
             nc.tensor.matmul_mx(
                 out=acc[:], lhsT=codes[:, part].bitcast(FP8X4), lhsT_scale=scales[:, part],
-                rhs=hq[g][0][:].bitcast(FP8X4), rhs_scale=hq[g][1][:], start=(g == 0), stop=(g == 1),
+                rhs=hq[g][0][:].bitcast(FP8X4), rhs_scale=hq[g][1][:], start=False, stop=(g == 1),
             )
 
-        accs = []
+        def wr_pass(acc, a, c, lo=0, hi=S):
+            cols = slice(P * c, P * (c + 1))
+            nc.tensor.matmul_mx(
+                out=acc[:, lo:hi], lhsT=wrw[a][:, cols].bitcast(FP8X4), lhsT_scale=swr[4 * a : P, cols],
+                rhs=v1[a][:, lo:hi].bitcast(FP8X4), rhs_scale=v1s[4 * a : P, lo:hi],
+                start=(a == 0), stop=False,
+            )
+
+        accs = [ps.tile([P, S], F32, name="acc%d" % c, tag="bank%d" % c) for c in range(N // P)]
         for c in range(N // P):
-            acc = ps.tile([P, S], F32, name="acc%d" % c, tag="bank%d" % (4 * (c % 2) + c // 2))
-            w4_pass(acc, 0, c)
-            accs.append(acc)
-        for a in range(2):
+            wr_pass(accs[c], 0, c)
+        for c in range(N // P):
+            w4_pass(accs[c], 0, c)
+        for lo in range(0, S, 256):
             for c in range(N // P):
-                cols = slice(P * c, P * (c + 1))
-                nc.tensor.matmul_mx(
-                    out=accs[c][:], lhsT=wrw[a][:, cols].bitcast(FP8X4), lhsT_scale=swr[4 * a : P, cols],
-                    rhs=v1[a][:].bitcast(FP8X4), rhs_scale=v1s[4 * a : P, :], start=False, stop=False,
-                )
-        for lo in range(0, N, 256):
-            quantised = quantise("w4q1_%d" % lo, cast_w4(1, lo, lo + 256, "scalar")[:], 256)
-            for c in range(lo // P, lo // P + 2):
-                w4q[1, c] = (quantised, slice(P * c - lo, P * (c + 1) - lo))
-                w4_pass(accs[c], 1, c)
-                res = tile("res%d" % c, [P, S], F32)
-                if c % 2 == 0:
-                    nc.scalar.activation(res[:], accs[c][:], ACT.Identity, bias=bot[:, c : c + 1])
-                else:
-                    nc.vector.tensor_scalar(res[:], accs[c][:], bot[:, c : c + 1], None, ADD)
-                nc.sync.dma_start(out=out[P * c : P * (c + 1), :], in_=res[:])
+                wr_pass(accs[c], 1, c, lo, lo + 256)
+        for c in range(N // P):
+            w4_pass(accs[c], 1, c)
+            res = tile("res%d" % c, [P, S], F32)
+            if c % 2 == 0:
+                nc.scalar.activation(res[:], accs[c][:], ACT.Identity, bias=bot[:, c : c + 1])
+            else:
+                nc.vector.tensor_scalar(res[:], accs[c][:], bot[:, c : c + 1], None, ADD)
+            nc.sync.dma_start(out=out[P * c : P * (c + 1), :], in_=res[:])

@@ -78,9 +78,9 @@ def tile_list_warhead_site_triage_kernel(
             nc.sync.dma_start(out=raw[:], in_=w3v[:, :, lo:hi])
             return raw
 
-        def load_w4(g):
-            raw = tile("w4_raw%d" % g, [P, PACK, N], F32)
-            nc.sync.dma_start(out=raw[:], in_=w4[KP * g : KP * (g + 1), :].rearrange("(p j) n -> p j n", j=PACK))
+        def load_w4(g, lo, hi):
+            raw = tile("w4_raw%d_%d" % (g, lo), [P, PACK, hi - lo], F32)
+            nc.sync.dma_start(out=raw[:], in_=w4[KP * g : KP * (g + 1), lo:hi].rearrange("(p j) n -> p j n", j=PACK))
             return raw
 
         def load_channels(name, vec):
@@ -91,27 +91,29 @@ def tile_list_warhead_site_triage_kernel(
         t3 = tile("t3", [P, T3], U16)
         nc.sync.dma_start(out=t3[:].bitcast(I32), in_=tab3_words[0].bitcast(I32))
         l3 = load_list("l3", offs3)
+        w3_first = [load_w3(0, 256)]
         load_plane(nc.sync, s3, tab3_scales)
-        w3_first = load_w3(0, KP)
-        l2 = load_list("l2", offs2)
+        w3_first.append(load_w3(256, KP))
         w2w = tile("w2w", [P, H], U16)
         nc.sync.dma_start(out=w2w[:].bitcast(I32), in_=w2_words[0].bitcast(I32))
+        l2 = load_list("l2", offs2)
         load_plane(nc.sync, s2, tab2_scales)
         t2 = load_words("t2", tab2_words[0])
-        b3t = load_channels("b3t", b3)
-        w3_second = [load_w3(KP, KP + 256)]
         load_plane(nc.sync, sw2, w2_scales)
-        w3_second.append(load_w3(KP + 256, H))
+        b3t = load_channels("b3t", b3)
+        w3_second = [load_w3(KP, KP + 256), load_w3(KP + 256, H)]
         l1 = load_list("l1", offs)
         t1 = [load_words("t1_0", tab_words[0])]
         gaint = load_channels("gaint", gain)
-        w4_raw = [load_w4(0)]
         load_plane(nc.sync, s1, tab_scales)
-        w4_raw.append(load_w4(1))
         wrw = [load_words("wrw0", wr_words[0])]
+        w4_raw = {(0, 0): load_w4(0, 0, 512)}
         load_plane(nc.sync, swr, wr_scales)
-        wrw.append(load_words("wrw1", wr_words[1]))
+        w4_raw[0, 512] = load_w4(0, 512, N)
         t1.append(load_words("t1_1", tab_words[1]))
+        wrw.append(load_words("wrw1", wr_words[1]))
+        w4_raw[1, 0] = load_w4(1, 0, 512)
+        w4_raw[1, 512] = load_w4(1, 512, N)
         bot = tile("bot", [P, N // P], F32)
         with nc.allow_non_contiguous_dma(reason="one bias value a partition"):
             nc.sync.dma_start(out=bot[:], in_=bo.rearrange("(c p) -> p c", p=P))
@@ -130,13 +132,7 @@ def tile_list_warhead_site_triage_kernel(
                 nc.scalar.copy(out=dst[:, n * u : n * (u + 1)], in_=raw[:].rearrange("p j (m t) -> p m j t", t=PACK))
             return grouped
 
-        def cast_w4(g, lo, hi, grouped):
-            nc.scalar.copy(
-                out=grouped.rearrange("p (c i j) -> p c j i", i=4, j=PACK),
-                in_=w4_raw[g][:, :, lo:hi].rearrange("p j (c i) -> p c j i", i=4),
-            )
-
-        w3_bf0 = cast_w3(0, [w3_first])
+        w3_bf0 = cast_w3(0, w3_first)
         v3 = gather("v3", t3[:], l3, U16)
         v3s = gather("v3s", s3[:], l3, U8)
         w2p = tile("w2p", [P, H], U16)
@@ -169,7 +165,7 @@ def tile_list_warhead_site_triage_kernel(
 
         halves = [slice(0, S // 2), slice(S // 2, S)]
 
-        def gelus(g, biased):
+        def gelus(g, biased, after=None):
             x = tile("x%d" % g, [P, PACK, S], F32)
             for t in range(PACK):
                 wide = slice(KP * g + P * t, KP * g + P * (t + 1))
@@ -179,7 +175,7 @@ def tile_list_warhead_site_triage_kernel(
                     rhs=v2[:].bitcast(FP8X4), rhs_scale=v2s[:], start=True, stop=True,
                 )
                 nc.vector.tensor_tensor(x[:, t, :], site_ps[:], biased[t][:], MULT)
-            gl = tile("gl%d" % g, [P, S, PACK], F32)
+            gl = tile("gl%d" % g, [P, S, PACK], F32, after)
             for half in halves:
                 nc.scalar.activation(
                     gl[:, half, :].rearrange("p (c i) t -> p c t i", i=4),
@@ -188,18 +184,22 @@ def tile_list_warhead_site_triage_kernel(
                 )
             return gl
 
-        def scaled(g, gl, after):
+        def scaled(g, gl, engine, pieces, after):
             hb = tile("hb%d" % g, [P, S, PACK], BF16, after)
-            factor = gaint[:, g : g + 1, :].to_broadcast([P, S // 2, PACK])
-            for half in halves:
-                nc.vector.tensor_tensor(hb[:, half, :], gl[:, half, :], factor, MULT)
+            n = S // pieces
+            factor = gaint[:, g : g + 1, :].to_broadcast([P, n, PACK])
+            for lo in range(0, S, n):
+                engine.tensor_tensor(hb[:, lo : lo + n, :], gl[:, lo : lo + n, :], factor, MULT)
             return hb[:].rearrange("p n t -> p (n t)")
 
         w4q = {}
 
-        def w4_cast(g, lo, hi, after):
+        def w4_cast(g, lo, hi, copy, after):
             grouped = tile("w4_bf%d_%d" % (g, lo), [P, PACK * (hi - lo)], BF16, after)
-            cast_w4(g, lo, hi, grouped[:])
+            copy(
+                out=grouped[:].rearrange("p (c i j) -> p c j i", i=4, j=PACK),
+                in_=w4_raw[g, lo][:].rearrange("p j (c i) -> p c j i", i=4),
+            )
             return grouped
 
         def w4_quantise(g, lo, hi, grouped, after=None):
@@ -211,24 +211,19 @@ def tile_list_warhead_site_triage_kernel(
         w3_bf1 = cast_w3(1, w3_second)
         gl0 = gelus(0, biased0)
         biased1 = buffers(1, quantise("w3q1", w3_bf1[:], KP))
+        hb0 = scaled(0, gl0, nc.gpsimd, 4, None)
         v1 = [gather("v1_0", t1[0][:].bitcast(U32), l1, U32, "bufb0_3")]
-        gl1 = gelus(1, biased1)
-        hb0 = scaled(0, gl0, "t1_0")
-        v1s = gather("v1s", s1[:], l1, U8, "bufb1_3")
-        hq = [quantise("hq0", hb0, S)]
-        hb1 = scaled(1, gl1, "s1")
-        w4_bf0 = w4_cast(0, 0, N, "x1")
+        v1s = gather("v1s", s1[:], l1, U8, "bufb0_2")
+        w4_first = w4_cast(0, 0, 512, nc.scalar.copy, "x0")
+        gl1 = gelus(1, biased1, "w4_raw0_0")
+        w4_quantise(0, 512, N, w4_cast(0, 512, N, nc.vector.tensor_copy, "bufb1_3")[:])
+        v1.append(gather("v1_1", t1[1][:].bitcast(U32), l1, U32, "bufb1_2"))
+        w4_quantise(0, 0, 512, w4_first[:])
+        hb1 = scaled(1, gl1, nc.vector, 2, "t1_1")
+        hq = [quantise("hq0", hb0, S, "x1")]
         hq.append(quantise("hq1", hb1, S))
-        w4_quantise(0, 0, 512, w4_bf0[:, 0 : PACK * 512])
-        w4_quantise(0, 512, N, w4_bf0[:, PACK * 512 : PACK * N])
-        last = tile("v1_1", [P, S], U32)
-        for u in range(2):
-            nc.vector.tensor_copy(
-                last[:, 256 * u : 256 * (u + 1)], t1[1][:].bitcast(U32).indirect(l1[:, 16 * u : 16 * (u + 1)])
-            )
-        v1.append(last)
-        w4_quantise(1, 0, 512, w4_cast(1, 0, 512, "w4_raw0")[:], "t1_1")
-        w4_quantise(1, 512, N, w4_cast(1, 512, N, "gl1")[:])
+        w4_quantise(1, 512, N, w4_cast(1, 512, N, nc.vector.tensor_copy, "w4_raw0_0")[:])
+        w4_quantise(1, 0, 512, w4_cast(1, 0, 512, nc.scalar.copy, "w4_raw0_512")[:])
 
         def w4_pass(acc, g, c):
             (codes, scales), part = w4q[g, c]
@@ -237,23 +232,17 @@ def tile_list_warhead_site_triage_kernel(
                 rhs=hq[g][0][:].bitcast(FP8X4), rhs_scale=hq[g][1][:], start=False, stop=(g == 1),
             )
 
-        def wr_pass(acc, a, c, lo=0, hi=S):
-            cols = slice(P * c, P * (c + 1))
-            nc.tensor.matmul_mx(
-                out=acc[:, lo:hi], lhsT=wrw[a][:, cols].bitcast(FP8X4), lhsT_scale=swr[4 * a : P, cols],
-                rhs=v1[a][:, lo:hi].bitcast(FP8X4), rhs_scale=v1s[4 * a : P, lo:hi],
-                start=(a == 0), stop=False,
-            )
-
         accs = [ps.tile([P, S], F32, name="acc%d" % c, tag="bank%d" % c) for c in range(N // P)]
-        for c in range(N // P):
-            wr_pass(accs[c], 0, c)
+        for a in range(2):
+            for c in range(N // P):
+                cols = slice(P * c, P * (c + 1))
+                nc.tensor.matmul_mx(
+                    out=accs[c][:], lhsT=wrw[a][:, cols].bitcast(FP8X4), lhsT_scale=swr[4 * a : P, cols],
+                    rhs=v1[a][:].bitcast(FP8X4), rhs_scale=v1s[4 * a : P, :], start=(a == 0), stop=False,
+                )
         for c in range(N // P):
             w4_pass(accs[c], 0, c)
-        for lo in range(0, S, 256):
-            for c in range(N // P):
-                wr_pass(accs[c], 1, c, lo, lo + 256)
-        for c in range(N // P):
+        for c in [4, 5, 0, 1, 2, 3]:
             w4_pass(accs[c], 1, c)
             res = tile("res%d" % c, [P, S], F32)
             if c % 2 == 0:

@@ -1,3 +1,4 @@
+import math
 from contextlib import ExitStack
 
 import concourse.mybir as mybir
@@ -17,9 +18,12 @@ ACT = mybir.ActivationFunctionType
 MULT = mybir.AluOpType.mult
 ADD = mybir.AluOpType.add
 
+BYTES_OF = {F32: 4, I32: 4, U32: 4, BF16: 2, U16: 2, U8: 1}
+
 P = 128
 PACK = 4
 KP = P * PACK
+RES_ROW = 8
 
 
 def tile_list_warhead_site_triage_kernel(
@@ -28,25 +32,37 @@ def tile_list_warhead_site_triage_kernel(
 ):
     nc = tc.nc
     with ExitStack() as ctx:
+        lists = ctx.enter_context(tc.tile_pool(name="lists", bufs=1))
         sb = ctx.enter_context(tc.tile_pool(name="sb", bufs=1))
         ps = ctx.enter_context(tc.psum_pool(name="ps", bufs=1))
 
+        place = {"free": 0}
+
         def tile(name, shape, dtype, after=None):
-            return sb.tile(shape, dtype, name=name, tag=after or name, align_bytes=64)
+            if after is None:
+                place[name] = place["free"]
+                place["free"] = place["free"] + -(-math.prod(shape[1:]) * BYTES_OF[dtype] // 64) * 64
+            else:
+                place[name] = place[after[0]] + after[1]
+            return sb.tile(shape, dtype, name=name, align_bytes=64, offset=place[name])
+
+        def bank(name, b):
+            return ps.tile([P, S], F32, name=name, tag="bank%d" % b)
 
         def zeroed_plane(name, width, engine):
             plane = tile(name, [P, width], U8)
             engine.memset(plane[:].bitcast(I32), 0)
             return plane
 
-        def load_plane(queue, plane, scales):
+        def load_plane(queue, plane, scales, first):
             passes = scales.shape[0]
             for q in range(4):
                 src = scales[0, 4 * q : 4 * q + 4, :] if passes == 1 else scales[:, 4 * q : 4 * q + 4, :]
-                queue.dma_start(out=plane[32 * q : 32 * q + 4 * passes, :].bitcast(I32), in_=src.bitcast(I32))
+                rows = slice(32 * q + first, 32 * q + first + 4 * passes)
+                queue.dma_start(out=plane[rows, :].bitcast(I32), in_=src.bitcast(I32))
 
         def load_list(name, src):
-            lst = sb.tile([P, S // 16], U16, name=name)
+            lst = lists.tile([P, S // 16], U16, name=name)
             nc.sync.dma_start(lst[:], src)
             return lst
 
@@ -57,30 +73,23 @@ def tile_list_warhead_site_triage_kernel(
 
         warm_in = tile("warm_in", [P, 1], F32)
         warm_out = tile("warm_out", [P, 1], F32)
-        nc.gpsimd.memset(warm_in[:], 0.0)
+        nc.vector.memset(warm_in[:], 0.0)
         nc.scalar.activation(warm_out[:], warm_in[:], ACT.Gelu_apprx_tanh)
 
         s3 = zeroed_plane("s3", T3, nc.gpsimd)
-        sw2 = zeroed_plane("sw2", H, nc.gpsimd)
-        s2 = zeroed_plane("s2", T2, nc.vector)
         s1 = zeroed_plane("s1", T, nc.gpsimd)
-        swr = zeroed_plane("swr", N, nc.gpsimd)
-
-        w3v = w3.rearrange("(p j) c -> p j c", j=PACK)
+        s2 = zeroed_plane("s2", T2, nc.vector)
+        sw2 = zeroed_plane("sw2", H, nc.vector)
+        swr = zeroed_plane("swr", N, nc.vector)
 
         def load_words(name, words):
             held = tile(name, [P, words.shape[1]], I32)
             nc.sync.dma_start(out=held[:], in_=words.rearrange("p t i -> p (t i)").bitcast(I32))
             return held
 
-        def load_w3(lo, hi):
-            raw = tile("w3_raw%d" % lo, [P, PACK, hi - lo], F32)
-            nc.sync.dma_start(out=raw[:], in_=w3v[:, :, lo:hi])
-            return raw
-
-        def load_w4(g, lo, hi):
-            raw = tile("w4_raw%d_%d" % (g, lo), [P, PACK, hi - lo], F32)
-            nc.sync.dma_start(out=raw[:], in_=w4[KP * g : KP * (g + 1), lo:hi].rearrange("(p j) n -> p j n", j=PACK))
+        def load_rows(name, w, g, lo, hi):
+            raw = tile(name, [P, PACK, hi - lo], F32)
+            nc.sync.dma_start(out=raw[:], in_=w[KP * g : KP * (g + 1), lo:hi].rearrange("(p j) n -> p j n", j=PACK))
             return raw
 
         def load_channels(name, vec):
@@ -88,32 +97,31 @@ def tile_list_warhead_site_triage_kernel(
             nc.sync.dma_start(out=held[:], in_=vec.rearrange("(g p t) -> p g t", g=2, t=PACK))
             return held
 
+        l3 = load_list("l3", offs3)
         t3 = tile("t3", [P, T3], U16)
         nc.sync.dma_start(out=t3[:].bitcast(I32), in_=tab3_words[0].bitcast(I32))
-        l3 = load_list("l3", offs3)
-        w3_first = [load_w3(0, 256)]
-        load_plane(nc.sync, s3, tab3_scales)
-        w3_first.append(load_w3(256, KP))
+        load_plane(nc.sync, s3, tab3_scales, 0)
+        w3_raw = [load_rows("w3_raw%d" % u, w3, 0, 256 * u, 256 * (u + 1)) for u in range(2)]
+        l2 = load_list("l2", offs2)
+        load_plane(nc.sync, s2, tab2_scales, 0)
+        w3_raw.append(load_rows("w3_raw2", w3, 0, 512, 768))
         w2w = tile("w2w", [P, H], U16)
         nc.sync.dma_start(out=w2w[:].bitcast(I32), in_=w2_words[0].bitcast(I32))
-        l2 = load_list("l2", offs2)
-        load_plane(nc.sync, s2, tab2_scales)
-        t2 = load_words("t2", tab2_words[0])
-        load_plane(nc.sync, sw2, w2_scales)
+        w3_raw.append(load_rows("w3_raw3", w3, 0, 768, H))
         b3t = load_channels("b3t", b3)
-        w3_second = [load_w3(KP, KP + 256), load_w3(KP + 256, H)]
         l1 = load_list("l1", offs)
-        t1 = [load_words("t1_0", tab_words[0])]
+        t2 = load_words("t2", tab2_words[0])
+        load_plane(nc.sync, sw2, w2_scales, 0)
         gaint = load_channels("gaint", gain)
-        load_plane(nc.sync, s1, tab_scales)
+        w4_raw0 = [load_rows("w4_raw0a", w4, 0, 0, 512)]
+        load_plane(nc.sync, s1, tab_scales, RES_ROW)
+        w4_raw0.append(load_rows("w4_raw0b", w4, 0, 512, N))
+        t1 = [load_words("t1_0", tab_words[0])]
+        load_plane(nc.sync, swr, wr_scales, RES_ROW)
         wrw = [load_words("wrw0", wr_words[0])]
-        w4_raw = {(0, 0): load_w4(0, 0, 512)}
-        load_plane(nc.sync, swr, wr_scales)
-        w4_raw[0, 512] = load_w4(0, 512, N)
         t1.append(load_words("t1_1", tab_words[1]))
         wrw.append(load_words("wrw1", wr_words[1]))
-        w4_raw[1, 0] = load_w4(1, 0, 512)
-        w4_raw[1, 512] = load_w4(1, 512, N)
+        w4_raw1 = [load_rows("w4_raw1_%d" % u, w4, 1, 256 * u, 256 * (u + 1)) for u in range(3)]
         bot = tile("bot", [P, N // P], F32)
         with nc.allow_non_contiguous_dma(reason="one bias value a partition"):
             nc.sync.dma_start(out=bot[:], in_=bo.rearrange("(c p) -> p c", p=P))
@@ -124,58 +132,65 @@ def tile_list_warhead_site_triage_kernel(
             nc.vector.quantize_mx(out=codes[:].bitcast(FP8X4), scales=scales[:], in_=src)
             return codes, scales
 
-        def cast_w3(g, parts):
+        def w3_cast(g):
             grouped = tile("w3_bf%d" % g, [P, PACK * KP], BF16)
             dst = grouped[:].rearrange("p (t m j) -> p m j t", t=PACK, j=PACK)
-            n = P // len(parts)
-            for u, raw in enumerate(parts):
-                nc.scalar.copy(out=dst[:, n * u : n * (u + 1)], in_=raw[:].rearrange("p j (m t) -> p m j t", t=PACK))
+            for u in range(2):
+                src = w3_raw[2 * g + u][:].rearrange("p j (m t) -> p m j t", t=PACK)
+                nc.scalar.copy(out=dst[:, 64 * u : 64 * (u + 1)], in_=src)
             return grouped
 
-        w3_bf0 = cast_w3(0, w3_first)
+        w3_bf = [w3_cast(0), w3_cast(1)]
         v3 = gather("v3", t3[:], l3, U16)
         v3s = gather("v3s", s3[:], l3, U8)
+        v2s = gather("v2s", s2[:], l2, U8)
+        w3q = [quantise("w3q0", w3_bf[0][:], KP, ("s2", 0))]
         w2p = tile("w2p", [P, H], U16)
         nc.vector.tensor_copy(
             out=w2p[:].rearrange("p (g t m) -> p g t m", g=2, t=PACK),
             in_=w2w[:].rearrange("p (g m t) -> p g t m", g=2, t=PACK),
         )
-        w3q0 = quantise("w3q0", w3_bf0[:], KP)
-        v2s = gather("v2s", s2[:], l2, U8)
+        w3q.append(quantise("w3q1", w3_bf[1][:], KP))
         v2 = gather("v2", t2[:].bitcast(U32), l2, U32)
-        w2s = tile("w2s", [P, H], U8)
+        w2s = tile("w2s", [P, H], U8, ("t2", 0))
         nc.vector.tensor_copy(
             out=w2s[:].rearrange("p (g t m) -> p g t m", g=2, t=PACK),
             in_=sw2[:].rearrange("p (g m t) -> p g t m", g=2, t=PACK),
         )
 
-        def buffers(g, w3q):
-            biased = []
+        def buf_pass(g, t, b):
+            cols = slice(P * t, P * (t + 1))
+            acc = bank("buf_ps", b)
+            nc.tensor.matmul_mx(
+                out=acc[:], lhsT=w3q[g][0][:, cols].bitcast(FP8X4), lhsT_scale=w3q[g][1][:, cols],
+                rhs=v3[:].bitcast(FP4X4), rhs_scale=v3s[:], start=True, stop=True,
+            )
+            return acc
+
+        def site_pass(g, t, b):
+            cols = slice(KP * g + P * t, KP * g + P * (t + 1))
+            acc = bank("site_ps", b)
+            nc.tensor.matmul_mx(
+                out=acc[:], lhsT=w2p[:, cols].bitcast(FP4X4), lhsT_scale=w2s[:, cols],
+                rhs=v2[:].bitcast(FP8X4), rhs_scale=v2s[:], start=True, stop=True,
+            )
+            return acc
+
+        def biased(g, t):
+            held = tile("buf%d_%d" % (g, t), [P, S], F32)
+            nc.scalar.activation(held[:], buf_pass(g, t, PACK * g + t)[:], ACT.Identity, bias=b3t[:, g, t : t + 1])
+            return held
+
+        def products(g, bufs):
+            x = tile("x%d" % g, [P, PACK, S], F32)
             for t in range(PACK):
-                cols = slice(P * t, P * (t + 1))
-                buf_ps = ps.tile([P, S], F32, name="buf_ps", tag="bank%d" % t)
-                nc.tensor.matmul_mx(
-                    out=buf_ps[:], lhsT=w3q[0][:, cols].bitcast(FP8X4), lhsT_scale=w3q[1][:, cols],
-                    rhs=v3[:].bitcast(FP4X4), rhs_scale=v3s[:], start=True, stop=True,
-                )
-                bufb = tile("bufb%d_%d" % (g, t), [P, S], F32)
-                nc.scalar.activation(bufb[:], buf_ps[:], ACT.Identity, bias=b3t[:, g, t : t + 1])
-                biased.append(bufb)
-            return biased
+                nc.vector.tensor_tensor(x[:, t, :], site_pass(g, t, PACK * g + t)[:], bufs[t][:], MULT)
+            return x
 
         halves = [slice(0, S // 2), slice(S // 2, S)]
 
-        def gelus(g, biased, after=None):
-            x = tile("x%d" % g, [P, PACK, S], F32)
-            for t in range(PACK):
-                wide = slice(KP * g + P * t, KP * g + P * (t + 1))
-                site_ps = ps.tile([P, S], F32, name="site_ps", tag="bank%d" % (4 + t))
-                nc.tensor.matmul_mx(
-                    out=site_ps[:], lhsT=w2p[:, wide].bitcast(FP4X4), lhsT_scale=w2s[:, wide],
-                    rhs=v2[:].bitcast(FP8X4), rhs_scale=v2s[:], start=True, stop=True,
-                )
-                nc.vector.tensor_tensor(x[:, t, :], site_ps[:], biased[t][:], MULT)
-            gl = tile("gl%d" % g, [P, S, PACK], F32, after)
+        def gelus(g, x):
+            gl = tile("gl%d" % g, [P, S, PACK], F32)
             for half in halves:
                 nc.scalar.activation(
                     gl[:, half, :].rearrange("p (c i) t -> p c t i", i=4),
@@ -184,69 +199,106 @@ def tile_list_warhead_site_triage_kernel(
                 )
             return gl
 
-        def scaled(g, gl, engine, pieces, after):
-            hb = tile("hb%d" % g, [P, S, PACK], BF16, after)
-            n = S // pieces
-            factor = gaint[:, g : g + 1, :].to_broadcast([P, n, PACK])
-            for lo in range(0, S, n):
-                engine.tensor_tensor(hb[:, lo : lo + n, :], gl[:, lo : lo + n, :], factor, MULT)
-            return hb[:].rearrange("p n t -> p (n t)")
+        def scale(hb, g, gl, engine, lo, hi):
+            factor = gaint[:, g : g + 1, :].to_broadcast([P, hi - lo, PACK])
+            engine.tensor_tensor(hb, gl[:, lo:hi, :], factor, MULT)
+
+        def w4_cast(grouped, lo, raw, raw_lo, copy):
+            copy(
+                out=grouped[:, PACK * lo : PACK * (lo + 256)].rearrange("p (c i j) -> p c j i", i=4, j=PACK),
+                in_=raw[:, :, raw_lo : raw_lo + 256].rearrange("p j (c i) -> p c j i", i=4),
+            )
 
         w4q = {}
 
-        def w4_cast(g, lo, hi, copy, after):
-            grouped = tile("w4_bf%d_%d" % (g, lo), [P, PACK * (hi - lo)], BF16, after)
-            copy(
-                out=grouped[:].rearrange("p (c i j) -> p c j i", i=4, j=PACK),
-                in_=w4_raw[g, lo][:].rearrange("p j (c i) -> p c j i", i=4),
-            )
-            return grouped
-
         def w4_quantise(g, lo, hi, grouped, after=None):
-            quantised = quantise("w4q%d_%d" % (g, lo), grouped, hi - lo, after)
+            quantised = quantise("w4q%d_%d" % (g, lo), grouped[:], hi - lo, after)
             for c in range(lo // P, hi // P):
                 w4q[g, c] = (quantised, slice(P * c - lo, P * (c + 1) - lo))
 
-        biased0 = buffers(0, w3q0)
-        w3_bf1 = cast_w3(1, w3_second)
-        gl0 = gelus(0, biased0)
-        biased1 = buffers(1, quantise("w3q1", w3_bf1[:], KP))
-        hb0 = scaled(0, gl0, nc.gpsimd, 4, None)
-        v1 = [gather("v1_0", t1[0][:].bitcast(U32), l1, U32, "bufb0_3")]
-        v1s = gather("v1s", s1[:], l1, U8, "bufb0_2")
-        w4_first = w4_cast(0, 0, 512, nc.scalar.copy, "x0")
-        gl1 = gelus(1, biased1, "w4_raw0_0")
-        w4_quantise(0, 512, N, w4_cast(0, 512, N, nc.vector.tensor_copy, "bufb1_3")[:])
-        v1.append(gather("v1_1", t1[1][:].bitcast(U32), l1, U32, "bufb1_2"))
-        w4_quantise(0, 0, 512, w4_first[:])
-        hb1 = scaled(1, gl1, nc.vector, 2, "t1_1")
-        hq = [quantise("hq0", hb0, S, "x1")]
-        hq.append(quantise("hq1", hb1, S))
-        w4_quantise(1, 512, N, w4_cast(1, 512, N, nc.vector.tensor_copy, "w4_raw0_0")[:])
-        w4_quantise(1, 0, 512, w4_cast(1, 0, 512, nc.scalar.copy, "w4_raw0_512")[:])
+        bufs = [[biased(g, t) for t in range(PACK)] for g in range(2)]
+        x0 = products(0, bufs[0])
+        gl0 = gelus(0, x0)
+        x1 = products(1, bufs[1])
+        w4_bf0 = [tile("w4_bf0a", [P, PACK * 512], BF16), tile("w4_bf0b", [P, PACK * 256], BF16)]
+        for part, lo in ((0, 0), (0, 256), (1, 0)):
+            nc.gpsimd.tensor_copy(
+                w4_bf0[part][:, PACK * lo : PACK * (lo + 256)].rearrange("p (c j) -> p c j", j=PACK),
+                w4_raw0[part][:, :, lo : lo + 256].rearrange("p j c -> p c j"),
+            )
+        gl1 = gelus(1, x1)
+        v1s = gather("v1s", s1[:], l1, U8, ("buf1_2", 0))
+        v1 = [gather("v1_0", t1[0][:].bitcast(U32), l1, U32, ("buf1_3", 0))]
+        hb0 = tile("hb0", [P, S, PACK], BF16, ("t1_0", 0))
+        scale(hb0[:], 0, gl0, nc.vector, 0, S)
+        w4_quantise(0, 0, 512, w4_bf0[0], ("t1_0", 4096))
+        hq = [quantise("hq0", hb0[:].rearrange("p n t -> p (n t)"), S, ("w4_bf0a", 0))]
+        w4_quantise(0, 512, N, w4_bf0[1], ("t1_0", 6144))
+        v1.append(gather("v1_1", t1[1][:].bitcast(U32), l1, U32, ("hb0", 0)))
+        w4_bf1 = [tile("w4_bf1_%d" % u, [P, PACK * 256], BF16, ("x1", 2048 * u)) for u in range(3)]
+        for u in range(3):
+            w4_cast(w4_bf1[u], 0, w4_raw1[u], 0, nc.scalar.copy)
+        hq.append((tile("hq1_c", [P, S], U32, ("w4_bf1_0", 0)), tile("hq1_s", [P, S], U8)))
 
-        def w4_pass(acc, g, c):
-            (codes, scales), part = w4q[g, c]
-            nc.tensor.matmul_mx(
-                out=acc[:], lhsT=codes[:, part].bitcast(FP8X4), lhsT_scale=scales[:, part],
-                rhs=hq[g][0][:].bitcast(FP8X4), rhs_scale=hq[g][1][:], start=False, stop=(g == 1),
+        def second_gain(h, after):
+            hb = tile("hb1_%d" % h, [P, S // 2, PACK], BF16, after)
+            scale(hb[:], 1, gl1, nc.vector, halves[h].start, halves[h].stop)
+            return hb
+
+        def second_quantise(h, hb):
+            nc.vector.quantize_mx(
+                out=hq[1][0][:, halves[h]].bitcast(FP8X4), scales=hq[1][1][:, halves[h]],
+                in_=hb[:].rearrange("p n t -> p (n t)"),
             )
 
-        accs = [ps.tile([P, S], F32, name="acc%d" % c, tag="bank%d" % c) for c in range(N // P)]
-        for a in range(2):
-            for c in range(N // P):
-                cols = slice(P * c, P * (c + 1))
-                nc.tensor.matmul_mx(
-                    out=accs[c][:], lhsT=wrw[a][:, cols].bitcast(FP8X4), lhsT_scale=swr[4 * a : P, cols],
-                    rhs=v1[a][:].bitcast(FP8X4), rhs_scale=v1s[4 * a : P, :], start=(a == 0), stop=False,
-                )
+        hb1_first = second_gain(0, ("t1_1", 4096))
+        w4_quantise(1, 0, 256, w4_bf1[0])
+        second_quantise(0, hb1_first)
+        w4_quantise(1, 256, 512, w4_bf1[1])
+        hb1_second = second_gain(1, ("w4_bf1_1", 0))
+        w4_quantise(1, 512, N, w4_bf1[2])
+        second_quantise(1, hb1_second)
+
+        accs = [[bank("acc%d_%d" % (h, b), 3 * h + b) for b in range(3)] for h in range(2)]
+
+        def sums(h, c):
+            return accs[h][c // 2][:, (c % 2) * (S // 2) : (c % 2 + 1) * (S // 2)]
+
+        def wr_pass(a, h, c):
+            cols = slice(P * c, P * (c + 1))
+            rows = slice(RES_ROW + 4 * a, P)
+            nc.tensor.matmul_mx(
+                out=sums(h, c), lhsT=wrw[a][:, cols].bitcast(FP8X4), lhsT_scale=swr[rows, cols],
+                rhs=v1[a][:, halves[h]].bitcast(FP8X4), rhs_scale=v1s[rows, halves[h]],
+                start=(a == 0 and c % 2 == 0), stop=False,
+            )
+
+        def w4_pass(g, h, c):
+            (codes, scales), part = w4q[g, c]
+            nc.tensor.matmul_mx(
+                out=sums(h, c), lhsT=codes[:, part].bitcast(FP8X4), lhsT_scale=scales[:, part],
+                rhs=hq[g][0][:, halves[h]].bitcast(FP8X4), rhs_scale=hq[g][1][:, halves[h]],
+                start=False, stop=(g == 1 and c % 2 == 1),
+            )
+
         for c in range(N // P):
-            w4_pass(accs[c], 0, c)
-        for c in [4, 5, 0, 1, 2, 3]:
-            w4_pass(accs[c], 1, c)
-            res = tile("res%d" % c, [P, S], F32)
-            if c % 2 == 0:
-                nc.scalar.activation(res[:], accs[c][:], ACT.Identity, bias=bot[:, c : c + 1])
-            else:
-                nc.vector.tensor_scalar(res[:], accs[c][:], bot[:, c : c + 1], None, ADD)
-            nc.sync.dma_start(out=out[P * c : P * (c + 1), :], in_=res[:])
+            for h in range(2):
+                wr_pass(0, h, c)
+        for c in range(N // P):
+            for h in range(2):
+                w4_pass(0, h, c)
+        for h in range(2):
+            for c in range(N // P):
+                wr_pass(1, h, c)
+        for h in range(2):
+            for b in range(3):
+                res = tile("res%d_%d" % (h, b), [P, 2, S // 2], F32)
+                for c in (2 * b, 2 * b + 1):
+                    w4_pass(1, h, c)
+                for c in (2 * b, 2 * b + 1):
+                    if h == 0 or b == 1:
+                        nc.scalar.activation(res[:, c % 2, :], sums(h, c), ACT.Identity, bias=bot[:, c : c + 1])
+                    else:
+                        nc.vector.tensor_scalar(res[:, c % 2, :], sums(h, c), bot[:, c : c + 1], None, ADD)
+                rows = out[2 * P * b : 2 * P * (b + 1), halves[h]]
+                nc.sync.dma_start(out=rows.rearrange("(c p) s -> p c s", p=P), in_=res[:])

@@ -97,31 +97,37 @@ def tile_list_warhead_site_triage_kernel(
             nc.sync.dma_start(out=held[:], in_=vec.rearrange("(g p t) -> p g t", g=2, t=PACK))
             return held
 
+        def load_gain(g):
+            held = tile("gain%d" % g, [P, 1, PACK], F32)
+            nc.sync.dma_start(out=held[:, 0, :], in_=gain[KP * g : KP * (g + 1)].rearrange("(p t) -> p t", t=PACK))
+            return held
+
         l3 = load_list("l3", offs3)
+        load_plane(nc.sync, s3, tab3_scales, 0)
+        l2 = load_list("l2", offs2)
         t3 = tile("t3", [P, T3], U16)
         nc.sync.dma_start(out=t3[:].bitcast(I32), in_=tab3_words[0].bitcast(I32))
-        load_plane(nc.sync, s3, tab3_scales, 0)
-        w3_raw = [load_rows("w3_raw%d" % u, w3, 0, 256 * u, 256 * (u + 1)) for u in range(2)]
-        l2 = load_list("l2", offs2)
+        w3_raw = [load_rows("w3_raw0", w3, 0, 0, KP)]
         load_plane(nc.sync, s2, tab2_scales, 0)
-        w3_raw.append(load_rows("w3_raw2", w3, 0, 512, 768))
+        l1 = load_list("l1", offs)
+        w3_raw.append(load_rows("w3_raw1", w3, 0, KP, H))
         w2w = tile("w2w", [P, H], U16)
         nc.sync.dma_start(out=w2w[:].bitcast(I32), in_=w2_words[0].bitcast(I32))
-        w3_raw.append(load_rows("w3_raw3", w3, 0, 768, H))
         b3t = load_channels("b3t", b3)
-        l1 = load_list("l1", offs)
-        t2 = load_words("t2", tab2_words[0])
         load_plane(nc.sync, sw2, w2_scales, 0)
-        gaint = load_channels("gaint", gain)
+        t2 = load_words("t2", tab2_words[0])
         w4_raw0 = [load_rows("w4_raw0a", w4, 0, 0, 512)]
         load_plane(nc.sync, s1, tab_scales, RES_ROW)
-        w4_raw0.append(load_rows("w4_raw0b", w4, 0, 512, N))
         t1 = [load_words("t1_0", tab_words[0])]
+        place["free"] = place["free"] + 4096
+        gains = [load_gain(0)]
+        w4_raw0.append(load_rows("w4_raw0b", w4, 0, 512, N))
         load_plane(nc.sync, swr, wr_scales, RES_ROW)
         wrw = [load_words("wrw0", wr_words[0])]
+        w4_raw1 = [load_rows("w4_raw1a", w4, 1, 0, 256), load_rows("w4_raw1b", w4, 1, 256, N)]
         t1.append(load_words("t1_1", tab_words[1]))
+        gains.append(load_gain(1))
         wrw.append(load_words("wrw1", wr_words[1]))
-        w4_raw1 = [load_rows("w4_raw1_%d" % u, w4, 1, 256 * u, 256 * (u + 1)) for u in range(3)]
         bot = tile("bot", [P, N // P], F32)
         with nc.allow_non_contiguous_dma(reason="one bias value a partition"):
             nc.sync.dma_start(out=bot[:], in_=bo.rearrange("(c p) -> p c", p=P))
@@ -134,10 +140,10 @@ def tile_list_warhead_site_triage_kernel(
 
         def w3_cast(g):
             grouped = tile("w3_bf%d" % g, [P, PACK * KP], BF16)
-            dst = grouped[:].rearrange("p (t m j) -> p m j t", t=PACK, j=PACK)
-            for u in range(2):
-                src = w3_raw[2 * g + u][:].rearrange("p j (m t) -> p m j t", t=PACK)
-                nc.scalar.copy(out=dst[:, 64 * u : 64 * (u + 1)], in_=src)
+            nc.scalar.copy(
+                out=grouped[:].rearrange("p (t m j) -> p m j t", t=PACK, j=PACK),
+                in_=w3_raw[g][:].rearrange("p j (m t) -> p m j t", t=PACK),
+            )
             return grouped
 
         w3_bf = [w3_cast(0), w3_cast(1)]
@@ -150,13 +156,13 @@ def tile_list_warhead_site_triage_kernel(
             out=w2p[:].rearrange("p (g t m) -> p g t m", g=2, t=PACK),
             in_=w2w[:].rearrange("p (g m t) -> p g t m", g=2, t=PACK),
         )
-        w3q.append(quantise("w3q1", w3_bf[1][:], KP))
-        v2 = gather("v2", t2[:].bitcast(U32), l2, U32)
-        w2s = tile("w2s", [P, H], U8, ("t2", 0))
+        w2s = tile("w2s", [P, H], U8)
         nc.vector.tensor_copy(
             out=w2s[:].rearrange("p (g t m) -> p g t m", g=2, t=PACK),
             in_=sw2[:].rearrange("p (g m t) -> p g t m", g=2, t=PACK),
         )
+        w3q.append(quantise("w3q1", w3_bf[1][:], KP))
+        v2 = gather("v2", t2[:].bitcast(U32), l2, U32)
 
         def buf_pass(g, t, b):
             cols = slice(P * t, P * (t + 1))
@@ -181,8 +187,8 @@ def tile_list_warhead_site_triage_kernel(
             nc.scalar.activation(held[:], buf_pass(g, t, PACK * g + t)[:], ACT.Identity, bias=b3t[:, g, t : t + 1])
             return held
 
-        def products(g, bufs):
-            x = tile("x%d" % g, [P, PACK, S], F32)
+        def products(g, bufs, after=None):
+            x = tile("x%d" % g, [P, PACK, S], F32, after)
             for t in range(PACK):
                 nc.vector.tensor_tensor(x[:, t, :], site_pass(g, t, PACK * g + t)[:], bufs[t][:], MULT)
             return x
@@ -200,7 +206,7 @@ def tile_list_warhead_site_triage_kernel(
             return gl
 
         def scale(hb, g, gl, engine, lo, hi):
-            factor = gaint[:, g : g + 1, :].to_broadcast([P, hi - lo, PACK])
+            factor = gains[g][:].to_broadcast([P, hi - lo, PACK])
             engine.tensor_tensor(hb, gl[:, lo:hi, :], factor, MULT)
 
         def w4_cast(grouped, lo, raw, raw_lo, copy):
@@ -219,26 +225,31 @@ def tile_list_warhead_site_triage_kernel(
         bufs = [[biased(g, t) for t in range(PACK)] for g in range(2)]
         x0 = products(0, bufs[0])
         gl0 = gelus(0, x0)
-        x1 = products(1, bufs[1])
         w4_bf0 = [tile("w4_bf0a", [P, PACK * 512], BF16), tile("w4_bf0b", [P, PACK * 256], BF16)]
-        for part, lo in ((0, 0), (0, 256), (1, 0)):
+        for lo in (0, 256):
             nc.gpsimd.tensor_copy(
-                w4_bf0[part][:, PACK * lo : PACK * (lo + 256)].rearrange("p (c j) -> p c j", j=PACK),
-                w4_raw0[part][:, :, lo : lo + 256].rearrange("p j c -> p c j"),
+                w4_bf0[0][:, PACK * lo : PACK * (lo + 256)].rearrange("p (c j) -> p c j", j=PACK),
+                w4_raw0[0][:, :, lo : lo + 256].rearrange("p j c -> p c j"),
             )
+        v1s = gather("v1s", s1[:], l1, U8)
+        v1 = [gather("v1_0", t1[0][:].bitcast(U32), l1, U32)]
+        x1 = products(1, bufs[1], ("t1_0", 4096))
+        w4_cast(w4_bf0[1], 0, w4_raw0[1], 0, nc.scalar.copy)
+        w4_bf1 = [tile("w4_bf1_0", [P, PACK * 256], BF16)]
+        w4_cast(w4_bf1[0], 0, w4_raw1[0], 0, nc.scalar.copy)
         gl1 = gelus(1, x1)
-        v1s = gather("v1s", s1[:], l1, U8, ("buf1_2", 0))
-        v1 = [gather("v1_0", t1[0][:].bitcast(U32), l1, U32, ("buf1_3", 0))]
         hb0 = tile("hb0", [P, S, PACK], BF16, ("t1_0", 0))
-        scale(hb0[:], 0, gl0, nc.vector, 0, S)
-        w4_quantise(0, 0, 512, w4_bf0[0], ("t1_0", 4096))
-        hq = [quantise("hq0", hb0[:].rearrange("p n t -> p (n t)"), S, ("w4_bf0a", 0))]
-        w4_quantise(0, 512, N, w4_bf0[1], ("t1_0", 6144))
-        v1.append(gather("v1_1", t1[1][:].bitcast(U32), l1, U32, ("hb0", 0)))
-        w4_bf1 = [tile("w4_bf1_%d" % u, [P, PACK * 256], BF16, ("x1", 2048 * u)) for u in range(3)]
-        for u in range(3):
-            w4_cast(w4_bf1[u], 0, w4_raw1[u], 0, nc.scalar.copy)
-        hq.append((tile("hq1_c", [P, S], U32, ("w4_bf1_0", 0)), tile("hq1_s", [P, S], U8)))
+        for lo in (0, 128):
+            scale(hb0[:, lo : lo + 128, :], 0, gl0, nc.gpsimd, lo, lo + 128)
+        scale(hb0[:, halves[1], :], 0, gl0, nc.vector, S // 2, S)
+        w4_quantise(0, 0, 512, w4_bf0[0], ("buf1_2", 0))
+        w4_quantise(0, 512, N, w4_bf0[1], ("buf1_1", 0))
+        hq = [quantise("hq0", hb0[:].rearrange("p n t -> p (n t)"), S)]
+        v1.append(gather("v1_1", t1[1][:].bitcast(U32), l1, U32))
+        for u in range(2):
+            w4_bf1.append(tile("w4_bf1_%d" % (u + 1), [P, PACK * 256], BF16, ("x1", 2048 * u)))
+            w4_cast(w4_bf1[u + 1], 0, w4_raw1[1], 256 * u, nc.scalar.copy)
+        hq.append((tile("hq1_c", [P, S], U32), tile("hq1_s", [P, S], U8)))
 
         def second_gain(h, after):
             hb = tile("hb1_%d" % h, [P, S // 2, PACK], BF16, after)
@@ -251,12 +262,12 @@ def tile_list_warhead_site_triage_kernel(
                 in_=hb[:].rearrange("p n t -> p (n t)"),
             )
 
-        hb1_first = second_gain(0, ("t1_1", 4096))
-        w4_quantise(1, 0, 256, w4_bf1[0])
+        hb1_first = second_gain(0, None)
+        w4_quantise(1, 0, 256, w4_bf1[0], ("t1_1", 0))
         second_quantise(0, hb1_first)
-        w4_quantise(1, 256, 512, w4_bf1[1])
-        hb1_second = second_gain(1, ("w4_bf1_1", 0))
-        w4_quantise(1, 512, N, w4_bf1[2])
+        w4_quantise(1, 256, 512, w4_bf1[1], ("t1_1", 1024))
+        hb1_second = second_gain(1, None)
+        w4_quantise(1, 512, N, w4_bf1[2], ("t1_1", 2048))
         second_quantise(1, hb1_second)
 
         accs = [[bank("acc%d_%d" % (h, b), 3 * h + b) for b in range(3)] for h in range(2)]
@@ -290,15 +301,14 @@ def tile_list_warhead_site_triage_kernel(
         for h in range(2):
             for c in range(N // P):
                 wr_pass(1, h, c)
-        for h in range(2):
-            for b in range(3):
-                res = tile("res%d_%d" % (h, b), [P, 2, S // 2], F32)
-                for c in (2 * b, 2 * b + 1):
-                    w4_pass(1, h, c)
-                for c in (2 * b, 2 * b + 1):
-                    if h == 0 or b == 1:
-                        nc.scalar.activation(res[:, c % 2, :], sums(h, c), ACT.Identity, bias=bot[:, c : c + 1])
-                    else:
-                        nc.vector.tensor_scalar(res[:, c % 2, :], sums(h, c), bot[:, c : c + 1], None, ADD)
-                rows = out[2 * P * b : 2 * P * (b + 1), halves[h]]
-                nc.sync.dma_start(out=rows.rearrange("(c p) s -> p c s", p=P), in_=res[:])
+        for h, b in ((0, 0), (0, 1), (0, 2), (1, 0), (1, 1), (1, 2)):
+            res = tile("res%d_%d" % (h, b), [P, 2, S // 2], F32)
+            for c in (2 * b, 2 * b + 1):
+                w4_pass(1, h, c)
+            for c in (2 * b, 2 * b + 1):
+                if (h, b) in ((1, 0), (1, 2)):
+                    nc.vector.tensor_scalar(res[:, c % 2, :], sums(h, c), bot[:, c : c + 1], None, ADD)
+                else:
+                    nc.scalar.activation(res[:, c % 2, :], sums(h, c), ACT.Identity, bias=bot[:, c : c + 1])
+            rows = out[2 * P * b : 2 * P * (b + 1), halves[h]]
+            nc.sync.dma_start(out=rows.rearrange("(c p) s -> p c s", p=P), in_=res[:])

@@ -17,12 +17,15 @@ FP4X4 = mybir.dt.float4_e2m1fn_x4
 ACT = mybir.ActivationFunctionType
 MULT = mybir.AluOpType.mult
 ADD = mybir.AluOpType.add
-
 BYTES_OF = {F32: 4, I32: 4, U32: 4, BF16: 2, U16: 2, U8: 1}
 
 P = 128
 PACK = 4
 KP = P * PACK
+ALIGN = 64
+RUN = 4
+HALF = S // 2
+PIECE = 2 * P
 RES_ROW = 8
 
 
@@ -41,50 +44,50 @@ def tile_list_warhead_site_triage_kernel(
         def tile(name, shape, dtype, after=None):
             if after is None:
                 place[name] = place["free"]
-                place["free"] = place["free"] + -(-math.prod(shape[1:]) * BYTES_OF[dtype] // 64) * 64
+                place["free"] = place["free"] + math.ceil(math.prod(shape[1:]) * BYTES_OF[dtype] / ALIGN) * ALIGN
             else:
                 place[name] = place[after[0]] + after[1]
-            return sb.tile(shape, dtype, name=name, align_bytes=64, offset=place[name])
+            return sb.tile(shape, dtype, name=name, align_bytes=ALIGN, offset=place[name])
 
         def bank(name, b):
             return ps.tile([P, S], F32, name=name, tag="bank%d" % b)
-
-        def zeroed_plane(name, width, engine):
-            plane = tile(name, [P, width], U8)
-            engine.memset(plane[:].bitcast(I32), 0)
-            return plane
-
-        def load_plane(queue, plane, scales, first):
-            passes = scales.shape[0]
-            for q in range(4):
-                src = scales[0, 4 * q : 4 * q + 4, :] if passes == 1 else scales[:, 4 * q : 4 * q + 4, :]
-                rows = slice(32 * q + first, 32 * q + first + 4 * passes)
-                queue.dma_start(out=plane[rows, :].bitcast(I32), in_=src.bitcast(I32))
-
-        def load_list(name, src):
-            lst = lists.tile([P, S // 16], U16, name=name)
-            nc.sync.dma_start(lst[:], src)
-            return lst
-
-        def gather(name, window, lst, dtype, after=None):
-            got = tile(name, [P, S], dtype, after)
-            nc.vector.tensor_copy(got[:], window.indirect(lst[:]))
-            return got
 
         warm_in = tile("warm_in", [P, 1], F32)
         warm_out = tile("warm_out", [P, 1], F32)
         nc.vector.memset(warm_in[:], 0.0)
         nc.scalar.activation(warm_out[:], warm_in[:], ACT.Gelu_apprx_tanh)
 
-        s3 = zeroed_plane("s3", T3, nc.gpsimd)
-        s1 = zeroed_plane("s1", T, nc.gpsimd)
-        s2 = zeroed_plane("s2", T2, nc.vector)
-        sw2 = zeroed_plane("sw2", H, nc.vector)
-        swr = zeroed_plane("swr", N, nc.vector)
+        def scale_tile(name, width, engine):
+            held = tile(name, [P, width], U8)
+            engine.memset(held[:].bitcast(I32), 0)
+            return held
 
-        def load_words(name, words):
+        s3 = scale_tile("s3", T3, nc.gpsimd)
+        s1 = scale_tile("s1", T, nc.gpsimd)
+        s2 = scale_tile("s2", T2, nc.vector)
+        sw2 = scale_tile("sw2", H, nc.vector)
+        swr = scale_tile("swr", N, nc.vector)
+
+        def load_scales(queue, held, scales, first):
+            passes = scales.shape[0]
+            for q in range(4):
+                src = scales[0, 4 * q : 4 * q + 4, :] if passes == 1 else scales[:, 4 * q : 4 * q + 4, :]
+                rows = slice(32 * q + first, 32 * q + first + 4 * passes)
+                queue.dma_start(out=held[rows, :].bitcast(I32), in_=src.bitcast(I32))
+
+        def load_list(name, src):
+            lst = lists.tile([P, S // 16], U16, name=name)
+            nc.sync.dma_start(lst[:], src)
+            return lst
+
+        def load_fp8_words(name, words):
             held = tile(name, [P, words.shape[1]], I32)
             nc.sync.dma_start(out=held[:], in_=words.rearrange("p t i -> p (t i)").bitcast(I32))
+            return held
+
+        def load_fp4_words(name, words):
+            held = tile(name, [P, words.shape[1] // 2], U16)
+            nc.sync.dma_start(out=held[:].bitcast(I32), in_=words.bitcast(I32))
             return held
 
         def load_rows(name, w, g, lo, hi):
@@ -97,40 +100,36 @@ def tile_list_warhead_site_triage_kernel(
             nc.sync.dma_start(out=held[:], in_=vec.rearrange("(g p t) -> p g t", g=2, t=PACK))
             return held
 
-        def load_gain(g):
-            held = tile("gain%d" % g, [P, 1, PACK], F32)
-            nc.sync.dma_start(out=held[:, 0, :], in_=gain[KP * g : KP * (g + 1)].rearrange("(p t) -> p t", t=PACK))
-            return held
-
         l3 = load_list("l3", offs3)
-        load_plane(nc.sync, s3, tab3_scales, 0)
+        load_scales(nc.sync, s3, tab3_scales, 0)
+        load_scales(nc.gpsimd, s1, tab_scales, RES_ROW)
         l2 = load_list("l2", offs2)
-        t3 = tile("t3", [P, T3], U16)
-        nc.sync.dma_start(out=t3[:].bitcast(I32), in_=tab3_words[0].bitcast(I32))
+        t3 = load_fp4_words("t3", tab3_words[0])
         w3_raw = [load_rows("w3_raw0", w3, 0, 0, KP)]
-        load_plane(nc.sync, s2, tab2_scales, 0)
+        load_scales(nc.sync, s2, tab2_scales, 0)
         l1 = load_list("l1", offs)
         w3_raw.append(load_rows("w3_raw1", w3, 0, KP, H))
-        w2w = tile("w2w", [P, H], U16)
-        nc.sync.dma_start(out=w2w[:].bitcast(I32), in_=w2_words[0].bitcast(I32))
+        w2w = load_fp4_words("w2w", w2_words[0])
         b3t = load_channels("b3t", b3)
-        load_plane(nc.sync, sw2, w2_scales, 0)
-        t2 = load_words("t2", tab2_words[0])
-        w4_raw0 = [load_rows("w4_raw0a", w4, 0, 0, 512)]
-        load_plane(nc.sync, s1, tab_scales, RES_ROW)
-        t1 = [load_words("t1_0", tab_words[0])]
-        place["free"] = place["free"] + 4096
-        gains = [load_gain(0)]
-        w4_raw0.append(load_rows("w4_raw0b", w4, 0, 512, N))
-        load_plane(nc.sync, swr, wr_scales, RES_ROW)
-        wrw = [load_words("wrw0", wr_words[0])]
-        w4_raw1 = [load_rows("w4_raw1a", w4, 1, 0, 256), load_rows("w4_raw1b", w4, 1, 256, N)]
-        t1.append(load_words("t1_1", tab_words[1]))
-        gains.append(load_gain(1))
-        wrw.append(load_words("wrw1", wr_words[1]))
+        load_scales(nc.sync, sw2, w2_scales, 0)
+        t2 = load_fp8_words("t2", tab2_words[0])
+        w4_head = load_rows("w4_head", w4, 0, 0, 2 * PIECE)
+        gaint = load_channels("gaint", gain)
+        t1 = [load_fp8_words("t1_%d" % a, tab_words[a]) for a in range(2)]
+        load_scales(nc.sync, swr, wr_scales, RES_ROW)
+        wrw = tile("wrw", [P, 2, N], I32)
+        nc.sync.dma_start(out=wrw[:], in_=wr_words.rearrange("a p n i -> p a (n i)").bitcast(I32))
+        w4_raw = {(0, u): w4_head[:, :, PIECE * u : PIECE * (u + 1)] for u in range(2)}
+        for g, u in ((1, 0), (1, 1), (0, 2), (1, 2)):
+            w4_raw[g, u] = load_rows("w4_raw%d_%d" % (g, u), w4, g, PIECE * u, PIECE * (u + 1))[:]
         bot = tile("bot", [P, N // P], F32)
         with nc.allow_non_contiguous_dma(reason="one bias value a partition"):
             nc.sync.dma_start(out=bot[:], in_=bo.rearrange("(c p) -> p c", p=P))
+
+        def gather(name, window, lst, dtype, after=None):
+            got = tile(name, [P, S], dtype, after)
+            nc.vector.tensor_copy(got[:], window.indirect(lst[:]))
+            return got
 
         def quantise(name, src, width, after=None):
             codes = tile(name + "_c", [P, width], U32, after)
@@ -138,177 +137,166 @@ def tile_list_warhead_site_triage_kernel(
             nc.vector.quantize_mx(out=codes[:].bitcast(FP8X4), scales=scales[:], in_=src)
             return codes, scales
 
-        def w3_cast(g):
-            grouped = tile("w3_bf%d" % g, [P, PACK * KP], BF16)
-            nc.scalar.copy(
-                out=grouped[:].rearrange("p (t m j) -> p m j t", t=PACK, j=PACK),
-                in_=w3_raw[g][:].rearrange("p j (m t) -> p m j t", t=PACK),
+        def reordered(name, src, dtype):
+            held = tile(name, [P, H], dtype)
+            nc.vector.tensor_copy(
+                out=held[:].rearrange("p (g t m) -> p g t m", g=2, t=PACK),
+                in_=src[:].rearrange("p (g m t) -> p g t m", g=2, t=PACK),
             )
-            return grouped
+            return held
 
-        w3_bf = [w3_cast(0), w3_cast(1)]
+        w3_bf = [tile("w3_bf%d" % g, [P, PACK * KP], BF16) for g in range(2)]
+        for g, ms in ((0, slice(0, P)), (1, slice(0, P // 2))):
+            nc.scalar.copy(
+                out=w3_bf[g][:].rearrange("p (t m j) -> p m j t", t=PACK, j=PACK)[:, ms],
+                in_=w3_raw[g][:].rearrange("p j (m t) -> p m j t", t=PACK)[:, ms],
+            )
         v3 = gather("v3", t3[:], l3, U16)
         v3s = gather("v3s", s3[:], l3, U8)
         v2s = gather("v2s", s2[:], l2, U8)
         w3q = [quantise("w3q0", w3_bf[0][:], KP, ("s2", 0))]
-        w2p = tile("w2p", [P, H], U16)
+        w2p = reordered("w2p", w2w, U16)
         nc.vector.tensor_copy(
-            out=w2p[:].rearrange("p (g t m) -> p g t m", g=2, t=PACK),
-            in_=w2w[:].rearrange("p (g m t) -> p g t m", g=2, t=PACK),
+            out=w3_bf[1][:].rearrange("p (u e m j) -> p u m j e", u=2, e=2, j=PACK)[:, :, P // 2 :],
+            in_=w3_raw[1][:].rearrange("p j (m u e) -> p u m j e", u=2, e=2)[:, :, P // 2 :],
         )
-        w2s = tile("w2s", [P, H], U8)
-        nc.vector.tensor_copy(
-            out=w2s[:].rearrange("p (g t m) -> p g t m", g=2, t=PACK),
-            in_=sw2[:].rearrange("p (g m t) -> p g t m", g=2, t=PACK),
-        )
+        w2s = reordered("w2s", sw2, U8)
         w3q.append(quantise("w3q1", w3_bf[1][:], KP))
         v2 = gather("v2", t2[:].bitcast(U32), l2, U32)
 
-        def buf_pass(g, t, b):
+        def biased_buffer(g, t):
             cols = slice(P * t, P * (t + 1))
-            acc = bank("buf_ps", b)
+            acc = bank("buf_ps", PACK * g + t)
+            held = tile("buf%d_%d" % (g, t), [P, S], F32)
             nc.tensor.matmul_mx(
                 out=acc[:], lhsT=w3q[g][0][:, cols].bitcast(FP8X4), lhsT_scale=w3q[g][1][:, cols],
                 rhs=v3[:].bitcast(FP4X4), rhs_scale=v3s[:], start=True, stop=True,
             )
-            return acc
-
-        def site_pass(g, t, b):
-            cols = slice(KP * g + P * t, KP * g + P * (t + 1))
-            acc = bank("site_ps", b)
-            nc.tensor.matmul_mx(
-                out=acc[:], lhsT=w2p[:, cols].bitcast(FP4X4), lhsT_scale=w2s[:, cols],
-                rhs=v2[:].bitcast(FP8X4), rhs_scale=v2s[:], start=True, stop=True,
-            )
-            return acc
-
-        def biased(g, t):
-            held = tile("buf%d_%d" % (g, t), [P, S], F32)
-            nc.scalar.activation(held[:], buf_pass(g, t, PACK * g + t)[:], ACT.Identity, bias=b3t[:, g, t : t + 1])
+            nc.scalar.activation(held[:], acc[:], ACT.Identity, bias=b3t[:, g, t : t + 1])
             return held
 
-        def products(g, bufs, after=None):
-            x = tile("x%d" % g, [P, PACK, S], F32, after)
+        def products(g, bufs):
+            x = tile("x%d" % g, [P, PACK, S], F32)
             for t in range(PACK):
-                nc.vector.tensor_tensor(x[:, t, :], site_pass(g, t, PACK * g + t)[:], bufs[t][:], MULT)
+                cols = slice(KP * g + P * t, KP * g + P * (t + 1))
+                acc = bank("site_ps", PACK * g + t)
+                nc.tensor.matmul_mx(
+                    out=acc[:], lhsT=w2p[:, cols].bitcast(FP4X4), lhsT_scale=w2s[:, cols],
+                    rhs=v2[:].bitcast(FP8X4), rhs_scale=v2s[:], start=True, stop=True,
+                )
+                nc.vector.tensor_tensor(x[:, t, :], acc[:], bufs[t][:], MULT)
             return x
 
-        halves = [slice(0, S // 2), slice(S // 2, S)]
+        halves = [slice(0, HALF), slice(HALF, S)]
 
         def gelus(g, x):
-            gl = tile("gl%d" % g, [P, S, PACK], F32)
-            for half in halves:
+            gl = [tile("gl%d_%d" % (g, h), [P, HALF, PACK], F32) for h in range(2)]
+            for h in range(2):
                 nc.scalar.activation(
-                    gl[:, half, :].rearrange("p (c i) t -> p c t i", i=4),
-                    x[:, :, half].rearrange("p t (c i) -> p c t i", i=4),
+                    gl[h][:].rearrange("p (c i) t -> p c t i", i=RUN),
+                    x[:, :, halves[h]].rearrange("p t (c i) -> p c t i", i=RUN),
                     ACT.Gelu_apprx_tanh,
                 )
             return gl
 
-        def scale(hb, g, gl, engine, lo, hi):
-            factor = gains[g][:].to_broadcast([P, hi - lo, PACK])
-            engine.tensor_tensor(hb, gl[:, lo:hi, :], factor, MULT)
+        def scaled(g, h, gl, engine, after=None):
+            hb = tile("hb%d_%d" % (g, h), [P, HALF, PACK], BF16, after)
+            factor = gaint[:, g : g + 1, :].to_broadcast([P, HALF, PACK])
+            engine.tensor_tensor(hb[:], gl[h][:], factor, MULT)
+            return hb[:].rearrange("p n t -> p (n t)")
 
-        def w4_cast(grouped, lo, raw, raw_lo, copy):
-            copy(
-                out=grouped[:, PACK * lo : PACK * (lo + 256)].rearrange("p (c i j) -> p c j i", i=4, j=PACK),
-                in_=raw[:, :, raw_lo : raw_lo + 256].rearrange("p j (c i) -> p c j i", i=4),
-            )
-
+        w4_bf = {}
         w4q = {}
 
-        def w4_quantise(g, lo, hi, grouped, after=None):
-            quantised = quantise("w4q%d_%d" % (g, lo), grouped[:], hi - lo, after)
-            for c in range(lo // P, hi // P):
-                w4q[g, c] = (quantised, slice(P * c - lo, P * (c + 1) - lo))
-
-        bufs = [[biased(g, t) for t in range(PACK)] for g in range(2)]
-        x0 = products(0, bufs[0])
-        gl0 = gelus(0, x0)
-        w4_bf0 = [tile("w4_bf0a", [P, PACK * 512], BF16), tile("w4_bf0b", [P, PACK * 256], BF16)]
-        for lo in (0, 256):
-            nc.gpsimd.tensor_copy(
-                w4_bf0[0][:, PACK * lo : PACK * (lo + 256)].rearrange("p (c j) -> p c j", j=PACK),
-                w4_raw0[0][:, :, lo : lo + 256].rearrange("p j c -> p c j"),
-            )
-        v1s = gather("v1s", s1[:], l1, U8)
-        v1 = [gather("v1_0", t1[0][:].bitcast(U32), l1, U32)]
-        x1 = products(1, bufs[1], ("t1_0", 4096))
-        w4_cast(w4_bf0[1], 0, w4_raw0[1], 0, nc.scalar.copy)
-        w4_bf1 = [tile("w4_bf1_0", [P, PACK * 256], BF16)]
-        w4_cast(w4_bf1[0], 0, w4_raw1[0], 0, nc.scalar.copy)
-        gl1 = gelus(1, x1)
-        hb0 = tile("hb0", [P, S, PACK], BF16, ("t1_0", 0))
-        for lo in (0, 128):
-            scale(hb0[:, lo : lo + 128, :], 0, gl0, nc.gpsimd, lo, lo + 128)
-        scale(hb0[:, halves[1], :], 0, gl0, nc.vector, S // 2, S)
-        w4_quantise(0, 0, 512, w4_bf0[0], ("buf1_2", 0))
-        w4_quantise(0, 512, N, w4_bf0[1], ("buf1_1", 0))
-        hq = [quantise("hq0", hb0[:].rearrange("p n t -> p (n t)"), S)]
-        v1.append(gather("v1_1", t1[1][:].bitcast(U32), l1, U32))
-        for u in range(2):
-            w4_bf1.append(tile("w4_bf1_%d" % (u + 1), [P, PACK * 256], BF16, ("x1", 2048 * u)))
-            w4_cast(w4_bf1[u + 1], 0, w4_raw1[1], 256 * u, nc.scalar.copy)
-        hq.append((tile("hq1_c", [P, S], U32), tile("hq1_s", [P, S], U8)))
-
-        def second_gain(h, after):
-            hb = tile("hb1_%d" % h, [P, S // 2, PACK], BF16, after)
-            scale(hb[:], 1, gl1, nc.vector, halves[h].start, halves[h].stop)
-            return hb
-
-        def second_quantise(h, hb):
-            nc.vector.quantize_mx(
-                out=hq[1][0][:, halves[h]].bitcast(FP8X4), scales=hq[1][1][:, halves[h]],
-                in_=hb[:].rearrange("p n t -> p (n t)"),
+        def w4_round(g, u, copy, after=None):
+            w4_bf[g, u] = tile("w4_bf%d_%d" % (g, u), [P, PACK * PIECE], BF16, after)
+            copy(
+                out=w4_bf[g, u][:].rearrange("p (c i j) -> p c j i", i=RUN, j=PACK),
+                in_=w4_raw[g, u].rearrange("p j (c i) -> p c j i", i=RUN),
             )
 
-        hb1_first = second_gain(0, None)
-        w4_quantise(1, 0, 256, w4_bf1[0], ("t1_1", 0))
-        second_quantise(0, hb1_first)
-        w4_quantise(1, 256, 512, w4_bf1[1], ("t1_1", 1024))
-        hb1_second = second_gain(1, None)
-        w4_quantise(1, 512, N, w4_bf1[2], ("t1_1", 2048))
-        second_quantise(1, hb1_second)
+        def w4_quantise(g, u, after=None):
+            w4q[g, u] = quantise("w4q%d_%d" % (g, u), w4_bf[g, u][:], PIECE, after)
 
-        accs = [[bank("acc%d_%d" % (h, b), 3 * h + b) for b in range(3)] for h in range(2)]
+        bufs = [[biased_buffer(g, t) for t in range(PACK)] for g in range(2)]
+        gl0 = gelus(0, products(0, bufs[0]))
+        w4_bf[0, 0] = tile("w4_bf0_0", [P, PACK * PIECE], BF16, ("t2", 0))
+        nc.gpsimd.tensor_copy(
+            w4_bf[0, 0][:].rearrange("p (c j) -> p c j", j=PACK), w4_raw[0, 0].rearrange("p j c -> p c j")
+        )
+        gl1 = gelus(1, products(1, bufs[1]))
+        w4_round(0, 1, nc.scalar.copy, ("x1", 0))
+        w4_round(1, 0, nc.scalar.copy)
+        w4_round(1, 1, nc.scalar.copy)
+        w4_round(0, 2, nc.scalar.copy, ("x1", 2 * PACK * PIECE))
+
+        v1s = gather("v1s", s1[:], l1, U8, ("buf1_1", 0))
+        v1 = [gather("v1_%d" % a, t1[a][:].bitcast(U32), l1, U32, ("buf1_%d" % (2 + a), 0)) for a in range(2)]
+        hb0 = [scaled(0, h, gl0, nc.gpsimd) for h in range(2)]
+        w4_quantise(0, 0, ("t1_1", 0))
+        hq = {(0, h): quantise("hq0_%d" % h, hb0[h], HALF, ("t1_1", 4 * (PIECE + HALF * h))) for h in range(2)}
+        hb1 = scaled(1, 0, gl1, nc.vector, ("hb0_0", 0))
+        w4_quantise(0, 1, ("hb0_1", 0))
+        hq[1, 0] = quantise("hq1_0", hb1, HALF)
+        w4_quantise(1, 0, ("w4_bf0_1", 0))
+        hb1_last = scaled(1, 1, gl1, nc.vector, ("w4_raw1_0", 0))
+        w4_quantise(1, 1, ("w4_bf1_0", 0))
+        hq[1, 1] = quantise("hq1_1", hb1_last, HALF, ("w4_raw1_1", 0))
+        w4_quantise(0, 2, ("w4_bf1_1", 0))
+        w4_round(1, 2, nc.vector.tensor_copy, ("hb1_1", 0))
+        w4_quantise(1, 2)
+
+        accs = {(h, u): bank("acc%d_%d" % (h, u), 3 * h + u) for h in range(2) for u in range(3)}
 
         def sums(h, c):
-            return accs[h][c // 2][:, (c % 2) * (S // 2) : (c % 2 + 1) * (S // 2)]
+            return accs[h, c // 2][:, halves[c % 2]]
 
         def wr_pass(a, h, c):
             cols = slice(P * c, P * (c + 1))
             rows = slice(RES_ROW + 4 * a, P)
             nc.tensor.matmul_mx(
-                out=sums(h, c), lhsT=wrw[a][:, cols].bitcast(FP8X4), lhsT_scale=swr[rows, cols],
+                out=sums(h, c), lhsT=wrw[:, a, cols].bitcast(FP8X4), lhsT_scale=swr[rows, cols],
                 rhs=v1[a][:, halves[h]].bitcast(FP8X4), rhs_scale=v1s[rows, halves[h]],
                 start=(a == 0 and c % 2 == 0), stop=False,
             )
 
         def w4_pass(g, h, c):
-            (codes, scales), part = w4q[g, c]
+            codes, scales = w4q[g, c // 2]
+            cols = slice(P * (c % 2), P * (c % 2 + 1))
             nc.tensor.matmul_mx(
-                out=sums(h, c), lhsT=codes[:, part].bitcast(FP8X4), lhsT_scale=scales[:, part],
-                rhs=hq[g][0][:, halves[h]].bitcast(FP8X4), rhs_scale=hq[g][1][:, halves[h]],
+                out=sums(h, c), lhsT=codes[:, cols].bitcast(FP8X4), lhsT_scale=scales[:, cols],
+                rhs=hq[g, h][0][:].bitcast(FP8X4), rhs_scale=hq[g, h][1][:],
                 start=False, stop=(g == 1 and c % 2 == 1),
             )
 
-        for c in range(N // P):
-            for h in range(2):
-                wr_pass(0, h, c)
-        for c in range(N // P):
-            for h in range(2):
-                w4_pass(0, h, c)
-        for h in range(2):
-            for c in range(N // P):
-                wr_pass(1, h, c)
-        for h, b in ((0, 0), (0, 1), (0, 2), (1, 0), (1, 1), (1, 2)):
-            res = tile("res%d_%d" % (h, b), [P, 2, S // 2], F32)
-            for c in (2 * b, 2 * b + 1):
+        def first_w4_passes(chunks):
+            for c in chunks:
+                for h in range(2):
+                    w4_pass(0, h, c)
+
+        def finish(h, u, on_scalar, after=None):
+            res = tile("res%d_%d" % (h, u), [P, 2, HALF], F32, after)
+            chunks = (2 * u, 2 * u + 1)
+            for c in chunks:
                 w4_pass(1, h, c)
-            for c in (2 * b, 2 * b + 1):
-                if (h, b) in ((1, 0), (1, 2)):
-                    nc.vector.tensor_scalar(res[:, c % 2, :], sums(h, c), bot[:, c : c + 1], None, ADD)
-                else:
+            if on_scalar:
+                for c in chunks:
                     nc.scalar.activation(res[:, c % 2, :], sums(h, c), ACT.Identity, bias=bot[:, c : c + 1])
-            rows = out[2 * P * b : 2 * P * (b + 1), halves[h]]
+            else:
+                bias = bot[:, 2 * u : 2 * u + 2].unsqueeze(2).to_broadcast([P, 2, HALF])
+                nc.vector.tensor_tensor(res[:], accs[h, u][:].rearrange("p (c s) -> p c s", c=2), bias, ADD)
+            rows = out[PIECE * u : PIECE * (u + 1), halves[h]]
             nc.sync.dma_start(out=rows.rearrange("(c p) s -> p c s", p=P), in_=res[:])
+
+        for a in range(2):
+            for c in range(N // P):
+                for h in range(2):
+                    wr_pass(a, h, c)
+        first_w4_passes(range(4))
+        finish(0, 0, True)
+        finish(0, 1, True)
+        finish(1, 0, True)
+        finish(1, 1, False, ("w4_bf1_2", 0))
+        first_w4_passes((4, 5))
+        finish(0, 2, True)
+        finish(1, 2, False)

@@ -2,6 +2,7 @@ import math
 from contextlib import ExitStack
 
 import concourse.mybir as mybir
+from concourse.masks import make_identity
 
 K, K2, H, N, T, T2, T3, S = 1024, 512, 1024, 768, 2048, 2048, 1024, 512
 FLOPS = 2 * S * (2 * K2 * H + H * N + K * N)
@@ -69,11 +70,12 @@ def tile_list_warhead_site_triage_kernel(
         swr = scale_tile("swr", N, nc.vector)
 
         def load_scales(queue, held, scales, first):
-            passes = scales.shape[0]
             for q in range(4):
-                src = scales[0, 4 * q : 4 * q + 4, :] if passes == 1 else scales[:, 4 * q : 4 * q + 4, :]
-                rows = slice(32 * q + first, 32 * q + first + 4 * passes)
-                queue.dma_start(out=held[rows, :].bitcast(I32), in_=src.bitcast(I32))
+                if scales.shape[0] == 1:
+                    queue.dma_start(out=held[q:P:32, :].bitcast(I32), in_=scales[0, q:16:4, :].bitcast(I32))
+                else:
+                    rows = slice(32 * q + first, 32 * q + first + 8)
+                    queue.dma_start(out=held[rows, :].bitcast(I32), in_=scales[:, 4 * q : 4 * q + 4, :].bitcast(I32))
 
         def load_list(name, src):
             lst = lists.tile([P, S // 16], U16, name=name)
@@ -115,6 +117,11 @@ def tile_list_warhead_site_triage_kernel(
         t2 = load_fp8_words("t2", tab2_words[0])
         w4_head = load_rows("w4_head", w4, 0, 0, 2 * PIECE)
         gaint = load_channels("gaint", gain)
+        bo_rows = tile("bo_rows", [P, N // 2], F32)
+        nc.gpsimd.memset(bo_rows[:], 0.0)
+        nc.sync.dma_start(out=bo_rows[0:2, :], in_=bo.rearrange("(r n) -> r n", r=2))
+        ident = tile("ident", [P, P], F32)
+        make_identity(nc, ident[:])
         t1 = [load_fp8_words("t1_%d" % a, tab_words[a]) for a in range(2)]
         load_scales(nc.sync, swr, wr_scales, RES_ROW)
         wrw = tile("wrw", [P, 2, N], I32)
@@ -122,9 +129,6 @@ def tile_list_warhead_site_triage_kernel(
         w4_raw = {(0, u): w4_head[:, :, PIECE * u : PIECE * (u + 1)] for u in range(2)}
         for g, u in ((1, 0), (1, 1), (0, 2), (1, 2)):
             w4_raw[g, u] = load_rows("w4_raw%d_%d" % (g, u), w4, g, PIECE * u, PIECE * (u + 1))[:]
-        bot = tile("bot", [P, N // P], F32)
-        with nc.allow_non_contiguous_dma(reason="one bias value a partition"):
-            nc.sync.dma_start(out=bot[:], in_=bo.rearrange("(c p) -> p c", p=P))
 
         def gather(name, window, lst, dtype, after=None):
             got = tile(name, [P, S], dtype, after)
@@ -225,6 +229,14 @@ def tile_list_warhead_site_triage_kernel(
             w4_bf[0, 0][:].rearrange("p (c j) -> p c j", j=PACK), w4_raw[0, 0].rearrange("p j c -> p c j")
         )
         gl1 = gelus(1, products(1, bufs[1]))
+        bo_ps = bank("bo_ps", 7)
+        for k in range(3):
+            nc.tensor.transpose(bo_ps[:, P * k : P * (k + 1)], bo_rows[:, P * k : P * (k + 1)], ident[:])
+        bot = tile("bot", [P, N // P], F32)
+        nc.scalar.copy(
+            out=bot[:].rearrange("p (r k) -> p r k", r=2),
+            in_=bo_ps[:, 0 : 3 * P].rearrange("p (k r) -> p r k", k=3)[:, 0:2],
+        )
         w4_round(0, 1, nc.scalar.copy, ("x1", 0))
         w4_round(1, 0, nc.scalar.copy)
         w4_round(1, 1, nc.scalar.copy)

@@ -63,11 +63,16 @@ def tile_list_warhead_site_triage_kernel(
             engine.memset(held[:].bitcast(I32), 0)
             return held
 
-        s3 = scale_tile("s3", T3, nc.gpsimd)
+        s3 = scale_tile("s3", T3, nc.vector)
         s1 = scale_tile("s1", T, nc.gpsimd)
         s2 = scale_tile("s2", T2, nc.vector)
-        sw2 = scale_tile("sw2", H, nc.vector)
         swr = scale_tile("swr", N, nc.vector)
+        sw2 = scale_tile("sw2", H, nc.vector)
+        place["free"] = place["free"] + H
+        bo_rows = tile("bo_rows", [P, N // 2], F32)
+        nc.vector.memset(bo_rows[:], 0.0)
+        ident = tile("ident", [P, P], F32)
+        make_identity(nc, ident[:])
 
         def load_scales(queue, held, scales, first):
             for q in range(4):
@@ -92,54 +97,58 @@ def tile_list_warhead_site_triage_kernel(
             nc.sync.dma_start(out=held[:].bitcast(I32), in_=words.bitcast(I32))
             return held
 
-        def load_rows(name, w, g, lo, hi):
-            raw = tile(name, [P, PACK, hi - lo], F32)
+        def load_rows(raw, w, g, lo, hi):
             nc.sync.dma_start(out=raw[:], in_=w[KP * g : KP * (g + 1), lo:hi].rearrange("(p j) n -> p j n", j=PACK))
-            return raw
 
         def load_channels(name, vec):
             held = tile(name, [P, 2, PACK], F32)
             nc.sync.dma_start(out=held[:], in_=vec.rearrange("(g p t) -> p g t", g=2, t=PACK))
             return held
 
+        w3_raw = [tile("w3_raw%d" % g, [P, PACK, KP], F32) for g in range(2)]
+        w4_raw = {}
+        for g, u in ((0, 0), (1, 0), (0, 1), (0, 2), (1, 1), (1, 2)):
+            w4_raw[g, u] = tile("w4_raw%d_%d" % (g, u), [P, PACK, PIECE], F32)
+
+        def load_w4(g, u):
+            load_rows(w4_raw[g, u], w4, g, PIECE * u, PIECE * (u + 1))
+
         l3 = load_list("l3", offs3)
+        t3 = load_fp4_words("t3", tab3_words[0])
         load_scales(nc.sync, s3, tab3_scales, 0)
         load_scales(nc.gpsimd, s1, tab_scales, RES_ROW)
         l2 = load_list("l2", offs2)
-        t3 = load_fp4_words("t3", tab3_words[0])
-        w3_raw = [load_rows("w3_raw0", w3, 0, 0, KP)]
+        load_rows(w3_raw[0], w3, 0, 0, KP)
         load_scales(nc.sync, s2, tab2_scales, 0)
-        l1 = load_list("l1", offs)
-        w3_raw.append(load_rows("w3_raw1", w3, 0, KP, H))
-        w2w = load_fp4_words("w2w", w2_words[0])
         b3t = load_channels("b3t", b3)
+        w2w = load_fp4_words("w2w", w2_words[0])
+        load_rows(w3_raw[1], w3, 0, KP, H)
         load_scales(nc.sync, sw2, w2_scales, 0)
+        l1 = load_list("l1", offs)
         t2 = load_fp8_words("t2", tab2_words[0])
-        w4_head = load_rows("w4_head", w4, 0, 0, 2 * PIECE)
         gaint = load_channels("gaint", gain)
-        bo_rows = tile("bo_rows", [P, N // 2], F32)
-        nc.gpsimd.memset(bo_rows[:], 0.0)
-        nc.sync.dma_start(out=bo_rows[0:2, :], in_=bo.rearrange("(r n) -> r n", r=2))
-        ident = tile("ident", [P, P], F32)
-        make_identity(nc, ident[:])
+        load_w4(0, 0)
+        load_w4(1, 0)
         t1 = [load_fp8_words("t1_%d" % a, tab_words[a]) for a in range(2)]
+        nc.sync.dma_start(out=bo_rows[0:2, :], in_=bo.rearrange("(r n) -> r n", r=2))
         load_scales(nc.sync, swr, wr_scales, RES_ROW)
         wrw = tile("wrw", [P, 2, N], I32)
         nc.sync.dma_start(out=wrw[:], in_=wr_words.rearrange("a p n i -> p a (n i)").bitcast(I32))
-        w4_raw = {(0, u): w4_head[:, :, PIECE * u : PIECE * (u + 1)] for u in range(2)}
-        for g, u in ((1, 0), (1, 1), (0, 2), (1, 2)):
-            w4_raw[g, u] = load_rows("w4_raw%d_%d" % (g, u), w4, g, PIECE * u, PIECE * (u + 1))[:]
+        for g, u in ((0, 1), (1, 1), (0, 2), (1, 2)):
+            load_w4(g, u)
+
+        halves = [slice(0, HALF), slice(HALF, S)]
 
         def gather(name, window, lst, dtype, after=None):
             got = tile(name, [P, S], dtype, after)
             nc.vector.tensor_copy(got[:], window.indirect(lst[:]))
             return got
 
-        def quantise(name, src, width, after=None):
-            codes = tile(name + "_c", [P, width], U32, after)
-            scales = tile(name + "_s", [P, width], U8)
-            nc.vector.quantize_mx(out=codes[:].bitcast(FP8X4), scales=scales[:], in_=src)
-            return codes, scales
+        def quantised(name, width, after=None):
+            return tile(name + "_c", [P, width], U32, after), tile(name + "_s", [P, width], U8)
+
+        def quantise(pair, cols, src):
+            nc.vector.quantize_mx(out=pair[0][:, cols].bitcast(FP8X4), scales=pair[1][:, cols], in_=src)
 
         def reordered(name, src, dtype):
             held = tile(name, [P, H], dtype)
@@ -150,63 +159,100 @@ def tile_list_warhead_site_triage_kernel(
             return held
 
         w3_bf = [tile("w3_bf%d" % g, [P, PACK * KP], BF16) for g in range(2)]
-        for g, ms in ((0, slice(0, P)), (1, slice(0, P // 2))):
+
+        def w3_round_on_scalar(g, ms):
             nc.scalar.copy(
                 out=w3_bf[g][:].rearrange("p (t m j) -> p m j t", t=PACK, j=PACK)[:, ms],
                 in_=w3_raw[g][:].rearrange("p j (m t) -> p m j t", t=PACK)[:, ms],
             )
-        v3 = gather("v3", t3[:], l3, U16)
-        v3s = gather("v3s", s3[:], l3, U8)
-        v2s = gather("v2s", s2[:], l2, U8)
-        w3q = [quantise("w3q0", w3_bf[0][:], KP, ("s2", 0))]
-        w2p = reordered("w2p", w2w, U16)
-        nc.vector.tensor_copy(
-            out=w3_bf[1][:].rearrange("p (u e m j) -> p u m j e", u=2, e=2, j=PACK)[:, :, P // 2 :],
-            in_=w3_raw[1][:].rearrange("p j (m u e) -> p u m j e", u=2, e=2)[:, :, P // 2 :],
-        )
-        w2s = reordered("w2s", sw2, U8)
-        w3q.append(quantise("w3q1", w3_bf[1][:], KP))
-        v2 = gather("v2", t2[:].bitcast(U32), l2, U32)
 
-        def biased_buffer(g, t):
-            cols = slice(P * t, P * (t + 1))
-            acc = bank("buf_ps", PACK * g + t)
-            held = tile("buf%d_%d" % (g, t), [P, S], F32)
-            nc.tensor.matmul_mx(
-                out=acc[:], lhsT=w3q[g][0][:, cols].bitcast(FP8X4), lhsT_scale=w3q[g][1][:, cols],
-                rhs=v3[:].bitcast(FP4X4), rhs_scale=v3s[:], start=True, stop=True,
+        def w3_round_on_vector(g, ms):
+            nc.vector.tensor_copy(
+                out=w3_bf[g][:].rearrange("p (u e m j) -> p u m j e", u=2, e=2, j=PACK)[:, :, ms],
+                in_=w3_raw[g][:].rearrange("p j (m u e) -> p u m j e", u=2, e=2)[:, :, ms],
             )
-            nc.scalar.activation(held[:], acc[:], ACT.Identity, bias=b3t[:, g, t : t + 1])
+
+        def biased_buffer(g, pair, banks, after=None):
+            held = tile("buf%d_%d" % (g, pair), [P, 2, S], F32, after)
+            for e in range(2):
+                t = 2 * pair + e
+                cols = slice(P * t, P * (t + 1))
+                acc = bank("buf_ps", banks[e])
+                nc.tensor.matmul_mx(
+                    out=acc[:], lhsT=w3q[g][0][:, cols].bitcast(FP8X4), lhsT_scale=w3q[g][1][:, cols],
+                    rhs=v3[:].bitcast(FP4X4), rhs_scale=v3s[:], start=True, stop=True,
+                )
+                nc.scalar.activation(held[:, e, :], acc[:], ACT.Identity, bias=b3t[:, g, t : t + 1])
             return held
 
-        def products(g, bufs):
-            x = tile("x%d" % g, [P, PACK, S], F32)
-            for t in range(PACK):
-                cols = slice(KP * g + P * t, KP * g + P * (t + 1))
-                acc = bank("site_ps", PACK * g + t)
+        v3 = gather("v3", t3[:], l3, U16)
+        v3s = gather("v3s", s3[:], l3, U8)
+        w3_round_on_scalar(0, slice(0, P))
+        v2s = gather("v2s", s2[:], l2, U8)
+        w2p = reordered("w2p", w2w, U16)
+        w3q = [quantised("w3q0", KP, ("w2w", 0))]
+        quantise(w3q[0], slice(0, KP), w3_bf[0][:])
+        w3_round_on_scalar(1, slice(0, P // 2))
+        w3_round_on_vector(1, slice(P // 2, P))
+        bufs = {(0, pair): biased_buffer(0, pair, (2 * pair, 2 * pair + 1), ("w3_raw1", 8 * S * pair)) for pair in range(2)}
+        w2s = reordered("w2s", sw2, U8)
+        w3q.append(quantised("w3q1", KP, ("sw2", 0)))
+        quantise(w3q[1], slice(0, KP), w3_bf[1][:])
+        bufs[1, 0] = biased_buffer(1, 0, (4, 5))
+        v2 = [tile("v2_%d" % h, [P, HALF], U32) for h in range(2)]
+        for h in range(2):
+            nc.vector.tensor_copy(v2[h][:], t2[:].bitcast(U32).indirect(l2[:, 16 * h : 16 * (h + 1)]))
+
+        x = {(g, h): tile("x%d_%d" % (g, h), [P, PACK, HALF], F32) for g in range(2) for h in range(2)}
+        gl = {}
+
+        def product(g, h, pair):
+            acc = bank("site_ps", PACK * g + 2 * pair + h)
+            for e in range(2):
+                lo = KP * g + P * (2 * pair + e)
                 nc.tensor.matmul_mx(
-                    out=acc[:], lhsT=w2p[:, cols].bitcast(FP4X4), lhsT_scale=w2s[:, cols],
-                    rhs=v2[:].bitcast(FP8X4), rhs_scale=v2s[:], start=True, stop=True,
+                    out=acc[:, halves[e]], lhsT=w2p[:, lo : lo + P].bitcast(FP4X4), lhsT_scale=w2s[:, lo : lo + P],
+                    rhs=v2[h][:].bitcast(FP8X4), rhs_scale=v2s[:, halves[h]], start=True, stop=True,
                 )
-                nc.vector.tensor_tensor(x[:, t, :], acc[:], bufs[t][:], MULT)
-            return x
+            nc.vector.tensor_tensor(
+                x[g, h][:, 2 * pair : 2 * pair + 2, :], acc[:].rearrange("p (e s) -> p e s", e=2),
+                bufs[g, pair][:, :, halves[h]], MULT,
+            )
 
-        halves = [slice(0, HALF), slice(HALF, S)]
+        def gelu(g, h):
+            gl[g, h] = tile("gl%d_%d" % (g, h), [P, HALF, PACK], F32)
+            nc.scalar.activation(
+                gl[g, h][:].rearrange("p (c i) t -> p c t i", i=RUN),
+                x[g, h][:].rearrange("p t (c i) -> p c t i", i=RUN),
+                ACT.Gelu_apprx_tanh,
+            )
 
-        def gelus(g, x):
-            gl = [tile("gl%d_%d" % (g, h), [P, HALF, PACK], F32) for h in range(2)]
-            for h in range(2):
-                nc.scalar.activation(
-                    gl[h][:].rearrange("p (c i) t -> p c t i", i=RUN),
-                    x[:, :, halves[h]].rearrange("p t (c i) -> p c t i", i=RUN),
-                    ACT.Gelu_apprx_tanh,
-                )
-            return gl
+        for h in range(2):
+            for pair in range(2):
+                product(0, h, pair)
+        gelu(0, 0)
+        bufs[1, 1] = biased_buffer(1, 1, (1, 3))
+        gelu(0, 1)
+        for h in range(2):
+            product(1, h, 0)
+        v1s = gather("v1s", s1[:], l1, U8, ("buf0_1", 0))
+        for h in range(2):
+            product(1, h, 1)
+            gelu(1, h)
 
-        def scaled(g, h, gl, engine, after=None):
+        bo_ps = bank("bo_ps", 7)
+        for k in range(3):
+            nc.tensor.transpose(bo_ps[:, P * k : P * (k + 1)], bo_rows[:, P * k : P * (k + 1)], ident[:])
+        bot = tile("bot", [P, N // P], F32)
+        nc.scalar.copy(
+            out=bot[:].rearrange("p (r k) -> p r k", r=2),
+            in_=bo_ps[:, 0 : 3 * P].rearrange("p (k r) -> p r k", k=3)[:, 0:2],
+        )
+
+        def scaled(g, h, engine, after=None):
             hb = tile("hb%d_%d" % (g, h), [P, HALF, PACK], BF16, after)
             factor = gaint[:, g : g + 1, :].to_broadcast([P, HALF, PACK])
-            engine.tensor_tensor(hb[:], gl[h][:], factor, MULT)
+            engine.tensor_tensor(hb[:], gl[g, h][:], factor, MULT)
             return hb[:].rearrange("p n t -> p (n t)")
 
         w4_bf = {}
@@ -216,99 +262,76 @@ def tile_list_warhead_site_triage_kernel(
             w4_bf[g, u] = tile("w4_bf%d_%d" % (g, u), [P, PACK * PIECE], BF16, after)
             copy(
                 out=w4_bf[g, u][:].rearrange("p (c i j) -> p c j i", i=RUN, j=PACK),
-                in_=w4_raw[g, u].rearrange("p j (c i) -> p c j i", i=RUN),
+                in_=w4_raw[g, u][:].rearrange("p j (c i) -> p c j i", i=RUN),
             )
 
         def w4_quantise(g, u, after=None):
-            w4q[g, u] = quantise("w4q%d_%d" % (g, u), w4_bf[g, u][:], PIECE, after)
+            w4q[g, u] = quantised("w4q%d_%d" % (g, u), PIECE, after)
+            quantise(w4q[g, u], slice(0, PIECE), w4_bf[g, u][:])
 
-        bufs = [[biased_buffer(g, t) for t in range(PACK)] for g in range(2)]
-        gl0 = gelus(0, products(0, bufs[0]))
-        w4_bf[0, 0] = tile("w4_bf0_0", [P, PACK * PIECE], BF16, ("t2", 0))
-        nc.gpsimd.tensor_copy(
-            w4_bf[0, 0][:].rearrange("p (c j) -> p c j", j=PACK), w4_raw[0, 0].rearrange("p j c -> p c j")
-        )
-        gl1 = gelus(1, products(1, bufs[1]))
-        bo_ps = bank("bo_ps", 7)
-        for k in range(3):
-            nc.tensor.transpose(bo_ps[:, P * k : P * (k + 1)], bo_rows[:, P * k : P * (k + 1)], ident[:])
-        bot = tile("bot", [P, N // P], F32)
-        nc.scalar.copy(
-            out=bot[:].rearrange("p (r k) -> p r k", r=2),
-            in_=bo_ps[:, 0 : 3 * P].rearrange("p (k r) -> p r k", k=3)[:, 0:2],
-        )
-        w4_round(0, 1, nc.scalar.copy, ("x1", 0))
-        w4_round(1, 0, nc.scalar.copy)
-        w4_round(1, 1, nc.scalar.copy)
-        w4_round(0, 2, nc.scalar.copy, ("x1", 2 * PACK * PIECE))
+        for g in range(2):
+            w4_bf[g, 0] = tile("w4_bf%d_0" % g, [P, PACK * PIECE], BF16, ("t2", 2 * PACK * PIECE * g))
+            nc.gpsimd.tensor_scalar(
+                w4_bf[g, 0][:].rearrange("p (c j) -> p c j", j=PACK), w4_raw[g, 0][:].rearrange("p j c -> p c j"),
+                1.0, 0.0, MULT, ADD,
+            )
+        w4_round(0, 1, nc.scalar.copy, ("x1_1", 0))
+        for g, u in ((1, 1), (0, 2)):
+            w4_round(g, u, nc.scalar.copy)
 
-        v1s = gather("v1s", s1[:], l1, U8, ("buf1_1", 0))
-        v1 = [gather("v1_%d" % a, t1[a][:].bitcast(U32), l1, U32, ("buf1_%d" % (2 + a), 0)) for a in range(2)]
-        hb0 = [scaled(0, h, gl0, nc.gpsimd) for h in range(2)]
-        w4_quantise(0, 0, ("t1_1", 0))
-        hq = {(0, h): quantise("hq0_%d" % h, hb0[h], HALF, ("t1_1", 4 * (PIECE + HALF * h))) for h in range(2)}
-        hb1 = scaled(1, 0, gl1, nc.vector, ("hb0_0", 0))
-        w4_quantise(0, 1, ("hb0_1", 0))
-        hq[1, 0] = quantise("hq1_0", hb1, HALF)
-        w4_quantise(1, 0, ("w4_bf0_1", 0))
-        hb1_last = scaled(1, 1, gl1, nc.vector, ("w4_raw1_0", 0))
-        w4_quantise(1, 1, ("w4_bf1_0", 0))
-        hq[1, 1] = quantise("hq1_1", hb1_last, HALF, ("w4_raw1_1", 0))
-        w4_quantise(0, 2, ("w4_bf1_1", 0))
-        w4_round(1, 2, nc.vector.tensor_copy, ("hb1_1", 0))
-        w4_quantise(1, 2)
+        v1 = [gather("v1_%d" % a, t1[a][:].bitcast(U32), l1, U32, ("buf1_%d" % a, 0)) for a in range(2)]
+        hb0 = [scaled(0, h, nc.gpsimd) for h in range(2)]
+        hq = [quantised("hq0", S, ("t1_1", 0)), quantised("hq1", S)]
+        for h in range(2):
+            quantise(hq[0], halves[h], hb0[h])
+        hb1 = [scaled(1, 0, nc.vector, ("t1_1", 4 * S))]
+        w4_quantise(0, 0, ("t1_1", 12 * S))
+        hb1.append(scaled(1, 1, nc.vector, ("t1_1", 8 * S)))
+        quantise(hq[1], halves[0], hb1[0])
+        w4_quantise(1, 0, ("t1_1", 14 * S))
+        quantise(hq[1], halves[1], hb1[1])
+        w4_quantise(0, 1)
+        w4_quantise(1, 1)
 
-        accs = {(h, u): bank("acc%d_%d" % (h, u), 3 * h + u) for h in range(2) for u in range(3)}
+        accs = [bank("acc%d" % c, c) for c in range(N // P)]
 
-        def sums(h, c):
-            return accs[h, c // 2][:, halves[c % 2]]
-
-        def wr_pass(a, h, c):
+        def wr_pass(a, c):
             cols = slice(P * c, P * (c + 1))
             rows = slice(RES_ROW + 4 * a, P)
             nc.tensor.matmul_mx(
-                out=sums(h, c), lhsT=wrw[:, a, cols].bitcast(FP8X4), lhsT_scale=swr[rows, cols],
-                rhs=v1[a][:, halves[h]].bitcast(FP8X4), rhs_scale=v1s[rows, halves[h]],
-                start=(a == 0 and c % 2 == 0), stop=False,
+                out=accs[c][:], lhsT=wrw[:, a, cols].bitcast(FP8X4), lhsT_scale=swr[rows, cols],
+                rhs=v1[a][:].bitcast(FP8X4), rhs_scale=v1s[rows, :], start=(a == 0), stop=False,
             )
 
-        def w4_pass(g, h, c):
+        def w4_pass(g, c):
             codes, scales = w4q[g, c // 2]
             cols = slice(P * (c % 2), P * (c % 2 + 1))
             nc.tensor.matmul_mx(
-                out=sums(h, c), lhsT=codes[:, cols].bitcast(FP8X4), lhsT_scale=scales[:, cols],
-                rhs=hq[g, h][0][:].bitcast(FP8X4), rhs_scale=hq[g, h][1][:],
-                start=False, stop=(g == 1 and c % 2 == 1),
+                out=accs[c][:], lhsT=codes[:, cols].bitcast(FP8X4), lhsT_scale=scales[:, cols],
+                rhs=hq[g][0][:].bitcast(FP8X4), rhs_scale=hq[g][1][:], start=False, stop=(g == 1),
             )
 
-        def first_w4_passes(chunks):
-            for c in chunks:
-                for h in range(2):
-                    w4_pass(0, h, c)
-
-        def finish(h, u, on_scalar, after=None):
-            res = tile("res%d_%d" % (h, u), [P, 2, HALF], F32, after)
-            chunks = (2 * u, 2 * u + 1)
-            for c in chunks:
-                w4_pass(1, h, c)
+        def finish(c, on_scalar, after=None):
+            res = tile("res%d" % c, [P, S], F32, after)
             if on_scalar:
-                for c in chunks:
-                    nc.scalar.activation(res[:, c % 2, :], sums(h, c), ACT.Identity, bias=bot[:, c : c + 1])
+                nc.scalar.activation(res[:], accs[c][:], ACT.Identity, bias=bot[:, c : c + 1])
             else:
-                bias = bot[:, 2 * u : 2 * u + 2].unsqueeze(2).to_broadcast([P, 2, HALF])
-                nc.vector.tensor_tensor(res[:], accs[h, u][:].rearrange("p (c s) -> p c s", c=2), bias, ADD)
-            rows = out[PIECE * u : PIECE * (u + 1), halves[h]]
-            nc.sync.dma_start(out=rows.rearrange("(c p) s -> p c s", p=P), in_=res[:])
+                nc.vector.tensor_scalar(res[:], accs[c][:], bot[:, c : c + 1], None, ADD)
+            nc.sync.dma_start(out=out[P * c : P * (c + 1), :], in_=res[:])
 
         for a in range(2):
             for c in range(N // P):
-                for h in range(2):
-                    wr_pass(a, h, c)
-        first_w4_passes(range(4))
-        finish(0, 0, True)
-        finish(0, 1, True)
-        finish(1, 0, True)
-        finish(1, 1, False, ("w4_bf1_2", 0))
-        first_w4_passes((4, 5))
-        finish(0, 2, True)
-        finish(1, 2, False)
+                wr_pass(a, c)
+        for g, c in ((0, 0), (0, 1), (1, 0), (1, 1), (0, 2), (0, 3), (1, 2), (1, 3)):
+            w4_pass(g, c)
+        finish(0, True, ("w4_raw0_2", -1024))
+        finish(1, True, ("w4_raw0_2", 1024))
+        finish(2, True, ("w4_raw0_2", 3072))
+        finish(3, True)
+        w4_quantise(0, 2)
+        w4_round(1, 2, nc.vector.tensor_copy)
+        w4_quantise(1, 2)
+        for g, c in ((0, 4), (0, 5), (1, 4), (1, 5)):
+            w4_pass(g, c)
+        finish(4, True)
+        finish(5, False)

@@ -64,15 +64,12 @@ def tile_list_warhead_site_triage_kernel(
             return held
 
         s3 = scale_tile("s3", T3, nc.vector)
-        s1 = scale_tile("s1", T, nc.gpsimd)
+        sw2 = scale_tile("sw2", H, nc.gpsimd)
         s2 = scale_tile("s2", T2, nc.vector)
+        s1 = scale_tile("s1", T, nc.vector)
         swr = scale_tile("swr", N, nc.vector)
-        sw2 = scale_tile("sw2", H, nc.vector)
-        place["free"] = place["free"] + H
         bo_rows = tile("bo_rows", [P, N // 2], F32)
         nc.vector.memset(bo_rows[:], 0.0)
-        ident = tile("ident", [P, P], F32)
-        make_identity(nc, ident[:])
 
         def load_scales(queue, held, scales, first):
             for q in range(4):
@@ -116,14 +113,16 @@ def tile_list_warhead_site_triage_kernel(
         l3 = load_list("l3", offs3)
         t3 = load_fp4_words("t3", tab3_words[0])
         load_scales(nc.sync, s3, tab3_scales, 0)
+        load_scales(nc.gpsimd, sw2, w2_scales, 0)
         load_scales(nc.gpsimd, s1, tab_scales, RES_ROW)
+        ident = tile("ident", [P, P], F32)
+        make_identity(nc, ident[:])
         l2 = load_list("l2", offs2)
         load_rows(w3_raw[0], w3, 0, 0, KP)
         load_scales(nc.sync, s2, tab2_scales, 0)
         b3t = load_channels("b3t", b3)
         w2w = load_fp4_words("w2w", w2_words[0])
         load_rows(w3_raw[1], w3, 0, KP, H)
-        load_scales(nc.sync, sw2, w2_scales, 0)
         l1 = load_list("l1", offs)
         t2 = load_fp8_words("t2", tab2_words[0])
         gaint = load_channels("gaint", gain)
@@ -150,8 +149,8 @@ def tile_list_warhead_site_triage_kernel(
         def quantise(pair, cols, src):
             nc.vector.quantize_mx(out=pair[0][:, cols].bitcast(FP8X4), scales=pair[1][:, cols], in_=src)
 
-        def reordered(name, src, dtype):
-            held = tile(name, [P, H], dtype)
+        def reordered(name, src, dtype, after=None):
+            held = tile(name, [P, H], dtype, after)
             nc.vector.tensor_copy(
                 out=held[:].rearrange("p (g t m) -> p g t m", g=2, t=PACK),
                 in_=src[:].rearrange("p (g m t) -> p g t m", g=2, t=PACK),
@@ -192,11 +191,11 @@ def tile_list_warhead_site_triage_kernel(
         w2p = reordered("w2p", w2w, U16)
         w3q = [quantised("w3q0", KP, ("w2w", 0))]
         quantise(w3q[0], slice(0, KP), w3_bf[0][:])
+        w2s = reordered("w2s", sw2, U8, ("w3_bf0", 0))
         w3_round_on_scalar(1, slice(0, P // 2))
         w3_round_on_vector(1, slice(P // 2, P))
         bufs = {(0, pair): biased_buffer(0, pair, (2 * pair, 2 * pair + 1), ("w3_raw1", 8 * S * pair)) for pair in range(2)}
-        w2s = reordered("w2s", sw2, U8)
-        w3q.append(quantised("w3q1", KP, ("sw2", 0)))
+        w3q.append(quantised("w3q1", KP))
         quantise(w3q[1], slice(0, KP), w3_bf[1][:])
         bufs[1, 0] = biased_buffer(1, 0, (4, 5))
         v2 = [tile("v2_%d" % h, [P, HALF], U32) for h in range(2)]
@@ -249,49 +248,44 @@ def tile_list_warhead_site_triage_kernel(
             in_=bo_ps[:, 0 : 3 * P].rearrange("p (k r) -> p r k", k=3)[:, 0:2],
         )
 
-        def scaled(g, h, engine, after=None):
-            hb = tile("hb%d_%d" % (g, h), [P, HALF, PACK], BF16, after)
+        def scale(hb, g, h, engine):
             factor = gaint[:, g : g + 1, :].to_broadcast([P, HALF, PACK])
-            engine.tensor_tensor(hb[:], gl[g, h][:], factor, MULT)
-            return hb[:].rearrange("p n t -> p (n t)")
+            engine.tensor_tensor(hb.rearrange("p (n t) -> p n t", t=PACK), gl[g, h][:], factor, MULT)
 
-        w4_bf = {}
-        w4q = {}
+        WIDE = PACK * PIECE
 
-        def w4_round(g, u, copy, after=None):
-            w4_bf[g, u] = tile("w4_bf%d_%d" % (g, u), [P, PACK * PIECE], BF16, after)
+        def w4_round(dst, g, u, copy):
             copy(
-                out=w4_bf[g, u][:].rearrange("p (c i j) -> p c j i", i=RUN, j=PACK),
+                out=dst.rearrange("p (c i j) -> p c j i", i=RUN, j=PACK),
                 in_=w4_raw[g, u][:].rearrange("p j (c i) -> p c j i", i=RUN),
             )
 
-        def w4_quantise(g, u, after=None):
-            w4q[g, u] = quantised("w4q%d_%d" % (g, u), PIECE, after)
-            quantise(w4q[g, u], slice(0, PIECE), w4_bf[g, u][:])
-
+        w4_bf0 = tile("w4_bf0", [P, 2 * WIDE], BF16, ("t2", 0))
         for g in range(2):
-            w4_bf[g, 0] = tile("w4_bf%d_0" % g, [P, PACK * PIECE], BF16, ("t2", 2 * PACK * PIECE * g))
             nc.gpsimd.tensor_scalar(
-                w4_bf[g, 0][:].rearrange("p (c j) -> p c j", j=PACK), w4_raw[g, 0][:].rearrange("p j c -> p c j"),
-                1.0, 0.0, MULT, ADD,
+                w4_bf0[:, WIDE * g : WIDE * (g + 1)].rearrange("p (c j) -> p c j", j=PACK),
+                w4_raw[g, 0][:].rearrange("p j c -> p c j"), 1.0, 0.0, MULT, ADD,
             )
-        w4_round(0, 1, nc.scalar.copy, ("x1_1", 0))
-        for g, u in ((1, 1), (0, 2)):
-            w4_round(g, u, nc.scalar.copy)
+        w4_bf1 = tile("w4_bf1", [P, 2 * WIDE], BF16, ("x1_1", 0))
+        for g in range(2):
+            w4_round(w4_bf1[:, WIDE * g : WIDE * (g + 1)], g, 1, nc.scalar.copy)
+        w4_bf2 = [tile("w4_bf2_%d" % g, [P, WIDE], BF16) for g in range(2)]
+        w4_round(w4_bf2[0][:], 0, 2, nc.scalar.copy)
 
         v1 = [gather("v1_%d" % a, t1[a][:].bitcast(U32), l1, U32, ("buf1_%d" % a, 0)) for a in range(2)]
-        hb0 = [scaled(0, h, nc.gpsimd) for h in range(2)]
-        hq = [quantised("hq0", S, ("t1_1", 0)), quantised("hq1", S)]
+        hb0 = tile("hb0", [P, 2 * WIDE], BF16)
         for h in range(2):
-            quantise(hq[0], halves[h], hb0[h])
-        hb1 = [scaled(1, 0, nc.vector, ("t1_1", 4 * S))]
-        w4_quantise(0, 0, ("t1_1", 12 * S))
-        hb1.append(scaled(1, 1, nc.vector, ("t1_1", 8 * S)))
-        quantise(hq[1], halves[0], hb1[0])
-        w4_quantise(1, 0, ("t1_1", 14 * S))
-        quantise(hq[1], halves[1], hb1[1])
-        w4_quantise(0, 1)
-        w4_quantise(1, 1)
+            scale(hb0[:, WIDE * h : WIDE * (h + 1)], 0, h, nc.gpsimd)
+        hq = [quantised("hq0", S, ("t1_1", 0)), quantised("hq1", S)]
+        hb1 = [tile("hb1_%d" % h, [P, WIDE], BF16, ("t1_1", 4 * S * (h + 1))) for h in range(2)]
+        w4q = [quantised("w4q0", S, ("t1_1", 12 * S)), quantised("w4q1", S), quantised("w4q2", S)]
+        quantise(hq[0], slice(0, S), hb0[:])
+        scale(hb1[0][:], 1, 0, nc.vector)
+        quantise(w4q[0], slice(0, S), w4_bf0[:])
+        scale(hb1[1][:], 1, 1, nc.vector)
+        quantise(hq[1], halves[0], hb1[0][:])
+        quantise(hq[1], halves[1], hb1[1][:])
+        quantise(w4q[1], slice(0, S), w4_bf1[:])
 
         accs = [bank("acc%d" % c, c) for c in range(N // P)]
 
@@ -304,8 +298,8 @@ def tile_list_warhead_site_triage_kernel(
             )
 
         def w4_pass(g, c):
-            codes, scales = w4q[g, c // 2]
-            cols = slice(P * (c % 2), P * (c % 2 + 1))
+            codes, scales = w4q[c // 2]
+            cols = slice(PIECE * g + P * (c % 2), PIECE * g + P * (c % 2 + 1))
             nc.tensor.matmul_mx(
                 out=accs[c][:], lhsT=codes[:, cols].bitcast(FP8X4), lhsT_scale=scales[:, cols],
                 rhs=hq[g][0][:].bitcast(FP8X4), rhs_scale=hq[g][1][:], start=False, stop=(g == 1),
@@ -327,11 +321,11 @@ def tile_list_warhead_site_triage_kernel(
         finish(0, True, ("w4_raw0_2", -1024))
         finish(1, True, ("w4_raw0_2", 1024))
         finish(2, True, ("w4_raw0_2", 3072))
-        finish(3, True)
-        w4_quantise(0, 2)
-        w4_round(1, 2, nc.vector.tensor_copy)
-        w4_quantise(1, 2)
+        quantise(w4q[2], halves[0], w4_bf2[0][:])
+        w4_round(w4_bf2[1][:], 1, 2, nc.vector.tensor_copy)
+        quantise(w4q[2], halves[1], w4_bf2[1][:])
         for g, c in ((0, 4), (0, 5), (1, 4), (1, 5)):
             w4_pass(g, c)
+        finish(3, False, ("w4_raw1_2", 0))
         finish(4, True)
         finish(5, False)

@@ -63,11 +63,12 @@ def tile_list_warhead_site_triage_kernel(
             engine.memset(held[:].bitcast(I32), 0)
             return held
 
-        s3 = scale_tile("s3", T3, nc.vector)
-        sw2 = scale_tile("sw2", H, nc.gpsimd)
+        s3 = scale_tile("s3", T3, nc.gpsimd)
         s2 = scale_tile("s2", T2, nc.vector)
         s1 = scale_tile("s1", T, nc.vector)
         swr = scale_tile("swr", N, nc.vector)
+        sw2 = scale_tile("sw2", H, nc.vector)
+        place["free"] = place["free"] + H
         bo_rows = tile("bo_rows", [P, N // 2], F32)
         nc.vector.memset(bo_rows[:], 0.0)
 
@@ -112,19 +113,20 @@ def tile_list_warhead_site_triage_kernel(
 
         l3 = load_list("l3", offs3)
         t3 = load_fp4_words("t3", tab3_words[0])
-        load_scales(nc.sync, s3, tab3_scales, 0)
-        load_scales(nc.gpsimd, sw2, w2_scales, 0)
+        load_scales(nc.gpsimd, s3, tab3_scales, 0)
         load_scales(nc.gpsimd, s1, tab_scales, RES_ROW)
         ident = tile("ident", [P, P], F32)
         make_identity(nc, ident[:])
-        l2 = load_list("l2", offs2)
         load_rows(w3_raw[0], w3, 0, 0, KP)
+        l2 = load_list("l2", offs2)
         load_scales(nc.sync, s2, tab2_scales, 0)
-        b3t = load_channels("b3t", b3)
         w2w = load_fp4_words("w2w", w2_words[0])
+        place["free"] = place["free"] + S
         load_rows(w3_raw[1], w3, 0, KP, H)
-        l1 = load_list("l1", offs)
+        b3t = load_channels("b3t", b3)
+        load_scales(nc.sync, sw2, w2_scales, 0)
         t2 = load_fp8_words("t2", tab2_words[0])
+        l1 = load_list("l1", offs)
         gaint = load_channels("gaint", gain)
         load_w4(0, 0)
         load_w4(1, 0)
@@ -149,8 +151,8 @@ def tile_list_warhead_site_triage_kernel(
         def quantise(pair, cols, src):
             nc.vector.quantize_mx(out=pair[0][:, cols].bitcast(FP8X4), scales=pair[1][:, cols], in_=src)
 
-        def reordered(name, src, dtype, after=None):
-            held = tile(name, [P, H], dtype, after)
+        def reordered(name, src, dtype):
+            held = tile(name, [P, H], dtype)
             nc.vector.tensor_copy(
                 out=held[:].rearrange("p (g t m) -> p g t m", g=2, t=PACK),
                 in_=src[:].rearrange("p (g m t) -> p g t m", g=2, t=PACK),
@@ -159,16 +161,10 @@ def tile_list_warhead_site_triage_kernel(
 
         w3_bf = [tile("w3_bf%d" % g, [P, PACK * KP], BF16) for g in range(2)]
 
-        def w3_round_on_scalar(g, ms):
+        def w3_round(g):
             nc.scalar.copy(
-                out=w3_bf[g][:].rearrange("p (t m j) -> p m j t", t=PACK, j=PACK)[:, ms],
-                in_=w3_raw[g][:].rearrange("p j (m t) -> p m j t", t=PACK)[:, ms],
-            )
-
-        def w3_round_on_vector(g, ms):
-            nc.vector.tensor_copy(
-                out=w3_bf[g][:].rearrange("p (u e m j) -> p u m j e", u=2, e=2, j=PACK)[:, :, ms],
-                in_=w3_raw[g][:].rearrange("p j (m u e) -> p u m j e", u=2, e=2)[:, :, ms],
+                out=w3_bf[g][:].rearrange("p (t m j) -> p m j t", t=PACK, j=PACK),
+                in_=w3_raw[g][:].rearrange("p j (m t) -> p m j t", t=PACK),
             )
 
         def biased_buffer(g, pair, banks, after=None):
@@ -185,17 +181,15 @@ def tile_list_warhead_site_triage_kernel(
             return held
 
         v3 = gather("v3", t3[:], l3, U16)
-        v3s = gather("v3s", s3[:], l3, U8)
-        w3_round_on_scalar(0, slice(0, P))
+        for g in range(2):
+            w3_round(g)
         v2s = gather("v2s", s2[:], l2, U8)
         w2p = reordered("w2p", w2w, U16)
-        w3q = [quantised("w3q0", KP, ("w2w", 0))]
+        w3q = [quantised("w3q0", KP, ("w2w", S)), quantised("w3q1", KP, ("sw2", 0))]
         quantise(w3q[0], slice(0, KP), w3_bf[0][:])
-        w2s = reordered("w2s", sw2, U8, ("w3_bf0", 0))
-        w3_round_on_scalar(1, slice(0, P // 2))
-        w3_round_on_vector(1, slice(P // 2, P))
+        v3s = gather("v3s", s3[:], l3, U8, ("w2w", 0))
         bufs = {(0, pair): biased_buffer(0, pair, (2 * pair, 2 * pair + 1), ("w3_raw1", 8 * S * pair)) for pair in range(2)}
-        w3q.append(quantised("w3q1", KP))
+        w2s = reordered("w2s", sw2, U8)
         quantise(w3q[1], slice(0, KP), w3_bf[1][:])
         bufs[1, 0] = biased_buffer(1, 0, (4, 5))
         v2 = [tile("v2_%d" % h, [P, HALF], U32) for h in range(2)]

@@ -58,19 +58,13 @@ def tile_list_warhead_site_triage_kernel(
         nc.vector.memset(warm_in[:], 0.0)
         nc.scalar.activation(warm_out[:], warm_in[:], ACT.Gelu_apprx_tanh)
 
-        def scale_tile(name, width, engine):
-            held = tile(name, [P, width], U8)
+        def scale_tile(name, width, engine, after=None):
+            held = tile(name, [P, width], U8, after)
             engine.memset(held[:].bitcast(I32), 0)
             return held
 
         s3 = scale_tile("s3", T3, nc.gpsimd)
         s2 = scale_tile("s2", T2, nc.vector)
-        s1 = scale_tile("s1", T, nc.vector)
-        swr = scale_tile("swr", N, nc.vector)
-        sw2 = scale_tile("sw2", H, nc.vector)
-        place["free"] = place["free"] + H
-        bo_rows = tile("bo_rows", [P, N // 2], F32)
-        nc.vector.memset(bo_rows[:], 0.0)
 
         def load_scales(queue, held, scales, first):
             for q in range(4):
@@ -111,9 +105,22 @@ def tile_list_warhead_site_triage_kernel(
         def load_w4(g, u):
             load_rows(w4_raw[g, u], w4, g, PIECE * u, PIECE * (u + 1))
 
+        def gather(name, window, lst, dtype, after=None):
+            got = tile(name, [P, S], dtype, after)
+            nc.vector.tensor_copy(got[:], window.indirect(lst[:]))
+            return got
+
         l3 = load_list("l3", offs3)
+        place["free"] = place["free"] + 2 * N
         t3 = load_fp4_words("t3", tab3_words[0])
+        place["free"] = place["free"] + 2 * H
+        v3 = gather("v3", t3[:], l3, U16)
         load_scales(nc.gpsimd, s3, tab3_scales, 0)
+        s1 = scale_tile("s1", T, nc.gpsimd)
+        sw2 = scale_tile("sw2", H, nc.vector, ("t3", 2 * T3 - ALIGN))
+        swr = scale_tile("swr", N, nc.vector, ("t3", ALIGN))
+        bo_rows = tile("bo_rows", [P, N // 2], F32, ("t3", ALIGN - 2 * N))
+        nc.vector.memset(bo_rows[:], 0.0)
         load_scales(nc.gpsimd, s1, tab_scales, RES_ROW)
         ident = tile("ident", [P, P], F32)
         make_identity(nc, ident[:])
@@ -139,11 +146,6 @@ def tile_list_warhead_site_triage_kernel(
             load_w4(g, u)
 
         halves = [slice(0, HALF), slice(HALF, S)]
-
-        def gather(name, window, lst, dtype, after=None):
-            got = tile(name, [P, S], dtype, after)
-            nc.vector.tensor_copy(got[:], window.indirect(lst[:]))
-            return got
 
         def quantised(name, width, after=None):
             return tile(name + "_c", [P, width], U32, after), tile(name + "_s", [P, width], U8)
@@ -180,7 +182,6 @@ def tile_list_warhead_site_triage_kernel(
                 nc.scalar.activation(held[:, e, :], acc[:], ACT.Identity, bias=b3t[:, g, t : t + 1])
             return held
 
-        v3 = gather("v3", t3[:], l3, U16)
         for g in range(2):
             w3_round(g)
         v2s = gather("v2s", s2[:], l2, U8)
@@ -267,7 +268,7 @@ def tile_list_warhead_site_triage_kernel(
         w4_round(w4_bf2[0][:], 0, 2, nc.scalar.copy)
 
         v1 = [gather("v1_%d" % a, t1[a][:].bitcast(U32), l1, U32, ("buf1_%d" % a, 0)) for a in range(2)]
-        hb0 = tile("hb0", [P, 2 * WIDE], BF16)
+        hb0 = tile("hb0", [P, 2 * WIDE], BF16, ("w4_raw1_0", 0))
         for h in range(2):
             scale(hb0[:, WIDE * h : WIDE * (h + 1)], 0, h, nc.gpsimd)
         hq = [quantised("hq0", S, ("t1_1", 0)), quantised("hq1", S)]

@@ -28,6 +28,7 @@ RUN = 4
 HALF = S // 2
 PIECE = 2 * P
 RES_ROW = 8
+W3_ON_SCALAR = 64
 
 
 def tile_list_warhead_site_triage_kernel(
@@ -53,18 +54,22 @@ def tile_list_warhead_site_triage_kernel(
         def bank(name, b):
             return ps.tile([P, S], F32, name=name, tag="bank%d" % b)
 
+        def scale_tile(name, width):
+            held = tile(name, [P, width], U8)
+            nc.vector.memset(held[:].bitcast(I32), 0)
+            return held
+
         warm_in = tile("warm_in", [P, 1], F32)
         warm_out = tile("warm_out", [P, 1], F32)
         nc.vector.memset(warm_in[:], 0.0)
         nc.scalar.activation(warm_out[:], warm_in[:], ACT.Gelu_apprx_tanh)
-
-        def scale_tile(name, width, engine, after=None):
-            held = tile(name, [P, width], U8, after)
-            engine.memset(held[:].bitcast(I32), 0)
-            return held
-
-        s3 = scale_tile("s3", T3, nc.gpsimd)
-        s2 = scale_tile("s2", T2, nc.vector)
+        s3 = scale_tile("s3", T3)
+        s2 = scale_tile("s2", T2)
+        s1 = scale_tile("s1", T)
+        sw2 = scale_tile("sw2", H)
+        swr = scale_tile("swr", N)
+        bo_rows = tile("bo_rows", [P, N // 2], F32)
+        nc.vector.memset(bo_rows[:], 0.0)
 
         def load_scales(queue, held, scales, first):
             for q in range(4):
@@ -89,61 +94,51 @@ def tile_list_warhead_site_triage_kernel(
             nc.sync.dma_start(out=held[:].bitcast(I32), in_=words.bitcast(I32))
             return held
 
-        def load_rows(raw, w, g, lo, hi):
+        def load_rows(name, w, g, lo, hi):
+            raw = tile(name, [P, PACK, hi - lo], F32)
             nc.sync.dma_start(out=raw[:], in_=w[KP * g : KP * (g + 1), lo:hi].rearrange("(p j) n -> p j n", j=PACK))
+            return raw
 
         def load_channels(name, vec):
             held = tile(name, [P, 2, PACK], F32)
             nc.sync.dma_start(out=held[:], in_=vec.rearrange("(g p t) -> p g t", g=2, t=PACK))
             return held
 
-        w3_raw = [tile("w3_raw%d" % g, [P, PACK, KP], F32) for g in range(2)]
         w4_raw = {}
-        for g, u in ((0, 0), (1, 0), (0, 1), (0, 2), (1, 1), (1, 2)):
-            w4_raw[g, u] = tile("w4_raw%d_%d" % (g, u), [P, PACK, PIECE], F32)
 
         def load_w4(g, u):
-            load_rows(w4_raw[g, u], w4, g, PIECE * u, PIECE * (u + 1))
+            w4_raw[g, u] = load_rows("w4_raw%d_%d" % (g, u), w4, g, PIECE * u, PIECE * (u + 1))
 
         def gather(name, window, lst, dtype, after=None):
             got = tile(name, [P, S], dtype, after)
             nc.vector.tensor_copy(got[:], window.indirect(lst[:]))
             return got
 
-        l3 = load_list("l3", offs3)
-        place["free"] = place["free"] + 2 * N
-        t3 = load_fp4_words("t3", tab3_words[0])
-        place["free"] = place["free"] + 2 * H
-        v3 = gather("v3", t3[:], l3, U16)
-        load_scales(nc.gpsimd, s3, tab3_scales, 0)
-        s1 = scale_tile("s1", T, nc.gpsimd)
-        sw2 = scale_tile("sw2", H, nc.vector, ("t3", 2 * T3 - ALIGN))
-        swr = scale_tile("swr", N, nc.vector, ("t3", ALIGN))
-        bo_rows = tile("bo_rows", [P, N // 2], F32, ("t3", ALIGN - 2 * N))
-        nc.vector.memset(bo_rows[:], 0.0)
+        load_scales(nc.scalar, s3, tab3_scales, 0)
+        load_scales(nc.scalar, s2, tab2_scales, 0)
         load_scales(nc.gpsimd, s1, tab_scales, RES_ROW)
         ident = tile("ident", [P, P], F32)
         make_identity(nc, ident[:])
-        load_rows(w3_raw[0], w3, 0, 0, KP)
+        l3 = load_list("l3", offs3)
+        t3 = load_fp4_words("t3", tab3_words[0])
         l2 = load_list("l2", offs2)
-        load_scales(nc.sync, s2, tab2_scales, 0)
-        w2w = load_fp4_words("w2w", w2_words[0])
-        place["free"] = place["free"] + S
-        load_rows(w3_raw[1], w3, 0, KP, H)
+        w3_raw = [load_rows("w3_raw0", w3, 0, 0, KP)]
         b3t = load_channels("b3t", b3)
+        w3_raw.append(load_rows("w3_raw1", w3, 0, KP, H))
+        w2w = load_fp4_words("w2w", w2_words[0])
         load_scales(nc.sync, sw2, w2_scales, 0)
-        t2 = load_fp8_words("t2", tab2_words[0])
         l1 = load_list("l1", offs)
+        t2 = load_fp8_words("t2", tab2_words[0])
         gaint = load_channels("gaint", gain)
-        load_w4(0, 0)
-        load_w4(1, 0)
-        t1 = [load_fp8_words("t1_%d" % a, tab_words[a]) for a in range(2)]
+        t1 = [load_fp8_words("t1_0", tab_words[0])]
         nc.sync.dma_start(out=bo_rows[0:2, :], in_=bo.rearrange("(r n) -> r n", r=2))
         load_scales(nc.sync, swr, wr_scales, RES_ROW)
         wrw = tile("wrw", [P, 2, N], I32)
         nc.sync.dma_start(out=wrw[:], in_=wr_words.rearrange("a p n i -> p a (n i)").bitcast(I32))
-        for g, u in ((0, 1), (1, 1), (0, 2), (1, 2)):
-            load_w4(g, u)
+        t1.append(load_fp8_words("t1_1", tab_words[1]))
+        for u in range(3):
+            for g in range(2):
+                load_w4(g, u)
 
         halves = [slice(0, HALF), slice(HALF, S)]
 
@@ -153,9 +148,9 @@ def tile_list_warhead_site_triage_kernel(
         def quantise(pair, cols, src):
             nc.vector.quantize_mx(out=pair[0][:, cols].bitcast(FP8X4), scales=pair[1][:, cols], in_=src)
 
-        def reordered(name, src, dtype):
-            held = tile(name, [P, H], dtype)
-            nc.vector.tensor_copy(
+        def reordered(name, src, dtype, engine, after=None):
+            held = tile(name, [P, H], dtype, after)
+            engine.tensor_copy(
                 out=held[:].rearrange("p (g t m) -> p g t m", g=2, t=PACK),
                 in_=src[:].rearrange("p (g m t) -> p g t m", g=2, t=PACK),
             )
@@ -164,17 +159,18 @@ def tile_list_warhead_site_triage_kernel(
         w3_bf = [tile("w3_bf%d" % g, [P, PACK * KP], BF16) for g in range(2)]
 
         def w3_round(g):
-            nc.scalar.copy(
-                out=w3_bf[g][:].rearrange("p (t m j) -> p m j t", t=PACK, j=PACK),
-                in_=w3_raw[g][:].rearrange("p j (m t) -> p m j t", t=PACK),
-            )
+            dst = w3_bf[g][:].rearrange("p (t m j) -> p m j t", t=PACK, j=PACK)
+            src = w3_raw[g][:].rearrange("p j (m t) -> p m j t", t=PACK)
+            cut = W3_ON_SCALAR
+            nc.scalar.copy(out=dst[:, 0:cut], in_=src[:, 0:cut])
+            nc.vector.tensor_copy(out=dst[:, cut:P], in_=src[:, cut:P])
 
-        def biased_buffer(g, pair, banks, after=None):
+        def biased_buffer(g, pair, after=None):
             held = tile("buf%d_%d" % (g, pair), [P, 2, S], F32, after)
             for e in range(2):
                 t = 2 * pair + e
                 cols = slice(P * t, P * (t + 1))
-                acc = bank("buf_ps", banks[e])
+                acc = bank("buf_ps", PACK * g + t)
                 nc.tensor.matmul_mx(
                     out=acc[:], lhsT=w3q[g][0][:, cols].bitcast(FP8X4), lhsT_scale=w3q[g][1][:, cols],
                     rhs=v3[:].bitcast(FP4X4), rhs_scale=v3s[:], start=True, stop=True,
@@ -182,17 +178,20 @@ def tile_list_warhead_site_triage_kernel(
                 nc.scalar.activation(held[:, e, :], acc[:], ACT.Identity, bias=b3t[:, g, t : t + 1])
             return held
 
-        for g in range(2):
-            w3_round(g)
+        v3 = gather("v3", t3[:], l3, U16)
+        v3s = gather("v3s", s3[:], l3, U8)
         v2s = gather("v2s", s2[:], l2, U8)
-        w2p = reordered("w2p", w2w, U16)
-        w3q = [quantised("w3q0", KP, ("w2w", S)), quantised("w3q1", KP, ("sw2", 0))]
+        w3_round(0)
+        w3q = [quantised("w3q%d" % g, KP) for g in range(2)]
         quantise(w3q[0], slice(0, KP), w3_bf[0][:])
-        v3s = gather("v3s", s3[:], l3, U8, ("w2w", 0))
-        bufs = {(0, pair): biased_buffer(0, pair, (2 * pair, 2 * pair + 1), ("w3_raw1", 8 * S * pair)) for pair in range(2)}
-        w2s = reordered("w2s", sw2, U8)
+        w3_round(1)
+        w2p = reordered("w2p", w2w, U16, nc.vector)
         quantise(w3q[1], slice(0, KP), w3_bf[1][:])
-        bufs[1, 0] = biased_buffer(1, 0, (4, 5))
+        w2s = reordered("w2s", sw2, U8, nc.gpsimd, ("w3_bf1", 0))
+        v1s = gather("v1s", s1[:], l1, U8)
+        bufs = {(0, pair): biased_buffer(0, pair, ("w3_raw1", 8 * S * pair)) for pair in range(2)}
+        for pair in range(2):
+            bufs[1, pair] = biased_buffer(1, pair)
         v2 = [tile("v2_%d" % h, [P, HALF], U32) for h in range(2)]
         for h in range(2):
             nc.vector.tensor_copy(v2[h][:], t2[:].bitcast(U32).indirect(l2[:, 16 * h : 16 * (h + 1)]))
@@ -201,7 +200,7 @@ def tile_list_warhead_site_triage_kernel(
         gl = {}
 
         def product(g, h, pair):
-            acc = bank("site_ps", PACK * g + 2 * pair + h)
+            acc = bank("site_ps", PACK * g + 2 * h + pair)
             for e in range(2):
                 lo = KP * g + P * (2 * pair + e)
                 nc.tensor.matmul_mx(
@@ -221,18 +220,11 @@ def tile_list_warhead_site_triage_kernel(
                 ACT.Gelu_apprx_tanh,
             )
 
-        for h in range(2):
-            for pair in range(2):
-                product(0, h, pair)
-        gelu(0, 0)
-        bufs[1, 1] = biased_buffer(1, 1, (1, 3))
-        gelu(0, 1)
-        for h in range(2):
-            product(1, h, 0)
-        v1s = gather("v1s", s1[:], l1, U8, ("buf0_1", 0))
-        for h in range(2):
-            product(1, h, 1)
-            gelu(1, h)
+        for g in range(2):
+            for h in range(2):
+                for pair in range(2):
+                    product(g, h, pair)
+                gelu(g, h)
 
         bo_ps = bank("bo_ps", 7)
         for k in range(3):
@@ -249,38 +241,42 @@ def tile_list_warhead_site_triage_kernel(
 
         WIDE = PACK * PIECE
 
-        def w4_round(dst, g, u, copy):
+        w4_bf = {}
+
+        def w4_round(g, u, copy):
+            w4_bf[g, u] = tile("w4_bf%d_%d" % (g, u), [P, WIDE], BF16)
             copy(
-                out=dst.rearrange("p (c i j) -> p c j i", i=RUN, j=PACK),
+                out=w4_bf[g, u][:].rearrange("p (c i j) -> p c j i", i=RUN, j=PACK),
                 in_=w4_raw[g, u][:].rearrange("p j (c i) -> p c j i", i=RUN),
             )
 
-        w4_bf0 = tile("w4_bf0", [P, 2 * WIDE], BF16, ("t2", 0))
-        for g in range(2):
-            nc.gpsimd.tensor_scalar(
-                w4_bf0[:, WIDE * g : WIDE * (g + 1)].rearrange("p (c j) -> p c j", j=PACK),
-                w4_raw[g, 0][:].rearrange("p j c -> p c j"), 1.0, 0.0, MULT, ADD,
-            )
-        w4_bf1 = tile("w4_bf1", [P, 2 * WIDE], BF16, ("x1_1", 0))
-        for g in range(2):
-            w4_round(w4_bf1[:, WIDE * g : WIDE * (g + 1)], g, 1, nc.scalar.copy)
-        w4_bf2 = [tile("w4_bf2_%d" % g, [P, WIDE], BF16) for g in range(2)]
-        w4_round(w4_bf2[0][:], 0, 2, nc.scalar.copy)
+        for u in range(2):
+            for g in range(2):
+                w4_round(g, u, nc.scalar.copy)
 
         v1 = [gather("v1_%d" % a, t1[a][:].bitcast(U32), l1, U32, ("buf1_%d" % a, 0)) for a in range(2)]
-        hb0 = tile("hb0", [P, 2 * WIDE], BF16, ("w4_raw1_0", 0))
+        hb0 = tile("hb0", [P, 2 * WIDE], BF16)
         for h in range(2):
             scale(hb0[:, WIDE * h : WIDE * (h + 1)], 0, h, nc.gpsimd)
         hq = [quantised("hq0", S, ("t1_1", 0)), quantised("hq1", S)]
         hb1 = [tile("hb1_%d" % h, [P, WIDE], BF16, ("t1_1", 4 * S * (h + 1))) for h in range(2)]
-        w4q = [quantised("w4q0", S, ("t1_1", 12 * S)), quantised("w4q1", S), quantised("w4q2", S)]
-        quantise(hq[0], slice(0, S), hb0[:])
+        w4q = {(g, u): quantised("w4q%d_%d" % (g, u), PIECE) for u in range(3) for g in range(2)}
+
+        def w4_quantise(g, u):
+            quantise(w4q[g, u], slice(0, PIECE), w4_bf[g, u][:])
+
         scale(hb1[0][:], 1, 0, nc.vector)
-        quantise(w4q[0], slice(0, S), w4_bf0[:])
+        quantise(hq[0], slice(0, S), hb0[:])
+        w4_quantise(0, 0)
         scale(hb1[1][:], 1, 1, nc.vector)
         quantise(hq[1], halves[0], hb1[0][:])
+        w4_quantise(1, 0)
         quantise(hq[1], halves[1], hb1[1][:])
-        quantise(w4q[1], slice(0, S), w4_bf1[:])
+        w4_quantise(0, 1)
+        w4_quantise(1, 1)
+        for g in range(2):
+            w4_round(g, 2, nc.vector.tensor_copy)
+            w4_quantise(g, 2)
 
         accs = [bank("acc%d" % c, c) for c in range(N // P)]
 
@@ -293,8 +289,8 @@ def tile_list_warhead_site_triage_kernel(
             )
 
         def w4_pass(g, c):
-            codes, scales = w4q[c // 2]
-            cols = slice(PIECE * g + P * (c % 2), PIECE * g + P * (c % 2 + 1))
+            codes, scales = w4q[g, c // 2]
+            cols = slice(P * (c % 2), P * (c % 2 + 1))
             nc.tensor.matmul_mx(
                 out=accs[c][:], lhsT=codes[:, cols].bitcast(FP8X4), lhsT_scale=scales[:, cols],
                 rhs=hq[g][0][:].bitcast(FP8X4), rhs_scale=hq[g][1][:], start=False, stop=(g == 1),
@@ -311,16 +307,13 @@ def tile_list_warhead_site_triage_kernel(
         for a in range(2):
             for c in range(N // P):
                 wr_pass(a, c)
-        for g, c in ((0, 0), (0, 1), (1, 0), (1, 1), (0, 2), (0, 3), (1, 2), (1, 3)):
-            w4_pass(g, c)
-        finish(0, True, ("w4_raw0_2", -1024))
-        finish(1, True, ("w4_raw0_2", 1024))
-        finish(2, True, ("w4_raw0_2", 3072))
-        quantise(w4q[2], halves[0], w4_bf2[0][:])
-        w4_round(w4_bf2[1][:], 1, 2, nc.vector.tensor_copy)
-        quantise(w4q[2], halves[1], w4_bf2[1][:])
-        for g, c in ((0, 4), (0, 5), (1, 4), (1, 5)):
-            w4_pass(g, c)
-        finish(3, False, ("w4_raw1_2", 0))
+        for u in range(3):
+            for g in range(2):
+                for c in (2 * u, 2 * u + 1):
+                    w4_pass(g, c)
+        finish(0, True, ("w4_raw1_1", 0))
+        finish(1, True, ("w4_raw1_1", 4 * S))
+        finish(2, True)
+        finish(3, True)
         finish(4, True)
         finish(5, False)

@@ -54,22 +54,19 @@ def tile_list_warhead_site_triage_kernel(
         def bank(name, b):
             return ps.tile([P, S], F32, name=name, tag="bank%d" % b)
 
-        def scale_tile(name, width):
+        def scale_tile(name, width, engine):
             held = tile(name, [P, width], U8)
-            nc.vector.memset(held[:].bitcast(I32), 0)
+            engine.memset(held[:].bitcast(I32), 0)
             return held
 
         warm_in = tile("warm_in", [P, 1], F32)
         warm_out = tile("warm_out", [P, 1], F32)
         nc.vector.memset(warm_in[:], 0.0)
         nc.scalar.activation(warm_out[:], warm_in[:], ACT.Gelu_apprx_tanh)
-        s3 = scale_tile("s3", T3)
-        s2 = scale_tile("s2", T2)
-        s1 = scale_tile("s1", T)
-        sw2 = scale_tile("sw2", H)
-        swr = scale_tile("swr", N)
-        bo_rows = tile("bo_rows", [P, N // 2], F32)
-        nc.vector.memset(bo_rows[:], 0.0)
+        s3 = scale_tile("s3", T3, nc.gpsimd)
+        s1 = scale_tile("s1", T, nc.gpsimd)
+        s2 = scale_tile("s2", T2, nc.vector)
+        sw2 = scale_tile("sw2", H, nc.vector)
 
         def load_scales(queue, held, scales, first):
             for q in range(4):
@@ -114,15 +111,18 @@ def tile_list_warhead_site_triage_kernel(
             nc.vector.tensor_copy(got[:], window.indirect(lst[:]))
             return got
 
-        load_scales(nc.scalar, s3, tab3_scales, 0)
-        load_scales(nc.scalar, s2, tab2_scales, 0)
         load_scales(nc.gpsimd, s1, tab_scales, RES_ROW)
+        swr = scale_tile("swr", N, nc.gpsimd)
+        bo_rows = tile("bo_rows", [P, N // 2], F32)
+        nc.gpsimd.memset(bo_rows[:], 0.0)
         ident = tile("ident", [P, P], F32)
         make_identity(nc, ident[:])
         l3 = load_list("l3", offs3)
         t3 = load_fp4_words("t3", tab3_words[0])
-        l2 = load_list("l2", offs2)
+        load_scales(nc.sync, s3, tab3_scales, 0)
         w3_raw = [load_rows("w3_raw0", w3, 0, 0, KP)]
+        l2 = load_list("l2", offs2)
+        load_scales(nc.sync, s2, tab2_scales, 0)
         b3t = load_channels("b3t", b3)
         w3_raw.append(load_rows("w3_raw1", w3, 0, KP, H))
         w2w = load_fp4_words("w2w", w2_words[0])

@@ -101,10 +101,15 @@ def tile_list_warhead_site_triage_kernel(
             nc.sync.dma_start(out=held[:], in_=vec.rearrange("(g p t) -> p g t", g=2, t=PACK))
             return held
 
+        def load_gain(g):
+            held = tile("gain%d" % g, [P, 1, PACK], F32)
+            nc.sync.dma_start(out=held[:, 0, :], in_=gain[KP * g : KP * (g + 1)].rearrange("(p t) -> p t", t=PACK))
+            return held
+
         w4_raw = {}
 
-        def load_w4(g, u):
-            w4_raw[g, u] = load_rows("w4_raw%d_%d" % (g, u), w4, g, PIECE * u, PIECE * (u + 1))
+        def load_w4(g, lo, hi):
+            w4_raw[g, lo] = load_rows("w4_raw%d_%d" % (g, lo), w4, g, P * lo, P * hi)
 
         def gather(name, window, lst, dtype, after=None):
             got = tile(name, [P, S], dtype, after)
@@ -129,16 +134,17 @@ def tile_list_warhead_site_triage_kernel(
         load_scales(nc.sync, sw2, w2_scales, 0)
         l1 = load_list("l1", offs)
         t2 = load_fp8_words("t2", tab2_words[0])
-        gaint = load_channels("gaint", gain)
+        gains = [load_gain(0)]
         t1 = [load_fp8_words("t1_0", tab_words[0])]
         nc.sync.dma_start(out=bo_rows[0:2, :], in_=bo.rearrange("(r n) -> r n", r=2))
         load_scales(nc.sync, swr, wr_scales, RES_ROW)
         wrw = tile("wrw", [P, 2, N], I32)
         nc.sync.dma_start(out=wrw[:], in_=wr_words.rearrange("a p n i -> p a (n i)").bitcast(I32))
         t1.append(load_fp8_words("t1_1", tab_words[1]))
-        for u in range(3):
-            for g in range(2):
-                load_w4(g, u)
+        load_w4(0, 0, 2)
+        gains.append(load_gain(1))
+        for g, lo, hi in ((1, 0, 2), (0, 2, 4), (1, 2, 4), (0, 4, 6), (1, 4, 5), (1, 5, 6)):
+            load_w4(g, lo, hi)
 
         halves = [slice(0, HALF), slice(HALF, S)]
 
@@ -236,47 +242,37 @@ def tile_list_warhead_site_triage_kernel(
         )
 
         def scale(hb, g, h, engine):
-            factor = gaint[:, g : g + 1, :].to_broadcast([P, HALF, PACK])
+            factor = gains[g][:].to_broadcast([P, HALF, PACK])
             engine.tensor_tensor(hb.rearrange("p (n t) -> p n t", t=PACK), gl[g, h][:], factor, MULT)
 
         WIDE = PACK * PIECE
 
-        w4_bf = {}
-
-        def w4_round(g, u, copy):
-            w4_bf[g, u] = tile("w4_bf%d_%d" % (g, u), [P, WIDE], BF16)
+        def w4_round(dst, g, lo, copy):
             copy(
-                out=w4_bf[g, u][:].rearrange("p (c i j) -> p c j i", i=RUN, j=PACK),
-                in_=w4_raw[g, u][:].rearrange("p j (c i) -> p c j i", i=RUN),
+                out=dst.rearrange("p (c i j) -> p c j i", i=RUN, j=PACK),
+                in_=w4_raw[g, lo][:].rearrange("p j (c i) -> p c j i", i=RUN),
             )
 
+        w4_bf = [tile("w4_bf%d" % u, [P, 2 * WIDE], BF16) for u in range(2)]
         for u in range(2):
             for g in range(2):
-                w4_round(g, u, nc.scalar.copy)
+                w4_round(w4_bf[u][:, WIDE * g : WIDE * (g + 1)], g, 2 * u, nc.scalar.copy)
 
         v1 = [gather("v1_%d" % a, t1[a][:].bitcast(U32), l1, U32, ("buf1_%d" % a, 0)) for a in range(2)]
-        hb0 = tile("hb0", [P, 2 * WIDE], BF16)
-        for h in range(2):
-            scale(hb0[:, WIDE * h : WIDE * (h + 1)], 0, h, nc.gpsimd)
-        hq = [quantised("hq0", S, ("t1_1", 0)), quantised("hq1", S)]
-        hb1 = [tile("hb1_%d" % h, [P, WIDE], BF16, ("t1_1", 4 * S * (h + 1))) for h in range(2)]
-        w4q = {(g, u): quantised("w4q%d_%d" % (g, u), PIECE) for u in range(3) for g in range(2)}
-
-        def w4_quantise(g, u):
-            quantise(w4q[g, u], slice(0, PIECE), w4_bf[g, u][:])
-
-        scale(hb1[0][:], 1, 0, nc.vector)
-        quantise(hq[0], slice(0, S), hb0[:])
-        w4_quantise(0, 0)
-        scale(hb1[1][:], 1, 1, nc.vector)
-        quantise(hq[1], halves[0], hb1[0][:])
-        w4_quantise(1, 0)
-        quantise(hq[1], halves[1], hb1[1][:])
-        w4_quantise(0, 1)
-        w4_quantise(1, 1)
-        for g in range(2):
-            w4_round(g, 2, nc.vector.tensor_copy)
-            w4_quantise(g, 2)
+        hb = [tile("hb%d" % g, [P, 2 * WIDE], BF16) for g in range(2)]
+        for g, engine in enumerate((nc.gpsimd, nc.vector)):
+            for h in range(2):
+                scale(hb[g][:, WIDE * h : WIDE * (h + 1)], g, h, engine)
+        hq = [quantised("hq0", S, ("gl1_0", 0)), quantised("hq1", S)]
+        w4q = [quantised("w4q%d" % u, S) for u in range(3)]
+        quantise(hq[0], slice(0, S), hb[0][:])
+        quantise(w4q[0], slice(0, S), w4_bf[0][:])
+        quantise(hq[1], slice(0, S), hb[1][:])
+        quantise(w4q[1], slice(0, S), w4_bf[1][:])
+        for g, lo, hi in ((0, 4, 6), (1, 4, 5), (1, 5, 6)):
+            late = tile("w4_late%d_%d" % (g, lo), [P, KP * (hi - lo)], BF16)
+            w4_round(late[:], g, lo, nc.vector.tensor_copy)
+            quantise(w4q[2], slice(PIECE * g + P * (lo - 4), PIECE * g + P * (hi - 4)), late[:])
 
         accs = [bank("acc%d" % c, c) for c in range(N // P)]
 
@@ -289,8 +285,8 @@ def tile_list_warhead_site_triage_kernel(
             )
 
         def w4_pass(g, c):
-            codes, scales = w4q[g, c // 2]
-            cols = slice(P * (c % 2), P * (c % 2 + 1))
+            codes, scales = w4q[c // 2]
+            cols = slice(PIECE * g + P * (c % 2), PIECE * g + P * (c % 2 + 1))
             nc.tensor.matmul_mx(
                 out=accs[c][:], lhsT=codes[:, cols].bitcast(FP8X4), lhsT_scale=scales[:, cols],
                 rhs=hq[g][0][:].bitcast(FP8X4), rhs_scale=hq[g][1][:], start=False, stop=(g == 1),
@@ -311,8 +307,8 @@ def tile_list_warhead_site_triage_kernel(
             for g in range(2):
                 for c in (2 * u, 2 * u + 1):
                     w4_pass(g, c)
-        finish(0, True, ("w4_raw1_1", 0))
-        finish(1, True, ("w4_raw1_1", 4 * S))
+        finish(0, True, ("w4_raw1_2", 0))
+        finish(1, True, ("w4_raw1_2", 4 * S))
         finish(2, True)
         finish(3, True)
         finish(4, True)

@@ -27,7 +27,7 @@ ALIGN = 64
 RUN = 4
 HALF = S // 2
 PIECE = 2 * P
-RES_ROW = 8
+TAB_ROW, WR_ROW = 4, 8
 W3_ON_SCALAR = 64
 
 
@@ -116,8 +116,8 @@ def tile_list_warhead_site_triage_kernel(
             nc.vector.tensor_copy(got[:], window.indirect(lst[:]))
             return got
 
-        load_scales(nc.gpsimd, s1, tab_scales, RES_ROW)
-        swr = scale_tile("swr", N, nc.gpsimd)
+        load_scales(nc.gpsimd, s1, tab_scales, TAB_ROW)
+        swr = scale_tile("swr", 2 * N, nc.gpsimd)
         bo_rows = tile("bo_rows", [P, N // 2], F32)
         nc.gpsimd.memset(bo_rows[:], 0.0)
         ident = tile("ident", [P, P], F32)
@@ -137,14 +137,18 @@ def tile_list_warhead_site_triage_kernel(
         gains = [load_gain(0)]
         t1 = [load_fp8_words("t1_0", tab_words[0])]
         nc.sync.dma_start(out=bo_rows[0:2, :], in_=bo.rearrange("(r n) -> r n", r=2))
-        load_scales(nc.sync, swr, wr_scales, RES_ROW)
+        for r in range(4):
+            nc.sync.dma_start(
+                out=swr[WR_ROW + r : P : 32, :].bitcast(I32).rearrange("q (a n) -> q a n", a=2),
+                in_=wr_scales[:, r:16:4, :].bitcast(I32).rearrange("a q n -> q a n"),
+            )
         wrw = tile("wrw", [P, 2, N], I32)
         nc.sync.dma_start(out=wrw[:], in_=wr_words.rearrange("a p n i -> p a (n i)").bitcast(I32))
         t1.append(load_fp8_words("t1_1", tab_words[1]))
-        load_w4(0, 0, 2)
         gains.append(load_gain(1))
-        for g, lo, hi in ((1, 0, 2), (0, 2, 4), (1, 2, 4), (0, 4, 6), (1, 4, 5), (1, 5, 6)):
-            load_w4(g, lo, hi)
+        for lo in (0, 2, 4):
+            for g in range(2):
+                load_w4(g, lo, lo + 2)
 
         halves = [slice(0, HALF), slice(HALF, S)]
 
@@ -253,10 +257,10 @@ def tile_list_warhead_site_triage_kernel(
                 in_=w4_raw[g, lo][:].rearrange("p j (c i) -> p c j i", i=RUN),
             )
 
-        w4_bf = [tile("w4_bf%d" % u, [P, 2 * WIDE], BF16) for u in range(2)]
+        w4_bf = {(g, u): tile("w4_bf%d_%d" % (g, u), [P, WIDE], BF16) for g, u in ((0, 0), (1, 0), (0, 1), (1, 1), (0, 2))}
         for u in range(2):
             for g in range(2):
-                w4_round(w4_bf[u][:, WIDE * g : WIDE * (g + 1)], g, 2 * u, nc.scalar.copy)
+                w4_round(w4_bf[g, u][:], g, 2 * u, nc.scalar.copy)
 
         v1 = [gather("v1_%d" % a, t1[a][:].bitcast(U32), l1, U32, ("buf1_%d" % a, 0)) for a in range(2)]
         hb = [tile("hb%d" % g, [P, 2 * WIDE], BF16) for g in range(2)]
@@ -266,22 +270,30 @@ def tile_list_warhead_site_triage_kernel(
         hq = [quantised("hq0", S, ("gl1_0", 0)), quantised("hq1", S)]
         w4q = [quantised("w4q%d" % u, S) for u in range(3)]
         quantise(hq[0], slice(0, S), hb[0][:])
-        quantise(w4q[0], slice(0, S), w4_bf[0][:])
+        quantise(w4q[0], halves[0], w4_bf[0, 0][:])
         quantise(hq[1], slice(0, S), hb[1][:])
-        quantise(w4q[1], slice(0, S), w4_bf[1][:])
-        for g, lo, hi in ((0, 4, 6), (1, 4, 5), (1, 5, 6)):
-            late = tile("w4_late%d_%d" % (g, lo), [P, KP * (hi - lo)], BF16)
-            w4_round(late[:], g, lo, nc.vector.tensor_copy)
-            quantise(w4q[2], slice(PIECE * g + P * (lo - 4), PIECE * g + P * (hi - 4)), late[:])
+        quantise(w4q[0], halves[1], w4_bf[1, 0][:])
+        for g in range(2):
+            quantise(w4q[1], halves[g], w4_bf[g, 1][:])
+        w4_round(w4_bf[0, 2][:], 0, 4, nc.vector.tensor_copy)
+        quantise(w4q[2], halves[0], w4_bf[0, 2][:])
+        last = [tile("w4_last%d" % e, [P, KP], BF16) for e in range(2)]
+        for e in range(2):
+            nc.vector.tensor_copy(
+                out=last[e][:].rearrange("p (c i j) -> p c j i", i=RUN, j=PACK),
+                in_=w4_raw[1, 4][:, :, P * e : P * (e + 1)].rearrange("p j (c i) -> p c j i", i=RUN),
+            )
+        for e in range(2):
+            quantise(w4q[2], slice(PIECE + P * e, PIECE + P * (e + 1)), last[e][:])
 
         accs = [bank("acc%d" % c, c) for c in range(N // P)]
 
         def wr_pass(a, c):
             cols = slice(P * c, P * (c + 1))
-            rows = slice(RES_ROW + 4 * a, P)
+            scales = swr[WR_ROW:P, N * a + P * c : N * a + P * (c + 1)]
             nc.tensor.matmul_mx(
-                out=accs[c][:], lhsT=wrw[:, a, cols].bitcast(FP8X4), lhsT_scale=swr[rows, cols],
-                rhs=v1[a][:].bitcast(FP8X4), rhs_scale=v1s[rows, :], start=(a == 0), stop=False,
+                out=accs[c][:], lhsT=wrw[:, a, cols].bitcast(FP8X4), lhsT_scale=scales,
+                rhs=v1[a][:].bitcast(FP8X4), rhs_scale=v1s[TAB_ROW + 4 * a : P, :], start=(a == 0), stop=False,
             )
 
         def w4_pass(g, c):

@@ -28,7 +28,7 @@ RUN = 4
 HALF = S // 2
 PIECE = 2 * P
 TAB_ROW, WR_ROW = 4, 8
-W3_ON_SCALAR = 64
+W3_ON_SCALAR = (64, 40)
 
 
 def tile_list_warhead_site_triage_kernel(
@@ -135,6 +135,7 @@ def tile_list_warhead_site_triage_kernel(
         l1 = load_list("l1", offs)
         t2 = load_fp8_words("t2", tab2_words[0])
         gains = [load_gain(0)]
+        load_w4(0, 0, 2)
         t1 = [load_fp8_words("t1_0", tab_words[0])]
         nc.sync.dma_start(out=bo_rows[0:2, :], in_=bo.rearrange("(r n) -> r n", r=2))
         for r in range(4):
@@ -142,13 +143,12 @@ def tile_list_warhead_site_triage_kernel(
                 out=swr[WR_ROW + r : P : 32, :].bitcast(I32).rearrange("q (a n) -> q a n", a=2),
                 in_=wr_scales[:, r:16:4, :].bitcast(I32).rearrange("a q n -> q a n"),
             )
-        wrw = tile("wrw", [P, 2, N], I32)
-        nc.sync.dma_start(out=wrw[:], in_=wr_words.rearrange("a p n i -> p a (n i)").bitcast(I32))
+        wrw = [load_fp8_words("wr0", wr_words[0])]
         t1.append(load_fp8_words("t1_1", tab_words[1]))
         gains.append(load_gain(1))
-        for lo in (0, 2, 4):
-            for g in range(2):
-                load_w4(g, lo, lo + 2)
+        wrw.append(load_fp8_words("wr1", wr_words[1]))
+        for g, lo in ((1, 0), (0, 2), (1, 2), (0, 4), (1, 4)):
+            load_w4(g, lo, lo + 2)
 
         halves = [slice(0, HALF), slice(HALF, S)]
 
@@ -171,7 +171,7 @@ def tile_list_warhead_site_triage_kernel(
         def w3_round(g):
             dst = w3_bf[g][:].rearrange("p (t m j) -> p m j t", t=PACK, j=PACK)
             src = w3_raw[g][:].rearrange("p j (m t) -> p m j t", t=PACK)
-            cut = W3_ON_SCALAR
+            cut = W3_ON_SCALAR[g]
             nc.scalar.copy(out=dst[:, 0:cut], in_=src[:, 0:cut])
             nc.vector.tensor_copy(out=dst[:, cut:P], in_=src[:, cut:P])
 
@@ -257,18 +257,22 @@ def tile_list_warhead_site_triage_kernel(
                 in_=w4_raw[g, lo][:].rearrange("p j (c i) -> p c j i", i=RUN),
             )
 
-        w4_bf = {(g, u): tile("w4_bf%d_%d" % (g, u), [P, WIDE], BF16) for g, u in ((0, 0), (1, 0), (0, 1), (1, 1), (0, 2))}
-        for u in range(2):
-            for g in range(2):
-                w4_round(w4_bf[g, u][:], g, 2 * u, nc.scalar.copy)
+        w4_bf = {(g, u): tile("w4_bf%d_%d" % (g, u), [P, WIDE], BF16) for g, u in ((1, 0), (0, 1), (1, 1), (0, 2))}
+        w4_bf[0, 0] = tile("w4_bf0_0", [P, WIDE], BF16, ("t2", 0))
+        nc.gpsimd.tensor_scalar(
+            w4_bf[0, 0][:].rearrange("p (c j) -> p c j", j=PACK),
+            w4_raw[0, 0][:].rearrange("p j c -> p c j"), 1.0, 0.0, MULT, ADD,
+        )
+        for g, u in ((1, 0), (0, 1), (1, 1)):
+            w4_round(w4_bf[g, u][:], g, 2 * u, nc.scalar.copy)
 
         v1 = [gather("v1_%d" % a, t1[a][:].bitcast(U32), l1, U32, ("buf1_%d" % a, 0)) for a in range(2)]
-        hb = [tile("hb%d" % g, [P, 2 * WIDE], BF16) for g in range(2)]
+        hb = [tile("hb0", [P, 2 * WIDE], BF16, ("w4_raw0_0", 0)), tile("hb1", [P, 2 * WIDE], BF16)]
         for g, engine in enumerate((nc.gpsimd, nc.vector)):
             for h in range(2):
                 scale(hb[g][:, WIDE * h : WIDE * (h + 1)], g, h, engine)
         hq = [quantised("hq0", S, ("gl1_0", 0)), quantised("hq1", S)]
-        w4q = [quantised("w4q%d" % u, S) for u in range(3)]
+        w4q = [quantised("w4q0", S, ("gl1_0", 4 * S)), quantised("w4q1", S), quantised("w4q2", S)]
         quantise(hq[0], slice(0, S), hb[0][:])
         quantise(w4q[0], halves[0], w4_bf[0, 0][:])
         quantise(hq[1], slice(0, S), hb[1][:])
@@ -292,7 +296,7 @@ def tile_list_warhead_site_triage_kernel(
             cols = slice(P * c, P * (c + 1))
             scales = swr[WR_ROW:P, N * a + P * c : N * a + P * (c + 1)]
             nc.tensor.matmul_mx(
-                out=accs[c][:], lhsT=wrw[:, a, cols].bitcast(FP8X4), lhsT_scale=scales,
+                out=accs[c][:], lhsT=wrw[a][:, cols].bitcast(FP8X4), lhsT_scale=scales,
                 rhs=v1[a][:].bitcast(FP8X4), rhs_scale=v1s[TAB_ROW + 4 * a : P, :], start=(a == 0), stop=False,
             )
 

@@ -101,11 +101,6 @@ def tile_list_warhead_site_triage_kernel(
             nc.sync.dma_start(out=held[:], in_=vec.rearrange("(g p t) -> p g t", g=2, t=PACK))
             return held
 
-        def load_gain(g):
-            held = tile("gain%d" % g, [P, 1, PACK], F32)
-            nc.sync.dma_start(out=held[:, 0, :], in_=gain[KP * g : KP * (g + 1)].rearrange("(p t) -> p t", t=PACK))
-            return held
-
         w4_raw = {}
 
         def load_w4(g, lo, hi):
@@ -120,6 +115,8 @@ def tile_list_warhead_site_triage_kernel(
         swr = scale_tile("swr", 2 * N, nc.gpsimd)
         bo_rows = tile("bo_rows", [P, N // 2], F32)
         nc.gpsimd.memset(bo_rows[:], 0.0)
+        gain_row = tile("gain_row", [P, KP], F32)
+        nc.gpsimd.memset(gain_row[:], 0.0)
         ident = tile("ident", [P, P], F32)
         make_identity(nc, ident[:])
         l3 = load_list("l3", offs3)
@@ -134,20 +131,19 @@ def tile_list_warhead_site_triage_kernel(
         load_scales(nc.sync, sw2, w2_scales, 0)
         l1 = load_list("l1", offs)
         t2 = load_fp8_words("t2", tab2_words[0])
-        gains = [load_gain(0)]
-        load_w4(0, 0, 2)
-        t1 = [load_fp8_words("t1_0", tab_words[0])]
+        gain0 = tile("gain0", [P, 1, PACK], F32)
+        nc.sync.dma_start(out=gain0[:, 0, :], in_=gain[0:KP].rearrange("(p t) -> p t", t=PACK))
+        t1 = [load_fp8_words("t1_%d" % a, tab_words[a]) for a in range(2)]
+        nc.sync.dma_start(out=gain_row[0:1, :], in_=gain[KP:H].rearrange("(r n) -> r n", r=1))
         nc.sync.dma_start(out=bo_rows[0:2, :], in_=bo.rearrange("(r n) -> r n", r=2))
         for r in range(4):
             nc.sync.dma_start(
                 out=swr[WR_ROW + r : P : 32, :].bitcast(I32).rearrange("q (a n) -> q a n", a=2),
                 in_=wr_scales[:, r:16:4, :].bitcast(I32).rearrange("a q n -> q a n"),
             )
-        wrw = [load_fp8_words("wr0", wr_words[0])]
-        t1.append(load_fp8_words("t1_1", tab_words[1]))
-        gains.append(load_gain(1))
-        wrw.append(load_fp8_words("wr1", wr_words[1]))
-        for g, lo in ((1, 0), (0, 2), (1, 2), (0, 4), (1, 4)):
+        wrw = tile("wrw", [P, 2, N], I32)
+        nc.sync.dma_start(out=wrw[:], in_=wr_words.rearrange("a p n i -> p a (n i)").bitcast(I32))
+        for g, lo in ((0, 0), (1, 0), (0, 2), (1, 2), (0, 4), (1, 4)):
             load_w4(g, lo, lo + 2)
 
         halves = [slice(0, HALF), slice(HALF, S)]
@@ -236,6 +232,11 @@ def tile_list_warhead_site_triage_kernel(
                     product(g, h, pair)
                 gelu(g, h)
 
+        gain_ps = bank("gain_ps", 6)
+        for t in range(PACK):
+            nc.tensor.transpose(gain_ps[:, P * t : P * (t + 1)], gain_row[:, t:KP:PACK], ident[:])
+        gains = [gain0[:], gain_ps[:].rearrange("p (t c) -> p c t", t=PACK)[:, 0:1, :]]
+
         bo_ps = bank("bo_ps", 7)
         for k in range(3):
             nc.tensor.transpose(bo_ps[:, P * k : P * (k + 1)], bo_rows[:, P * k : P * (k + 1)], ident[:])
@@ -246,7 +247,7 @@ def tile_list_warhead_site_triage_kernel(
         )
 
         def scale(hb, g, h, engine):
-            factor = gains[g][:].to_broadcast([P, HALF, PACK])
+            factor = gains[g].to_broadcast([P, HALF, PACK])
             engine.tensor_tensor(hb.rearrange("p (n t) -> p n t", t=PACK), gl[g, h][:], factor, MULT)
 
         WIDE = PACK * PIECE
@@ -257,22 +258,18 @@ def tile_list_warhead_site_triage_kernel(
                 in_=w4_raw[g, lo][:].rearrange("p j (c i) -> p c j i", i=RUN),
             )
 
-        w4_bf = {(g, u): tile("w4_bf%d_%d" % (g, u), [P, WIDE], BF16) for g, u in ((1, 0), (0, 1), (1, 1), (0, 2))}
-        w4_bf[0, 0] = tile("w4_bf0_0", [P, WIDE], BF16, ("t2", 0))
-        nc.gpsimd.tensor_scalar(
-            w4_bf[0, 0][:].rearrange("p (c j) -> p c j", j=PACK),
-            w4_raw[0, 0][:].rearrange("p j c -> p c j"), 1.0, 0.0, MULT, ADD,
-        )
-        for g, u in ((1, 0), (0, 1), (1, 1)):
-            w4_round(w4_bf[g, u][:], g, 2 * u, nc.scalar.copy)
+        w4_bf = {(g, u): tile("w4_bf%d_%d" % (g, u), [P, WIDE], BF16) for g, u in ((0, 0), (1, 0), (0, 1), (1, 1), (0, 2))}
+        for u in range(2):
+            for g in range(2):
+                w4_round(w4_bf[g, u][:], g, 2 * u, nc.scalar.copy)
 
         v1 = [gather("v1_%d" % a, t1[a][:].bitcast(U32), l1, U32, ("buf1_%d" % a, 0)) for a in range(2)]
-        hb = [tile("hb0", [P, 2 * WIDE], BF16, ("w4_raw0_0", 0)), tile("hb1", [P, 2 * WIDE], BF16)]
+        hb = [tile("hb%d" % g, [P, 2 * WIDE], BF16) for g in range(2)]
         for g, engine in enumerate((nc.gpsimd, nc.vector)):
             for h in range(2):
                 scale(hb[g][:, WIDE * h : WIDE * (h + 1)], g, h, engine)
         hq = [quantised("hq0", S, ("gl1_0", 0)), quantised("hq1", S)]
-        w4q = [quantised("w4q0", S, ("gl1_0", 4 * S)), quantised("w4q1", S), quantised("w4q2", S)]
+        w4q = [quantised("w4q%d" % u, S) for u in range(3)]
         quantise(hq[0], slice(0, S), hb[0][:])
         quantise(w4q[0], halves[0], w4_bf[0, 0][:])
         quantise(hq[1], slice(0, S), hb[1][:])
@@ -296,7 +293,7 @@ def tile_list_warhead_site_triage_kernel(
             cols = slice(P * c, P * (c + 1))
             scales = swr[WR_ROW:P, N * a + P * c : N * a + P * (c + 1)]
             nc.tensor.matmul_mx(
-                out=accs[c][:], lhsT=wrw[a][:, cols].bitcast(FP8X4), lhsT_scale=scales,
+                out=accs[c][:], lhsT=wrw[:, a, cols].bitcast(FP8X4), lhsT_scale=scales,
                 rhs=v1[a][:].bitcast(FP8X4), rhs_scale=v1s[TAB_ROW + 4 * a : P, :], start=(a == 0), stop=False,
             )
 

@@ -28,6 +28,7 @@ RUN = 4
 HALF = S // 2
 PIECE = 2 * P
 TAB_ROW, WR_ROW = 4, 8
+H1_ON_GPSIMD = 104
 W3_ON_SCALAR = (64, 40)
 
 
@@ -131,8 +132,7 @@ def tile_list_warhead_site_triage_kernel(
         load_scales(nc.sync, sw2, w2_scales, 0)
         l1 = load_list("l1", offs)
         t2 = load_fp8_words("t2", tab2_words[0])
-        gain0 = tile("gain0", [P, 1, PACK], F32)
-        nc.sync.dma_start(out=gain0[:, 0, :], in_=gain[0:KP].rearrange("(p t) -> p t", t=PACK))
+        gaint = load_channels("gaint", gain)
         t1 = [load_fp8_words("t1_%d" % a, tab_words[a]) for a in range(2)]
         nc.sync.dma_start(out=gain_row[0:1, :], in_=gain[KP:H].rearrange("(r n) -> r n", r=1))
         nc.sync.dma_start(out=bo_rows[0:2, :], in_=bo.rearrange("(r n) -> r n", r=2))
@@ -202,10 +202,9 @@ def tile_list_warhead_site_triage_kernel(
         for h in range(2):
             nc.vector.tensor_copy(v2[h][:], t2[:].bitcast(U32).indirect(l2[:, 16 * h : 16 * (h + 1)]))
 
-        x = {(g, h): tile("x%d_%d" % (g, h), [P, PACK, HALF], F32) for g in range(2) for h in range(2)}
         gl = {}
 
-        def product(g, h, pair):
+        def site(g, h, pair):
             acc = bank("site_ps", PACK * g + 2 * h + pair)
             for e in range(2):
                 lo = KP * g + P * (2 * pair + e)
@@ -213,29 +212,33 @@ def tile_list_warhead_site_triage_kernel(
                     out=acc[:, halves[e]], lhsT=w2p[:, lo : lo + P].bitcast(FP4X4), lhsT_scale=w2s[:, lo : lo + P],
                     rhs=v2[h][:].bitcast(FP8X4), rhs_scale=v2s[:, halves[h]], start=True, stop=True,
                 )
-            nc.vector.tensor_tensor(
-                x[g, h][:, 2 * pair : 2 * pair + 2, :], acc[:].rearrange("p (e s) -> p e s", e=2),
-                bufs[g, pair][:, :, halves[h]], MULT,
-            )
+            return acc[:].rearrange("p (e s) -> p e s", e=2)
 
-        def gelu(g, h):
-            gl[g, h] = tile("gl%d_%d" % (g, h), [P, HALF, PACK], F32)
+        def gelu(g, lo, hi, sites):
+            x = tile("x%d_%d" % (g, lo), [P, PACK, hi - lo], F32)
+            for pair in range(2):
+                nc.vector.tensor_tensor(
+                    x[:, 2 * pair : 2 * pair + 2, :], sites[pair][:, :, lo % HALF : lo % HALF + hi - lo],
+                    bufs[g, pair][:, :, lo:hi], MULT,
+                )
+            gl[g, lo] = tile("gl%d_%d" % (g, lo), [P, hi - lo, PACK], F32)
             nc.scalar.activation(
-                gl[g, h][:].rearrange("p (c i) t -> p c t i", i=RUN),
-                x[g, h][:].rearrange("p t (c i) -> p c t i", i=RUN),
+                gl[g, lo][:].rearrange("p (c i) t -> p c t i", i=RUN),
+                x[:].rearrange("p t (c i) -> p c t i", i=RUN),
                 ACT.Gelu_apprx_tanh,
             )
 
         for g in range(2):
             for h in range(2):
-                for pair in range(2):
-                    product(g, h, pair)
-                gelu(g, h)
+                sites = [site(g, h, pair) for pair in range(2)]
+                step = HALF // 2 if (g, h) == (0, 0) else HALF
+                for lo in range(HALF * h, HALF * (h + 1), step):
+                    gelu(g, lo, lo + step, sites)
 
         gain_ps = bank("gain_ps", 6)
         for t in range(PACK):
             nc.tensor.transpose(gain_ps[:, P * t : P * (t + 1)], gain_row[:, t:KP:PACK], ident[:])
-        gains = [gain0[:], gain_ps[:].rearrange("p (t c) -> p c t", t=PACK)[:, 0:1, :]]
+        gain1 = gain_ps[:].rearrange("p (t c) -> p c t", t=PACK)[:, 0:1, :]
 
         bo_ps = bank("bo_ps", 7)
         for k in range(3):
@@ -246,9 +249,11 @@ def tile_list_warhead_site_triage_kernel(
             in_=bo_ps[:, 0 : 3 * P].rearrange("p (k r) -> p r k", k=3)[:, 0:2],
         )
 
-        def scale(hb, g, h, engine):
-            factor = gains[g].to_broadcast([P, HALF, PACK])
-            engine.tensor_tensor(hb.rearrange("p (n t) -> p n t", t=PACK), gl[g, h][:], factor, MULT)
+        def scale(g, first, lo, hi, engine, factor):
+            engine.tensor_tensor(
+                hb[g][:, PACK * lo : PACK * hi].rearrange("p (n t) -> p n t", t=PACK),
+                gl[g, first][:, lo - first : hi - first, :], factor.to_broadcast([P, hi - lo, PACK]), MULT,
+            )
 
         WIDE = PACK * PIECE
 
@@ -265,9 +270,11 @@ def tile_list_warhead_site_triage_kernel(
 
         v1 = [gather("v1_%d" % a, t1[a][:].bitcast(U32), l1, U32, ("buf1_%d" % a, 0)) for a in range(2)]
         hb = [tile("hb%d" % g, [P, 2 * WIDE], BF16) for g in range(2)]
-        for g, engine in enumerate((nc.gpsimd, nc.vector)):
-            for h in range(2):
-                scale(hb[g][:, WIDE * h : WIDE * (h + 1)], g, h, engine)
+        for lo, hi in ((0, HALF // 2), (HALF // 2, HALF), (HALF, S)):
+            scale(0, lo, lo, hi, nc.gpsimd, gaint[:, 0:1, :])
+        scale(1, 0, 0, H1_ON_GPSIMD, nc.gpsimd, gaint[:, 1:2, :])
+        scale(1, 0, H1_ON_GPSIMD, HALF, nc.vector, gain1)
+        scale(1, HALF, HALF, S, nc.vector, gain1)
         hq = [quantised("hq0", S, ("gl1_0", 0)), quantised("hq1", S)]
         w4q = [quantised("w4q%d" % u, S) for u in range(3)]
         quantise(hq[0], slice(0, S), hb[0][:])

@@ -143,8 +143,8 @@ def tile_list_warhead_site_triage_kernel(
             )
         wrw = tile("wrw", [P, 2, N], I32)
         nc.sync.dma_start(out=wrw[:], in_=wr_words.rearrange("a p n i -> p a (n i)").bitcast(I32))
-        for g, lo in ((0, 0), (1, 0), (0, 2), (1, 2), (0, 4), (1, 4)):
-            load_w4(g, lo, lo + 2)
+        for g, lo, hi in ((0, 0, 2), (1, 0, 2), (0, 2, 4), (1, 2, 4), (0, 4, 6), (1, 4, 5), (1, 5, 6)):
+            load_w4(g, lo, hi)
 
         halves = [slice(0, HALF), slice(HALF, S)]
 
@@ -257,16 +257,17 @@ def tile_list_warhead_site_triage_kernel(
 
         WIDE = PACK * PIECE
 
-        def w4_round(dst, g, lo, copy):
+        def w4_round(dst, g, lo, hi, copy):
+            first = max(start for k, start in w4_raw if k == g and start <= lo)
             copy(
                 out=dst.rearrange("p (c i j) -> p c j i", i=RUN, j=PACK),
-                in_=w4_raw[g, lo][:].rearrange("p j (c i) -> p c j i", i=RUN),
+                in_=w4_raw[g, first][:, :, P * (lo - first) : P * (hi - first)].rearrange("p j (c i) -> p c j i", i=RUN),
             )
 
         w4_bf = {(g, u): tile("w4_bf%d_%d" % (g, u), [P, WIDE], BF16) for g, u in ((0, 0), (1, 0), (0, 1), (1, 1), (0, 2))}
-        for u in range(2):
-            for g in range(2):
-                w4_round(w4_bf[g, u][:], g, 2 * u, nc.scalar.copy)
+        for g, u in ((0, 0), (1, 0), (0, 1)):
+            w4_round(w4_bf[g, u][:], g, 2 * u, 2 * u + 2, nc.scalar.copy)
+        w4_round(w4_bf[1, 1][:, 0:KP], 1, 2, 3, nc.scalar.copy)
 
         v1 = [gather("v1_%d" % a, t1[a][:].bitcast(U32), l1, U32, ("buf1_%d" % a, 0)) for a in range(2)]
         hb = [tile("hb%d" % g, [P, 2 * WIDE], BF16) for g in range(2)]
@@ -281,18 +282,15 @@ def tile_list_warhead_site_triage_kernel(
         quantise(w4q[0], halves[0], w4_bf[0, 0][:])
         quantise(hq[1], slice(0, S), hb[1][:])
         quantise(w4q[0], halves[1], w4_bf[1, 0][:])
+        w4_round(w4_bf[1, 1][:, KP:WIDE], 1, 3, 4, nc.vector.tensor_copy)
         for g in range(2):
             quantise(w4q[1], halves[g], w4_bf[g, 1][:])
-        w4_round(w4_bf[0, 2][:], 0, 4, nc.vector.tensor_copy)
+        w4_round(w4_bf[0, 2][:], 0, 4, 6, nc.vector.tensor_copy)
         quantise(w4q[2], halves[0], w4_bf[0, 2][:])
-        last = [tile("w4_last%d" % e, [P, KP], BF16) for e in range(2)]
         for e in range(2):
-            nc.vector.tensor_copy(
-                out=last[e][:].rearrange("p (c i j) -> p c j i", i=RUN, j=PACK),
-                in_=w4_raw[1, 4][:, :, P * e : P * (e + 1)].rearrange("p j (c i) -> p c j i", i=RUN),
-            )
-        for e in range(2):
-            quantise(w4q[2], slice(PIECE + P * e, PIECE + P * (e + 1)), last[e][:])
+            last = tile("w4_last%d" % e, [P, KP], BF16)
+            w4_round(last[:], 1, 4 + e, 5 + e, nc.vector.tensor_copy)
+            quantise(w4q[2], slice(PIECE + P * e, PIECE + P * (e + 1)), last[:])
 
         accs = [bank("acc%d" % c, c) for c in range(N // P)]
 

@@ -133,14 +133,15 @@ def tile_list_warhead_site_triage_kernel(
         l1 = load_list("l1", offs)
         t2 = load_fp8_words("t2", tab2_words[0])
         gaint = load_channels("gaint", gain)
-        t1 = [load_fp8_words("t1_%d" % a, tab_words[a]) for a in range(2)]
-        nc.sync.dma_start(out=gain_row[0:1, :], in_=gain[KP:H].rearrange("(r n) -> r n", r=1))
+        t1 = [load_fp8_words("t1_0", tab_words[0])]
         nc.sync.dma_start(out=bo_rows[0:2, :], in_=bo.rearrange("(r n) -> r n", r=2))
         for r in range(4):
             nc.sync.dma_start(
                 out=swr[WR_ROW + r : P : 32, :].bitcast(I32).rearrange("q (a n) -> q a n", a=2),
                 in_=wr_scales[:, r:16:4, :].bitcast(I32).rearrange("a q n -> q a n"),
             )
+        t1.append(load_fp8_words("t1_1", tab_words[1]))
+        nc.sync.dma_start(out=gain_row[0:1, :], in_=gain[KP:H].rearrange("(r n) -> r n", r=1))
         wrw = tile("wrw", [P, 2, N], I32)
         nc.sync.dma_start(out=wrw[:], in_=wr_words.rearrange("a p n i -> p a (n i)").bitcast(I32))
         for g, lo, hi in ((0, 0, 2), (1, 0, 2), (0, 2, 4), (1, 2, 4), (0, 4, 6), (1, 4, 5), (1, 5, 6)):

@@ -69,8 +69,8 @@ def tile_list_warhead_site_triage_kernel(
         s2 = scale_tile("s2", T2, nc.vector)
         sw2 = scale_tile("sw2", H, nc.vector)
 
-        def load_scales(queue, held, scales, first):
-            for q in range(4):
+        def load_scales(queue, held, scales, first, quadrants=range(4)):
+            for q in quadrants:
                 if scales.shape[0] == 1:
                     queue.dma_start(out=held[q:P:32, :].bitcast(I32), in_=scales[0, q:16:4, :].bitcast(I32))
                 else:
@@ -112,7 +112,7 @@ def tile_list_warhead_site_triage_kernel(
             nc.vector.tensor_copy(got[:], window.indirect(lst[:]))
             return got
 
-        load_scales(nc.gpsimd, s1, tab_scales, TAB_ROW)
+        load_scales(nc.gpsimd, s1, tab_scales, TAB_ROW, range(3))
         swr = scale_tile("swr", 2 * N, nc.gpsimd)
         bo_rows = tile("bo_rows", [P, N // 2], F32)
         nc.gpsimd.memset(bo_rows[:], 0.0)
@@ -123,6 +123,7 @@ def tile_list_warhead_site_triage_kernel(
         l3 = load_list("l3", offs3)
         t3 = load_fp4_words("t3", tab3_words[0])
         load_scales(nc.sync, s3, tab3_scales, 0)
+        load_scales(nc.sync, s1, tab_scales, TAB_ROW, range(3, 4))
         w3_raw = [load_rows("w3_raw0", w3, 0, 0, KP)]
         l2 = load_list("l2", offs2)
         load_scales(nc.sync, s2, tab2_scales, 0)
@@ -265,7 +266,7 @@ def tile_list_warhead_site_triage_kernel(
                 in_=w4_raw[g, first][:, :, P * (lo - first) : P * (hi - first)].rearrange("p j (c i) -> p c j i", i=RUN),
             )
 
-        w4_bf = {(g, u): tile("w4_bf%d_%d" % (g, u), [P, WIDE], BF16) for g, u in ((0, 0), (1, 0), (0, 1), (1, 1), (0, 2))}
+        w4_bf = {(g, u): tile("w4_bf%d_%d" % (g, u), [P, WIDE], BF16) for u in range(2) for g in range(2)}
         for g, u in ((0, 0), (1, 0), (0, 1)):
             w4_round(w4_bf[g, u][:], g, 2 * u, 2 * u + 2, nc.scalar.copy)
         w4_round(w4_bf[1, 1][:, 0:KP], 1, 2, 3, nc.scalar.copy)
@@ -286,12 +287,17 @@ def tile_list_warhead_site_triage_kernel(
         w4_round(w4_bf[1, 1][:, KP:WIDE], 1, 3, 4, nc.vector.tensor_copy)
         for g in range(2):
             quantise(w4q[1], halves[g], w4_bf[g, 1][:])
-        w4_round(w4_bf[0, 2][:], 0, 4, 6, nc.vector.tensor_copy)
-        quantise(w4q[2], halves[0], w4_bf[0, 2][:])
-        for e in range(2):
-            last = tile("w4_last%d" % e, [P, KP], BF16)
-            w4_round(last[:], 1, 4 + e, 5 + e, nc.vector.tensor_copy)
-            quantise(w4q[2], slice(PIECE + P * e, PIECE + P * (e + 1)), last[:])
+        for g, lo, hi in ((0, 4, 6), (1, 4, 5), (1, 5, 6)):
+            width = P * (hi - lo) // 2
+            parts = [tile("w4_last%d_%d_%d" % (g, lo, e), [P, PACK * width], BF16) for e in range(2)]
+            for e in range(2):
+                nc.vector.tensor_copy(
+                    out=parts[e][:].rearrange("p (c i j) -> p c j i", i=RUN, j=PACK),
+                    in_=w4_raw[g, lo][:, :, width * e : width * (e + 1)].rearrange("p j (c i) -> p c j i", i=RUN),
+                )
+            for e in range(2):
+                first = PIECE * g + P * (lo - 4) + width * e
+                quantise(w4q[2], slice(first, first + width), parts[e][:])
 
         accs = [bank("acc%d" % c, c) for c in range(N // P)]
 

@@ -171,7 +171,10 @@ def tile_list_warhead_site_triage_kernel(
             src = w3_raw[g][:].rearrange("p j (m t) -> p m j t", t=PACK)
             cut = W3_ON_SCALAR[g]
             nc.scalar.copy(out=dst[:, 0:cut], in_=src[:, 0:cut])
-            nc.vector.tensor_copy(out=dst[:, cut:P], in_=src[:, cut:P])
+            nc.vector.tensor_copy(
+                out=w3_bf[g][:].rearrange("p (a b m j) -> p a m j b", a=2, b=2, j=PACK)[:, :, cut:P],
+                in_=w3_raw[g][:].rearrange("p j (m a b) -> p a m j b", a=2, b=2)[:, :, cut:P],
+            )
 
         def biased_buffer(g, pair, after=None):
             held = tile("buf%d_%d" % (g, pair), [P, 2, S], F32, after)
@@ -317,12 +320,9 @@ def tile_list_warhead_site_triage_kernel(
                 rhs=hq[g][0][:].bitcast(FP8X4), rhs_scale=hq[g][1][:], start=False, stop=(g == 1),
             )
 
-        def finish(c, on_scalar, after=None):
+        def finish(c, after=None):
             res = tile("res%d" % c, [P, S], F32, after)
-            if on_scalar:
-                nc.scalar.activation(res[:], accs[c][:], ACT.Identity, bias=bot[:, c : c + 1])
-            else:
-                nc.vector.tensor_scalar(res[:], accs[c][:], bot[:, c : c + 1], None, ADD)
+            nc.scalar.activation(res[:], accs[c][:], ACT.Identity, bias=bot[:, c : c + 1])
             nc.sync.dma_start(out=out[P * c : P * (c + 1), :], in_=res[:])
 
         for a in range(2):
@@ -332,9 +332,11 @@ def tile_list_warhead_site_triage_kernel(
             for g in range(2):
                 for c in (2 * u, 2 * u + 1):
                     w4_pass(g, c)
-        finish(0, True, ("w4_raw1_2", 0))
-        finish(1, True, ("w4_raw1_2", 4 * S))
-        finish(2, True)
-        finish(3, True)
-        finish(4, True)
-        finish(5, False)
+        finish(0, ("w4_raw1_2", 0))
+        finish(1, ("w4_raw1_2", 4 * S))
+        for c in (2, 3, 4):
+            finish(c)
+        for h in range(2):
+            res = tile("res5_%d" % h, [P, HALF], F32)
+            nc.vector.tensor_scalar(res[:], accs[5][:, halves[h]], bot[:, 5:6], None, ADD)
+            nc.sync.dma_start(out=out[5 * P : N, halves[h]], in_=res[:])

@@ -282,14 +282,19 @@ def tile_list_warhead_site_triage_kernel(
         scale(1, 0, H1_ON_GPSIMD, HALF, nc.vector, gain1)
         scale(1, HALF, HALF, S, nc.vector, gain1)
         hq = [quantised("hq0", S, ("gl1_0", 0)), quantised("hq1", S)]
-        w4q = [quantised("w4q%d" % u, S) for u in range(3)]
-        quantise(hq[0], slice(0, S), hb[0][:])
-        quantise(w4q[0], halves[0], w4_bf[0, 0][:])
-        quantise(hq[1], slice(0, S), hb[1][:])
-        quantise(w4q[0], halves[1], w4_bf[1, 0][:])
-        w4_round(w4_bf[1, 1][:, KP:WIDE], 1, 3, 4, nc.vector.tensor_copy)
+        w4q = [quantised("w4q%d" % c, PIECE, ("w4_raw1_0", 0) if c == 1 else None) for c in range(N // P)]
+
+        def w4_quantise(g, c):
+            quantise(w4q[c], slice(P * g, P * (g + 1)), w4_bf[g, c // 2][:, KP * (c % 2) : KP * (c % 2 + 1)])
+
         for g in range(2):
-            quantise(w4q[1], halves[g], w4_bf[g, 1][:])
+            quantise(hq[g], slice(0, S), hb[g][:])
+            w4_quantise(g, 0)
+        for g in range(2):
+            w4_quantise(g, 1)
+        w4_round(w4_bf[1, 1][:, KP:WIDE], 1, 3, 4, nc.vector.tensor_copy)
+        for g, c in ((0, 2), (1, 2), (0, 3), (1, 3)):
+            w4_quantise(g, c)
         for g, lo, hi in ((0, 4, 6), (1, 4, 5), (1, 5, 6)):
             width = P * (hi - lo) // 2
             parts = [tile("w4_last%d_%d_%d" % (g, lo, e), [P, PACK * width], BF16) for e in range(2)]
@@ -299,8 +304,8 @@ def tile_list_warhead_site_triage_kernel(
                     in_=w4_raw[g, lo][:, :, width * e : width * (e + 1)].rearrange("p j (c i) -> p c j i", i=RUN),
                 )
             for e in range(2):
-                first = PIECE * g + P * (lo - 4) + width * e
-                quantise(w4q[2], slice(first, first + width), parts[e][:])
+                first = P * lo + width * e
+                quantise(w4q[first // P], slice(P * g + first % P, P * g + first % P + width), parts[e][:])
 
         accs = [bank("acc%d" % c, c) for c in range(N // P)]
 
@@ -313,8 +318,8 @@ def tile_list_warhead_site_triage_kernel(
             )
 
         def w4_pass(g, c):
-            codes, scales = w4q[c // 2]
-            cols = slice(PIECE * g + P * (c % 2), PIECE * g + P * (c % 2 + 1))
+            codes, scales = w4q[c]
+            cols = slice(P * g, P * (g + 1))
             nc.tensor.matmul_mx(
                 out=accs[c][:], lhsT=codes[:, cols].bitcast(FP8X4), lhsT_scale=scales[:, cols],
                 rhs=hq[g][0][:].bitcast(FP8X4), rhs_scale=hq[g][1][:], start=False, stop=(g == 1),
@@ -328,10 +333,12 @@ def tile_list_warhead_site_triage_kernel(
         for a in range(2):
             for c in range(N // P):
                 wr_pass(a, c)
-        for u in range(3):
+        for c in range(4):
             for g in range(2):
-                for c in (2 * u, 2 * u + 1):
-                    w4_pass(g, c)
+                w4_pass(g, c)
+        for g in range(2):
+            for c in (4, 5):
+                w4_pass(g, c)
         finish(0, ("w4_raw1_2", 0))
         finish(1, ("w4_raw1_2", 4 * S))
         for c in (2, 3, 4):

import math
from contextlib import ExitStack

import concourse.mybir as mybir
from concourse.masks import make_identity

K, K2, H, N, T, T2, T3, S = 1024, 512, 1024, 768, 2048, 2048, 1024, 512
FLOPS = 2 * S * (2 * K2 * H + H * N + K * N)

F32 = mybir.dt.float32
BF16 = mybir.dt.bfloat16
I32 = mybir.dt.int32
U32 = mybir.dt.uint32
U16 = mybir.dt.uint16
U8 = mybir.dt.uint8
FP8X4 = mybir.dt.float8_e4m3fn_x4
FP4X4 = mybir.dt.float4_e2m1fn_x4
ACT = mybir.ActivationFunctionType
MULT = mybir.AluOpType.mult
ADD = mybir.AluOpType.add
BYTES_OF = {F32: 4, I32: 4, U32: 4, BF16: 2, U16: 2, U8: 1}

P = 128
PACK = 4
KP = P * PACK
ALIGN = 64
RUN = 4
HALF = S // 2
PIECE = 2 * P
TAB_ROW, WR_ROW = 4, 8
H1_ON_GPSIMD = 104
W3_ON_SCALAR = (64, 40)


def tile_list_warhead_site_triage_kernel(
    tc, tab_words, tab_scales, tab2_words, tab2_scales, tab3_words, tab3_scales, offs, offs2, offs3,
    w2_words, w2_scales, w3, b3, gain, w4, wr_words, wr_scales, bo, out,
):
    nc = tc.nc
    with ExitStack() as ctx:
        lists = ctx.enter_context(tc.tile_pool(name="lists", bufs=1))
        sb = ctx.enter_context(tc.tile_pool(name="sb", bufs=1))
        ps = ctx.enter_context(tc.psum_pool(name="ps", bufs=1))

        place = {"free": 0}

        def tile(name, shape, dtype, after=None):
            if after is None:
                place[name] = place["free"]
                place["free"] = place["free"] + math.ceil(math.prod(shape[1:]) * BYTES_OF[dtype] / ALIGN) * ALIGN
            else:
                place[name] = place[after[0]] + after[1]
            return sb.tile(shape, dtype, name=name, align_bytes=ALIGN, offset=place[name])

        def bank(name, b):
            return ps.tile([P, S], F32, name=name, tag="bank%d" % b)

        def scale_tile(name, width, engine):
            held = tile(name, [P, width], U8)
            engine.memset(held[:].bitcast(I32), 0)
            return held

        warm_in = tile("warm_in", [P, 1], F32)
        warm_out = tile("warm_out", [P, 1], F32)
        nc.vector.memset(warm_in[:], 0.0)
        nc.scalar.activation(warm_out[:], warm_in[:], ACT.Gelu_apprx_tanh)
        s3 = scale_tile("s3", T3, nc.gpsimd)
        s1 = scale_tile("s1", T, nc.gpsimd)
        s2 = scale_tile("s2", T2, nc.vector)
        sw2 = scale_tile("sw2", H, nc.vector)

        def load_scales(queue, held, scales, first, quadrants=range(4)):
            for q in quadrants:
                if scales.shape[0] == 1:
                    queue.dma_start(out=held[q:P:32, :].bitcast(I32), in_=scales[0, q:16:4, :].bitcast(I32))
                else:
                    rows = slice(32 * q + first, 32 * q + first + 8)
                    queue.dma_start(out=held[rows, :].bitcast(I32), in_=scales[:, 4 * q : 4 * q + 4, :].bitcast(I32))

        def load_list(name, src):
            lst = lists.tile([P, S // 16], U16, name=name)
            nc.sync.dma_start(lst[:], src)
            return lst

        def load_fp8_words(name, words):
            held = tile(name, [P, words.shape[1]], I32)
            nc.sync.dma_start(out=held[:], in_=words.rearrange("p t i -> p (t i)").bitcast(I32))
            return held

        def load_fp4_words(name, words):
            held = tile(name, [P, words.shape[1] // 2], U16)
            nc.sync.dma_start(out=held[:].bitcast(I32), in_=words.bitcast(I32))
            return held

        def load_rows(name, w, g, lo, hi):
            raw = tile(name, [P, PACK, hi - lo], F32)
            nc.sync.dma_start(out=raw[:], in_=w[KP * g : KP * (g + 1), lo:hi].rearrange("(p j) n -> p j n", j=PACK))
            return raw

        def load_channels(name, vec):
            held = tile(name, [P, 2, PACK], F32)
            nc.sync.dma_start(out=held[:], in_=vec.rearrange("(g p t) -> p g t", g=2, t=PACK))
            return held

        w4_raw = {}

        def load_w4(g, lo, hi):
            w4_raw[g, lo] = load_rows("w4_raw%d_%d" % (g, lo), w4, g, P * lo, P * hi)

        def gather(name, window, lst, dtype, after=None):
            got = tile(name, [P, S], dtype, after)
            nc.vector.tensor_copy(got[:], window.indirect(lst[:]))
            return got

        load_scales(nc.gpsimd, s1, tab_scales, TAB_ROW, range(3))
        swr = scale_tile("swr", 2 * N, nc.gpsimd)
        bo_rows = tile("bo_rows", [P, N // 2], F32)
        nc.gpsimd.memset(bo_rows[:], 0.0)
        gain_row = tile("gain_row", [P, KP], F32)
        nc.gpsimd.memset(gain_row[:], 0.0)
        ident = tile("ident", [P, P], F32)
        make_identity(nc, ident[:])
        l3 = load_list("l3", offs3)
        t3 = load_fp4_words("t3", tab3_words[0])
        load_scales(nc.sync, s3, tab3_scales, 0)
        load_scales(nc.sync, s1, tab_scales, TAB_ROW, range(3, 4))
        w3_raw = [load_rows("w3_raw0", w3, 0, 0, KP)]
        l2 = load_list("l2", offs2)
        load_scales(nc.sync, s2, tab2_scales, 0)
        b3t = load_channels("b3t", b3)
        w3_raw.append(load_rows("w3_raw1", w3, 0, KP, H))
        w2w = load_fp4_words("w2w", w2_words[0])
        load_scales(nc.sync, sw2, w2_scales, 0)
        l1 = load_list("l1", offs)
        t2 = load_fp8_words("t2", tab2_words[0])
        gaint = load_channels("gaint", gain)
        t1 = [load_fp8_words("t1_0", tab_words[0])]
        nc.sync.dma_start(out=bo_rows[0:2, :], in_=bo.rearrange("(r n) -> r n", r=2))
        for r in range(4):
            nc.sync.dma_start(
                out=swr[WR_ROW + r : P : 32, :].bitcast(I32).rearrange("q (a n) -> q a n", a=2),
                in_=wr_scales[:, r:16:4, :].bitcast(I32).rearrange("a q n -> q a n"),
            )
        t1.append(load_fp8_words("t1_1", tab_words[1]))
        nc.sync.dma_start(out=gain_row[0:1, :], in_=gain[KP:H].rearrange("(r n) -> r n", r=1))
        wrw = tile("wrw", [P, 2, N], I32)
        nc.sync.dma_start(out=wrw[:], in_=wr_words.rearrange("a p n i -> p a (n i)").bitcast(I32))
        for g, lo, hi in ((0, 0, 2), (1, 0, 2), (0, 2, 4), (1, 2, 4), (0, 4, 6), (1, 4, 5), (1, 5, 6)):
            load_w4(g, lo, hi)

        halves = [slice(0, HALF), slice(HALF, S)]

        def quantised(name, width, after=None):
            return tile(name + "_c", [P, width], U32, after), tile(name + "_s", [P, width], U8)

        def quantise(pair, cols, src):
            nc.vector.quantize_mx(out=pair[0][:, cols].bitcast(FP8X4), scales=pair[1][:, cols], in_=src)

        def reordered(name, src, dtype, engine, after=None):
            held = tile(name, [P, H], dtype, after)
            engine.tensor_copy(
                out=held[:].rearrange("p (g t m) -> p g t m", g=2, t=PACK),
                in_=src[:].rearrange("p (g m t) -> p g t m", g=2, t=PACK),
            )
            return held

        w3_bf = [tile("w3_bf%d" % g, [P, PACK * KP], BF16) for g in range(2)]

        def w3_round(g):
            dst = w3_bf[g][:].rearrange("p (t m j) -> p m j t", t=PACK, j=PACK)
            src = w3_raw[g][:].rearrange("p j (m t) -> p m j t", t=PACK)
            cut = W3_ON_SCALAR[g]
            nc.scalar.copy(out=dst[:, 0:cut], in_=src[:, 0:cut])
            nc.vector.tensor_copy(
                out=w3_bf[g][:].rearrange("p (a b m j) -> p a m j b", a=2, b=2, j=PACK)[:, :, cut:P],
                in_=w3_raw[g][:].rearrange("p j (m a b) -> p a m j b", a=2, b=2)[:, :, cut:P],
            )

        def biased_buffer(g, pair, after=None):
            held = tile("buf%d_%d" % (g, pair), [P, 2, S], F32, after)
            for e in range(2):
                t = 2 * pair + e
                cols = slice(P * t, P * (t + 1))
                acc = bank("buf_ps", PACK * g + t)
                nc.tensor.matmul_mx(
                    out=acc[:], lhsT=w3q[g][0][:, cols].bitcast(FP8X4), lhsT_scale=w3q[g][1][:, cols],
                    rhs=v3[:].bitcast(FP4X4), rhs_scale=v3s[:], start=True, stop=True,
                )
                nc.scalar.activation(held[:, e, :], acc[:], ACT.Identity, bias=b3t[:, g, t : t + 1])
            return held

        v3 = gather("v3", t3[:], l3, U16)
        v3s = gather("v3s", s3[:], l3, U8)
        v2s = gather("v2s", s2[:], l2, U8)
        w3_round(0)
        w3q = [quantised("w3q%d" % g, KP) for g in range(2)]
        quantise(w3q[0], slice(0, KP), w3_bf[0][:])
        w3_round(1)
        w2p = reordered("w2p", w2w, U16, nc.vector)
        quantise(w3q[1], slice(0, KP), w3_bf[1][:])
        w2s = reordered("w2s", sw2, U8, nc.gpsimd, ("w3_bf1", 0))
        v1s = gather("v1s", s1[:], l1, U8)
        bufs = {(0, pair): biased_buffer(0, pair, ("w3_raw1", 8 * S * pair)) for pair in range(2)}
        for pair in range(2):
            bufs[1, pair] = biased_buffer(1, pair)
        v2 = [tile("v2_%d" % h, [P, HALF], U32) for h in range(2)]
        for h in range(2):
            nc.vector.tensor_copy(v2[h][:], t2[:].bitcast(U32).indirect(l2[:, 16 * h : 16 * (h + 1)]))

        gl = {}

        def site(g, h, pair):
            acc = bank("site_ps", PACK * g + 2 * h + pair)
            for e in range(2):
                lo = KP * g + P * (2 * pair + e)
                nc.tensor.matmul_mx(
                    out=acc[:, halves[e]], lhsT=w2p[:, lo : lo + P].bitcast(FP4X4), lhsT_scale=w2s[:, lo : lo + P],
                    rhs=v2[h][:].bitcast(FP8X4), rhs_scale=v2s[:, halves[h]], start=True, stop=True,
                )
            return acc[:].rearrange("p (e s) -> p e s", e=2)

        def gelu(g, lo, hi, sites):
            x = tile("x%d_%d" % (g, lo), [P, PACK, hi - lo], F32)
            for pair in range(2):
                nc.vector.tensor_tensor(
                    x[:, 2 * pair : 2 * pair + 2, :], sites[pair][:, :, lo % HALF : lo % HALF + hi - lo],
                    bufs[g, pair][:, :, lo:hi], MULT,
                )
            gl[g, lo] = tile("gl%d_%d" % (g, lo), [P, hi - lo, PACK], F32)
            nc.scalar.activation(
                gl[g, lo][:].rearrange("p (c i) t -> p c t i", i=RUN),
                x[:].rearrange("p t (c i) -> p c t i", i=RUN),
                ACT.Gelu_apprx_tanh,
            )

        for g in range(2):
            for h in range(2):
                sites = [site(g, h, pair) for pair in range(2)]
                step = HALF // 2 if (g, h) == (0, 0) else HALF
                for lo in range(HALF * h, HALF * (h + 1), step):
                    gelu(g, lo, lo + step, sites)

        gain_ps = bank("gain_ps", 6)
        for t in range(PACK):
            nc.tensor.transpose(gain_ps[:, P * t : P * (t + 1)], gain_row[:, t:KP:PACK], ident[:])
        gain1 = gain_ps[:].rearrange("p (t c) -> p c t", t=PACK)[:, 0:1, :]

        bo_ps = bank("bo_ps", 7)
        for k in range(3):
            nc.tensor.transpose(bo_ps[:, P * k : P * (k + 1)], bo_rows[:, P * k : P * (k + 1)], ident[:])
        bot = tile("bot", [P, N // P], F32)
        nc.scalar.copy(
            out=bot[:].rearrange("p (r k) -> p r k", r=2),
            in_=bo_ps[:, 0 : 3 * P].rearrange("p (k r) -> p r k", k=3)[:, 0:2],
        )

        def scale(g, first, lo, hi, engine, factor):
            engine.tensor_tensor(
                hb[g][:, PACK * lo : PACK * hi].rearrange("p (n t) -> p n t", t=PACK),
                gl[g, first][:, lo - first : hi - first, :], factor.to_broadcast([P, hi - lo, PACK]), MULT,
            )

        WIDE = PACK * PIECE

        def w4_round(dst, g, lo, hi, copy):
            first = max(start for k, start in w4_raw if k == g and start <= lo)
            copy(
                out=dst.rearrange("p (c i j) -> p c j i", i=RUN, j=PACK),
                in_=w4_raw[g, first][:, :, P * (lo - first) : P * (hi - first)].rearrange("p j (c i) -> p c j i", i=RUN),
            )

        w4_bf = {(g, u): tile("w4_bf%d_%d" % (g, u), [P, WIDE], BF16) for u in range(2) for g in range(2)}
        for g, u in ((0, 0), (1, 0), (0, 1)):
            w4_round(w4_bf[g, u][:], g, 2 * u, 2 * u + 2, nc.scalar.copy)
        w4_round(w4_bf[1, 1][:, 0:KP], 1, 2, 3, nc.scalar.copy)

        v1 = [gather("v1_%d" % a, t1[a][:].bitcast(U32), l1, U32, ("buf1_%d" % a, 0)) for a in range(2)]
        hb = [tile("hb%d" % g, [P, 2 * WIDE], BF16) for g in range(2)]
        for lo, hi in ((0, HALF // 2), (HALF // 2, HALF), (HALF, S)):
            scale(0, lo, lo, hi, nc.gpsimd, gaint[:, 0:1, :])
        scale(1, 0, 0, H1_ON_GPSIMD, nc.gpsimd, gaint[:, 1:2, :])
        scale(1, 0, H1_ON_GPSIMD, HALF, nc.vector, gain1)
        scale(1, HALF, HALF, S, nc.vector, gain1)
        hq = [quantised("hq0", S, ("gl1_0", 0)), quantised("hq1", S)]
        w4q = [quantised("w4q%d" % c, PIECE, ("w4_raw1_0", 0) if c == 1 else None) for c in range(N // P)]

        def w4_quantise(g, c):
            quantise(w4q[c], slice(P * g, P * (g + 1)), w4_bf[g, c // 2][:, KP * (c % 2) : KP * (c % 2 + 1)])

        for g in range(2):
            quantise(hq[g], slice(0, S), hb[g][:])
            w4_quantise(g, 0)
        for g in range(2):
            w4_quantise(g, 1)
        w4_round(w4_bf[1, 1][:, KP:WIDE], 1, 3, 4, nc.vector.tensor_copy)
        for g, c in ((0, 2), (1, 2), (0, 3), (1, 3)):
            w4_quantise(g, c)
        for g, lo, hi in ((0, 4, 6), (1, 4, 5), (1, 5, 6)):
            width = P * (hi - lo) // 2
            parts = [tile("w4_last%d_%d_%d" % (g, lo, e), [P, PACK * width], BF16) for e in range(2)]
            for e in range(2):
                nc.vector.tensor_copy(
                    out=parts[e][:].rearrange("p (c i j) -> p c j i", i=RUN, j=PACK),
                    in_=w4_raw[g, lo][:, :, width * e : width * (e + 1)].rearrange("p j (c i) -> p c j i", i=RUN),
                )
            for e in range(2):
                first = P * lo + width * e
                quantise(w4q[first // P], slice(P * g + first % P, P * g + first % P + width), parts[e][:])

        accs = [bank("acc%d" % c, c) for c in range(N // P)]

        def wr_pass(a, c):
            cols = slice(P * c, P * (c + 1))
            scales = swr[WR_ROW:P, N * a + P * c : N * a + P * (c + 1)]
            nc.tensor.matmul_mx(
                out=accs[c][:], lhsT=wrw[:, a, cols].bitcast(FP8X4), lhsT_scale=scales,
                rhs=v1[a][:].bitcast(FP8X4), rhs_scale=v1s[TAB_ROW + 4 * a : P, :], start=(a == 0), stop=False,
            )

        def w4_pass(g, c):
            codes, scales = w4q[c]
            cols = slice(P * g, P * (g + 1))
            nc.tensor.matmul_mx(
                out=accs[c][:], lhsT=codes[:, cols].bitcast(FP8X4), lhsT_scale=scales[:, cols],
                rhs=hq[g][0][:].bitcast(FP8X4), rhs_scale=hq[g][1][:], start=False, stop=(g == 1),
            )

        def finish(c, after=None):
            res = tile("res%d" % c, [P, S], F32, after)
            nc.scalar.activation(res[:], accs[c][:], ACT.Identity, bias=bot[:, c : c + 1])
            nc.sync.dma_start(out=out[P * c : P * (c + 1), :], in_=res[:])

        for a in range(2):
            for c in range(N // P):
                wr_pass(a, c)
        for c in range(4):
            for g in range(2):
                w4_pass(g, c)
        for g in range(2):
            for c in (4, 5):
                w4_pass(g, c)
        finish(0, ("w4_raw1_2", 0))
        finish(1, ("w4_raw1_2", 4 * S))
        for c in (2, 3, 4):
            finish(c)
        for h in range(2):
            res = tile("res5_%d" % h, [P, HALF], F32)
            nc.vector.tensor_scalar(res[:], accs[5][:, halves[h]], bot[:, 5:6], None, ADD)
            nc.sync.dma_start(out=out[5 * P : N, halves[h]], in_=res[:])
